import numpy as np
import ml_dtypes


def mxq(x, axis, fmt="e4m3"):
    dtype, down = {"e4m3": (ml_dtypes.float8_e4m3fn, 7), "e5m2": (ml_dtypes.float8_e5m2, 14)}[fmt]
    v = np.moveaxis(np.asarray(x, np.float32).astype(ml_dtypes.bfloat16).astype(np.float64), axis, -1)
    blocks = v.reshape(v.shape[:-1] + (-1, 32))
    amax = np.abs(blocks).max(-1, keepdims=True)
    byte = np.maximum(np.where(amax > 0, np.frexp(amax)[1] - 1 + 127, 0) - down, 1)
    scale = np.exp2(byte - 127.0)
    codes = (blocks / scale).astype(np.float32).astype(dtype).astype(np.float64)
    return np.moveaxis((codes * scale).reshape(v.shape), -1, axis)


WIDE = False


def mx_kscale(k):
    if not WIDE:
        return np.ones(k)
    levels = np.array([18, -18])
    if k % 512:
        return np.exp2(np.random.permutation(np.resize(levels, k // 32))).repeat(32)
    a = np.empty((k // 512, 16))
    for p in range(k // 512):
        a[p, :8] = np.random.permutation(np.resize(levels, 8))
        for g in range(8):
            far = levels[np.abs(levels - a[p, g]) >= 10]
            a[p, g + 8] = far[np.random.randint(len(far))]
    return np.exp2(a.ravel()).repeat(32)


def f64(x):
    return np.asarray(x).astype(np.float64)


def striped(idx):
    return np.tile(np.asarray(idx).reshape(-1, 16).T, (8, 1)).astype(np.uint16)


def unstriped(offs):
    return offs[:16].T.reshape(-1).astype(np.int64)

def planes(y):
    n, m = y.shape
    v = y.astype(np.float32).astype(ml_dtypes.bfloat16).astype(np.float64).reshape(n // 32, 32, m)
    top = np.abs(v).max(1)
    byte = np.clip(np.where(top > 0, np.frexp(top)[1] - 1 + 127 - 7, 1), 1, 254)
    codes = (v * np.exp2(127.0 - byte)[:, None, :]).reshape(n, m).astype(np.float32).astype(ml_dtypes.float8_e4m3fn).view(np.uint8)
    words = codes.reshape(n // 512, 128, 4, m).transpose(0, 1, 3, 2)
    return np.ascontiguousarray(words), np.ascontiguousarray(byte.astype(np.uint8).reshape(n // 512, 16, m))


def setup_inputs():
    n = np.random.standard_normal
    uni = np.random.uniform
    idx = np.random.permutation(2048)[:512]
    cs_ = uni(0.75, 1.3, 512)
    f_d = mx_kscale(512)
    f_r = mx_kscale(512)
    return {
        "xT": (n((512, 512)) / np.sqrt(512) * f_d[:, None] * f_r[None, :]).astype(np.float32),
        "cT": (n((512, 2048)) / np.sqrt(512) / f_d[:, None]).astype(np.float32),
        "hx": (uni(0.4, 0.6, (512, 1))).astype(np.float32),
        "cs": np.tile(cs_ * f_d, (128, 1)).astype(np.float32),
        "cd": (cs_[:, None] * f_d[:, None]).astype(np.float32),
        "dp": (n((512, 512))).astype(np.float32),
        "us": (uni(0.75, 1.3, (512, 1)) / f_r[:, None]).astype(np.float32),
        "wt": (uni(0.75, 1.3, (512, 1))).astype(np.float32),
        "offs": striped(idx),
    }


def reference(xT, cT, hx, cs, cd, dp, us, wt, offs):
    idx = unstriped(offs)
    c = f64(cT)[:, idx]
    ct = c.T
    n2 = (0.5 * np.square(f64(cs)[:1] * ct)).sum(-1, keepdims=True)
    nr = n2.T
    a = mxq(f64(xT), 0, "e4m3").T @ mxq(c, 0, "e4m3")
    p = np.exp(f64(us) * a - f64(hx) - nr)
    h = f64(wt) * f64(dp) * p
    g = f64(us) * h
    xg = mxq(f64(xT), 1, "e4m3") @ mxq(g, 0, "e5m2")
    ht = h.T
    sh = (ht).sum(-1, keepdims=True)
    sr = sh.T
    dc = xg - np.square(f64(cd)) * c * sr
    out_0 = np.zeros((512, 2048))
    out_0[:, idx] = dc
    return (out_0,) + planes(out_0)

@@ -1,0 +1,217 @@
+from contextlib import ExitStack
+
+import concourse.mybir as mybir
+from concourse.masks import make_identity
+
+F32 = mybir.dt.float32
+BF16 = mybir.dt.bfloat16
+I32 = mybir.dt.int32
+U32 = mybir.dt.uint32
+U16 = mybir.dt.uint16
+U8 = mybir.dt.uint8
+E4M3 = mybir.dt.float8_e4m3fn_x4
+E5M2 = mybir.dt.float8_e5m2_x4
+ACT = mybir.ActivationFunctionType
+ALU = mybir.AluOpType
+
+P = 128
+LANES = 4
+D = 512
+R = 512
+SLOTS = 512
+T = 2048
+CHUNK = 512
+G_SPLIT = 416
+
+FLOPS = 2 * 2 * D * R * SLOTS
+
+
+def tile_attend_grbf_pl_kernel(tc, xT, cT, hx, cs, cd, dp, us, wt, offs, out_0, out_1, out_2):
+    nc = tc.nc
+    with ExitStack() as ctx:
+        sb = ctx.enter_context(tc.tile_pool(name="sb", bufs=1))
+        ps = ctx.enter_context(tc.psum_pool(name="ps", bufs=1))
+
+        def quantize(name, src, fmt):
+            codes = sb.tile([P, 512], U32, name=name + "_codes", align_bytes=64)
+            scales = sb.tile([P, 512], U8, name=name + "_scales", align_bytes=64)
+            nc.vector.quantize_mx(out=codes[:].bitcast(fmt), scales=scales[:], in_=src)
+            return codes, scales
+
+        def column(name, src):
+            col = sb.tile([P, LANES], F32, name=name)
+            nc.scalar.dma_start(out=col[:], in_=src)
+            return col
+
+        def spread_sums(name, turned, row, scale):
+            for b in range(turned.shape[1]):
+                col = sb.tile([P, 1], F32, name=f"{name}_col{b}")
+                summed = sb.tile([P, P], F32, name=f"{name}_summed{b}")
+                nc.scalar.activation(summed[:], turned[:, b, :], ACT.Identity, scale=scale, accum_out=col[:])
+                nc.tensor.transpose(row[:, P * b : P * (b + 1)], col[:].to_broadcast([P, P]), ident[:])
+
+        x_raw = sb.tile([P, LANES, R], F32, name="x_raw")
+        nc.sync.dma_start(out=x_raw[:], in_=xT.rearrange("(p j) r -> p j r", j=LANES))
+        offsets = sb.tile([P, SLOTS // 16], U16, name="offsets")
+        nc.sync.dma_start(offsets[:], offs)
+        cs_col = column("cs_col", cs[0, :].rearrange("(p j) -> p j", j=LANES))
+        us_col = column("us_col", us.rearrange("(s t) o -> s (t o)", t=LANES))
+        hx_col = column("hx_col", hx.rearrange("(s t) o -> s (t o)", t=LANES))
+        wt_col = column("wt_col", wt.rearrange("(s t) o -> s (t o)", t=LANES))
+        cd_col = column("cd_col", cd.rearrange("(p j) o -> p (j o)", j=LANES))
+        cT_planes = cT.rearrange("(p j) c -> j p c", j=LANES)
+        table = []
+        for j in range(LANES):
+            plane = sb.tile([P, T], F32, name=f"table{j}")
+            nc.sync.dma_start(out=plane[:], in_=cT_planes[j])
+            table.append(plane)
+        dp_sb = sb.tile([P, LANES, SLOTS], F32, name="dp_sb")
+        nc.sync.dma_start(out=dp_sb[:], in_=dp.rearrange("(s t) i -> s t i", t=LANES))
+
+        ident = sb.tile([P, P], F32, name="ident")
+        make_identity(nc, ident[:])
+        ident_bf = sb.tile([P, P], BF16, name="ident_bf")
+        make_identity(nc, ident_bf[:])
+        windows = []
+        for j in range(LANES):
+            window = sb.tile([P, T], F32, name=f"window{j}")
+            (nc.vector if j < 2 else nc.gpsimd).memset(window[:], 0.0)
+            windows.append(window)
+        neg_hx = sb.tile([P, LANES], F32, name="neg_hx")
+        nc.gpsimd.tensor_scalar(neg_hx[:], hx_col[:], -1.0, 0.0, ALU.mult, ALU.add)
+        neg_cd = sb.tile([P, LANES], F32, name="neg_cd")
+        nc.gpsimd.tensor_scalar(neg_cd[:], cd_col[:], -1.0, 0.0, ALU.mult, ALU.add)
+        neg_cd2 = sb.tile([P, LANES], F32, name="neg_cd2")
+        nc.gpsimd.tensor_tensor(neg_cd2[:], neg_cd[:], cd_col[:], ALU.mult)
+        us_wt = sb.tile([P, LANES], F32, name="us_wt")
+        nc.gpsimd.tensor_tensor(us_wt[:], us_col[:], wt_col[:], ALU.mult)
+
+        xd = sb.tile([P, LANES, P, LANES], BF16, name="xd", align_bytes=64)
+        nc.vector.tensor_copy(
+            out=xd[:].rearrange("p t s j -> p s j t"),
+            in_=x_raw[:].rearrange("p j (s t) -> p s j t", t=LANES),
+        )
+        xd_codes, xd_scales = quantize("xd", xd[:].rearrange("p t s j -> p (t s j)"), E4M3)
+
+        xr = sb.tile([P, LANES, P, LANES], BF16, name="xr", align_bytes=64)
+        for j in range(LANES):
+            turned = ps.tile([P, LANES, P], BF16, name=f"x_turned{j}", tag=f"big{j}")
+            for t in range(LANES):
+                nc.tensor.transpose(turned[:, t, :], xd[:, t, :, j], ident_bf[:])
+            nc.scalar.copy(out=xr[:, j, :, :], in_=turned[:].rearrange("s t p -> s p t"))
+        xr_codes, xr_scales = quantize("xr", xr[:].rearrange("s j p t -> s (j p t)"), E4M3)
+
+        c_pairs = [sb.tile([P, 2, SLOTS], F32, name=f"c_pair{u}") for u in range(2)]
+        c_planes = [c_pairs[j // 2][:, j % 2, :] for j in range(LANES)]
+        c_words = sb.tile([P, SLOTS, LANES], BF16, name="c_words", align_bytes=64)
+        n2_turned = [ps.tile([P, 2, P], F32, name=f"n2_turned{u}", tag=f"big{2 + u}") for u in range(2)]
+        for j in range(LANES):
+            square = sb.tile([P, SLOTS], F32, name=f"square{j}")
+            parts = 2 if j == LANES - 1 else 1
+            width = SLOTS // parts
+            for part in range(parts):
+                cols = slice(width * part, width * (part + 1))
+                listed = offsets[:, width // 16 * part : width // 16 * (part + 1)]
+                nc.vector.tensor_copy(c_planes[j][:, cols], table[j][:].indirect(listed))
+                nc.scalar.activation(square[:, cols], c_planes[j][:, cols], ACT.Square, scale=cs_col[:, j : j + 1])
+            for b in range(LANES):
+                nc.tensor.matmul(
+                    n2_turned[b // 2][:, b % 2, :], square[:, P * b : P * (b + 1)], ident[:], is_transpose=True,
+                    start=(j == 0 and b % 2 == 0), stop=(j == LANES - 1 and b % 2 == 1),
+                )
+            if j == 1:
+                nc.scalar.copy(out=c_words[:, :, 0:2], in_=c_pairs[0][:].rearrange("p e i -> p i e"))
+        nc.vector.tensor_copy(out=c_words[:, :, 2:4], in_=c_pairs[1][:].rearrange("p e i -> p i e"))
+        c_codes, c_scales = quantize("c", c_words[:].rearrange("p i t -> p (i t)"), E4M3)
+        n2_row = sb.tile([P, SLOTS], F32, name="n2_row")
+        n2_row_ps = [ps.tile([P, 2 * P], F32, name=f"n2_row_ps{u}", tag=f"side{u}") for u in range(2)]
+        for u in range(2):
+            spread_sums(f"n2_{u}", n2_turned[u], n2_row_ps[u], 0.5)
+        for u in range(2):
+            nc.scalar.copy(out=n2_row[:, 2 * P * u : 2 * P * (u + 1)], in_=n2_row_ps[u][:])
+
+        g_planes = sb.tile([P, LANES, SLOTS], BF16, name="g_planes")
+        sh_turned = ps.tile([P, LANES, P], F32, name="sh_turned", tag="side2")
+        probs = []
+        for t in range(LANES):
+            a = ps.tile([P, SLOTS], F32, name=f"a{t}", tag=("big3", "big2", "side0", "side1")[t])
+            cols = slice(P * t, P * (t + 1))
+            nc.tensor.matmul_mx(
+                out=a[:], lhsT=xd_codes[:, cols].bitcast(E4M3), lhsT_scale=xd_scales[:, cols],
+                rhs=c_codes[:].bitcast(E4M3), rhs_scale=c_scales[:], start=True, stop=True,
+            )
+            expo = sb.tile([P, SLOTS], F32, name=f"expo{t}")
+            nc.vector.scalar_tensor_tensor(expo[:], a[:], us_col[:, t : t + 1], n2_row[:], ALU.mult, ALU.subtract)
+            prob = sb.tile([P, SLOTS], F32, name=f"prob{t}")
+            nc.scalar.activation(prob[:], expo[:], ACT.Exp, bias=neg_hx[:, t : t + 1])
+            probs.append(prob)
+        for t in range(LANES):
+            h = sb.tile([P, SLOTS], F32, name=f"h{t}")
+            nc.vector.scalar_tensor_tensor(h[:], probs[t][:], wt_col[:, t : t + 1], dp_sb[:, t, :], ALU.mult, ALU.mult)
+            for b in range(LANES):
+                nc.tensor.matmul(
+                    sh_turned[:, b, :], h[:, P * b : P * (b + 1)], ident[:], is_transpose=True,
+                    start=(t == 0 and b == 0), stop=(t == LANES - 1 and b == LANES - 1),
+                )
+            if t < LANES - 1:
+                nc.scalar.activation(g_planes[:, t, :], h[:], ACT.Copy, scale=us_col[:, t : t + 1])
+            else:
+                nc.vector.scalar_tensor_tensor(
+                    g_planes[:, t, :], probs[t][:], us_wt[:, t : t + 1], dp_sb[:, t, :], ALU.mult, ALU.mult
+                )
+        g_words = sb.tile([P, SLOTS, LANES], BF16, name="g_words", align_bytes=64)
+        for engine_copy, cols in ((nc.vector.tensor_copy, slice(0, G_SPLIT)), (nc.scalar.copy, slice(G_SPLIT, SLOTS))):
+            engine_copy(
+                out=g_words[:, cols, :].rearrange("s (c i) t -> s c t i", i=4),
+                in_=g_planes[:, :, cols].rearrange("s t (c i) -> s c t i", i=4),
+            )
+        sh_row = ps.tile([P, SLOTS], F32, name="sh_row", tag="side3")
+        spread_sums("sh", sh_turned, sh_row, 1.0)
+        g_codes, g_scales = quantize("g", g_words[:].rearrange("s i t -> s (i t)"), E5M2)
+
+        out_planes = out_0.rearrange("(p j) c -> j p c", j=LANES)
+        chunks = T // CHUNK
+        pairs = [sb.tile([P, 2, CHUNK, 2], BF16, name=f"pairs{k}") for k in range(chunks)]
+        for j in range(LANES):
+            xg_ps = ps.tile([P, SLOTS], F32, name=f"xg{j}", tag=("side2", "big1", "big2", "big3")[j])
+            cols = slice(P * j, P * (j + 1))
+            nc.tensor.matmul_mx(
+                out=xg_ps[:], lhsT=xr_codes[:, cols].bitcast(E4M3), lhsT_scale=xr_scales[:, cols],
+                rhs=g_codes[:].bitcast(E5M2), rhs_scale=g_scales[:], start=True, stop=True,
+            )
+            xg = sb.tile([P, SLOTS], F32, name=f"xg_sb{j}")
+            nc.scalar.copy(out=xg[:], in_=xg_ps[:])
+            pull = sb.tile([P, SLOTS], F32, name=f"pull{j}")
+            nc.vector.scalar_tensor_tensor(pull[:], c_planes[j], neg_cd2[:, j : j + 1], sh_row[:], ALU.mult, ALU.mult)
+            nc.vector.tensor_tensor(windows[j][:].indirect(offsets[:]), xg[:], pull[:], ALU.add)
+            nc.sync.dma_start(out=out_planes[j], in_=windows[j][:])
+        for j in range(LANES):
+            for k in range(chunks):
+                src = windows[j][:, CHUNK * k : CHUNK * (k + 1)]
+                if j == 2 and k < 2:
+                    nc.scalar.copy(out=pairs[k][:, 1, :, :], in_=src.unsqueeze(2).to_broadcast([P, CHUNK, 2]))
+                elif j == 3 and k < 2:
+                    nc.vector.tensor_copy(out=pairs[k][:, 1, :, 1], in_=src)
+                else:
+                    nc.scalar.copy(out=pairs[k][:, j // 2, :, j % 2], in_=src)
+
+        y_scales = sb.tile([P, T], U8, name="y_scales", align_bytes=64)
+        words_out = out_1[0].rearrange("p c l -> p (c l)").bitcast(I32)
+        for k in range(chunks):
+            y_words = sb.tile([P, CHUNK, LANES], BF16, name=f"y_words{k}", align_bytes=64)
+            word = I32 if k < 2 else U32
+            engine_copy = nc.vector.tensor_copy if k < 2 else nc.scalar.copy
+            engine_copy(
+                out=y_words[:].rearrange("p c t -> p (c t)").bitcast(word).rearrange("p (c u) -> p c u", u=2),
+                in_=pairs[k][:].rearrange("p u c e -> p (u c e)").bitcast(word).rearrange("p (u c) -> p c u", u=2),
+            )
+            y_codes = sb.tile([P, CHUNK], U32, name=f"y_codes{k}", align_bytes=64)
+            cols = slice(CHUNK * k, CHUNK * (k + 1))
+            nc.vector.quantize_mx(
+                out=y_codes[:].bitcast(E4M3), scales=y_scales[:, cols], in_=y_words[:].rearrange("p c t -> p (c t)")
+            )
+            nc.sync.dma_start(out=words_out[:, cols], in_=y_codes[:].bitcast(I32))
+        scales_out = out_2[0].bitcast(I32)
+        for q in range(4):
+            queue = nc.scalar if q < 2 else nc.sync
+            queue.dma_start(out=scales_out[4 * q : 4 * q + 4, :], in_=y_scales[32 * q : 32 * q + 4, :].bitcast(I32))

@@ -73,9 +73,9 @@ def tile_attend_grbf_pl_kernel(tc, xT, cT, hx, cs, cd, dp, us, wt, offs, out_0, 
         ident_bf = sb.tile([P, P], BF16, name="ident_bf")
         make_identity(nc, ident_bf[:])
         windows = []
-        for j in range(LANES):
+        for j in range(2):
             window = sb.tile([P, T], F32, name=f"window{j}")
-            (nc.vector if j < 2 else nc.gpsimd).memset(window[:], 0.0)
+            nc.vector.memset(window[:], 0.0)
             windows.append(window)
         neg_hx = sb.tile([P, LANES], F32, name="neg_hx")
         nc.gpsimd.tensor_scalar(neg_hx[:], hx_col[:], -1.0, 0.0, ALU.mult, ALU.add)
@@ -103,7 +103,7 @@ def tile_attend_grbf_pl_kernel(tc, xT, cT, hx, cs, cd, dp, us, wt, offs, out_0, 
 
         c_pairs = [sb.tile([P, 2, SLOTS], F32, name=f"c_pair{u}") for u in range(2)]
         c_planes = [c_pairs[j // 2][:, j % 2, :] for j in range(LANES)]
-        c_words = sb.tile([P, SLOTS, LANES], BF16, name="c_words", align_bytes=64)
+        c_words = sb.tile([P, SLOTS, LANES], BF16, name="c_words", tag="late2", align_bytes=64)
         n2_turned = [ps.tile([P, 2, P], F32, name=f"n2_turned{u}", tag=f"big{2 + u}") for u in range(2)]
         for j in range(LANES):
             square = sb.tile([P, SLOTS], F32, name=f"square{j}")
@@ -140,11 +140,15 @@ def tile_attend_grbf_pl_kernel(tc, xT, cT, hx, cs, cd, dp, us, wt, offs, out_0, 
                 out=a[:], lhsT=xd_codes[:, cols].bitcast(E4M3), lhsT_scale=xd_scales[:, cols],
                 rhs=c_codes[:].bitcast(E4M3), rhs_scale=c_scales[:], start=True, stop=True,
             )
-            expo = sb.tile([P, SLOTS], F32, name=f"expo{t}")
+            expo = sb.tile([P, SLOTS], F32, name=f"expo{t}", tag="late3" if t == 0 else f"expo{t}", align_bytes=64)
             nc.vector.scalar_tensor_tensor(expo[:], a[:], us_col[:, t : t + 1], n2_row[:], ALU.mult, ALU.subtract)
             prob = sb.tile([P, SLOTS], F32, name=f"prob{t}")
             nc.scalar.activation(prob[:], expo[:], ACT.Exp, bias=neg_hx[:, t : t + 1])
             probs.append(prob)
+        for j in range(2, LANES):
+            window = sb.tile([P, T], F32, name=f"window{j}", tag=f"late{j}", align_bytes=64)
+            nc.gpsimd.memset(window[:], 0.0)
+            windows.append(window)
         for t in range(LANES):
             h = sb.tile([P, SLOTS], F32, name=f"h{t}")
             nc.vector.scalar_tensor_tensor(h[:], probs[t][:], wt_col[:, t : t + 1], dp_sb[:, t, :], ALU.mult, ALU.mult)

@@ -20,7 +20,7 @@ D = 512
 R = 512
 SLOTS = 512
 T = 2048
-CHUNK = 512
+CHUNKS = ((0, 512), (512, 512), (1024, 512), (1536, 256), (1792, 256))
 G_SPLIT = 416
 
 FLOPS = 2 * 2 * D * R * SLOTS
@@ -32,8 +32,8 @@ def tile_attend_grbf_pl_kernel(tc, xT, cT, hx, cs, cd, dp, us, wt, offs, out_0, 
         sb = ctx.enter_context(tc.tile_pool(name="sb", bufs=1))
         ps = ctx.enter_context(tc.psum_pool(name="ps", bufs=1))
 
-        def quantize(name, src, fmt):
-            codes = sb.tile([P, 512], U32, name=name + "_codes", align_bytes=64)
+        def quantize(name, src, fmt, tag=""):
+            codes = sb.tile([P, 512], U32, name=name + "_codes", tag=tag, align_bytes=64)
             scales = sb.tile([P, 512], U8, name=name + "_scales", align_bytes=64)
             nc.vector.quantize_mx(out=codes[:].bitcast(fmt), scales=scales[:], in_=src)
             return codes, scales
@@ -99,14 +99,13 @@ def tile_attend_grbf_pl_kernel(tc, xT, cT, hx, cs, cd, dp, us, wt, offs, out_0, 
             for t in range(LANES):
                 nc.tensor.transpose(turned[:, t, :], xd[:, t, :, j], ident_bf[:])
             nc.scalar.copy(out=xr[:, j, :, :], in_=turned[:].rearrange("s t p -> s p t"))
-        xr_codes, xr_scales = quantize("xr", xr[:].rearrange("s j p t -> s (j p t)"), E4M3)
 
         c_pairs = [sb.tile([P, 2, SLOTS], F32, name=f"c_pair{u}") for u in range(2)]
         c_planes = [c_pairs[j // 2][:, j % 2, :] for j in range(LANES)]
         c_words = sb.tile([P, SLOTS, LANES], BF16, name="c_words", tag="late2", align_bytes=64)
-        n2_turned = [ps.tile([P, 2, P], F32, name=f"n2_turned{u}", tag=f"big{2 + u}") for u in range(2)]
+        n2_turned = [ps.tile([P, 2, P], F32, name=f"n2_turned{u}", tag=f"side{2 + u}") for u in range(2)]
         for j in range(LANES):
-            square = sb.tile([P, SLOTS], F32, name=f"square{j}")
+            square = sb.tile([P, SLOTS], F32, name=f"square{j}", tag=f"square{j}", align_bytes=64)
             parts = 2 if j == LANES - 1 else 1
             width = SLOTS // parts
             for part in range(parts):
@@ -123,6 +122,7 @@ def tile_attend_grbf_pl_kernel(tc, xT, cT, hx, cs, cd, dp, us, wt, offs, out_0, 
                 nc.scalar.copy(out=c_words[:, :, 0:2], in_=c_pairs[0][:].rearrange("p e i -> p i e"))
         nc.vector.tensor_copy(out=c_words[:, :, 2:4], in_=c_pairs[1][:].rearrange("p e i -> p i e"))
         c_codes, c_scales = quantize("c", c_words[:].rearrange("p i t -> p (i t)"), E4M3)
+        xr_codes, xr_scales = quantize("xr", xr[:].rearrange("s j p t -> s (j p t)"), E4M3, tag="square3")
         n2_row = sb.tile([P, SLOTS], F32, name="n2_row")
         n2_row_ps = [ps.tile([P, 2 * P], F32, name=f"n2_row_ps{u}", tag=f"side{u}") for u in range(2)]
         for u in range(2):
@@ -131,10 +131,10 @@ def tile_attend_grbf_pl_kernel(tc, xT, cT, hx, cs, cd, dp, us, wt, offs, out_0, 
             nc.scalar.copy(out=n2_row[:, 2 * P * u : 2 * P * (u + 1)], in_=n2_row_ps[u][:])
 
         g_planes = sb.tile([P, LANES, SLOTS], BF16, name="g_planes")
-        sh_turned = ps.tile([P, LANES, P], F32, name="sh_turned", tag="side2")
+        sh_turned = ps.tile([P, LANES, P], F32, name="sh_turned", tag="big0")
         probs = []
         for t in range(LANES):
-            a = ps.tile([P, SLOTS], F32, name=f"a{t}", tag=("big3", "big2", "side0", "side1")[t])
+            a = ps.tile([P, SLOTS], F32, name=f"a{t}", tag=("side3", "side2", "side0", "side1")[t])
             cols = slice(P * t, P * (t + 1))
             nc.tensor.matmul_mx(
                 out=a[:], lhsT=xd_codes[:, cols].bitcast(E4M3), lhsT_scale=xd_scales[:, cols],
@@ -169,15 +169,14 @@ def tile_attend_grbf_pl_kernel(tc, xT, cT, hx, cs, cd, dp, us, wt, offs, out_0, 
                 out=g_words[:, cols, :].rearrange("s (c i) t -> s c t i", i=4),
                 in_=g_planes[:, :, cols].rearrange("s t (c i) -> s c t i", i=4),
             )
-        sh_row = ps.tile([P, SLOTS], F32, name="sh_row", tag="side3")
+        sh_row = ps.tile([P, SLOTS], F32, name="sh_row", tag="big1")
         spread_sums("sh", sh_turned, sh_row, 1.0)
         g_codes, g_scales = quantize("g", g_words[:].rearrange("s i t -> s (i t)"), E5M2)
 
         out_planes = out_0.rearrange("(p j) c -> j p c", j=LANES)
-        chunks = T // CHUNK
-        pairs = [sb.tile([P, 2, CHUNK, 2], BF16, name=f"pairs{k}") for k in range(chunks)]
+        pairs = [sb.tile([P, 2, width, 2], BF16, name=f"pairs{k}") for k, (first, width) in enumerate(CHUNKS)]
         for j in range(LANES):
-            xg_ps = ps.tile([P, SLOTS], F32, name=f"xg{j}", tag=("side2", "big1", "big2", "big3")[j])
+            xg_ps = ps.tile([P, SLOTS], F32, name=f"xg{j}", tag=("big0", "big2", "big3", "side0")[j])
             cols = slice(P * j, P * (j + 1))
             nc.tensor.matmul_mx(
                 out=xg_ps[:], lhsT=xr_codes[:, cols].bitcast(E4M3), lhsT_scale=xr_scales[:, cols],
@@ -190,10 +189,10 @@ def tile_attend_grbf_pl_kernel(tc, xT, cT, hx, cs, cd, dp, us, wt, offs, out_0, 
             nc.vector.tensor_tensor(windows[j][:].indirect(offsets[:]), xg[:], pull[:], ALU.add)
             nc.sync.dma_start(out=out_planes[j], in_=windows[j][:])
         for j in range(LANES):
-            for k in range(chunks):
-                src = windows[j][:, CHUNK * k : CHUNK * (k + 1)]
+            for k, (first, width) in enumerate(CHUNKS):
+                src = windows[j][:, first : first + width]
                 if j == 2 and k < 2:
-                    nc.scalar.copy(out=pairs[k][:, 1, :, :], in_=src.unsqueeze(2).to_broadcast([P, CHUNK, 2]))
+                    nc.scalar.copy(out=pairs[k][:, 1, :, :], in_=src.unsqueeze(2).to_broadcast([P, width, 2]))
                 elif j == 3 and k < 2:
                     nc.vector.tensor_copy(out=pairs[k][:, 1, :, 1], in_=src)
                 else:
@@ -201,16 +200,16 @@ def tile_attend_grbf_pl_kernel(tc, xT, cT, hx, cs, cd, dp, us, wt, offs, out_0, 
 
         y_scales = sb.tile([P, T], U8, name="y_scales", align_bytes=64)
         words_out = out_1[0].rearrange("p c l -> p (c l)").bitcast(I32)
-        for k in range(chunks):
-            y_words = sb.tile([P, CHUNK, LANES], BF16, name=f"y_words{k}", align_bytes=64)
+        for k, (first, width) in enumerate(CHUNKS):
+            y_words = sb.tile([P, width, LANES], BF16, name=f"y_words{k}", align_bytes=64)
             word = I32 if k < 2 else U32
             engine_copy = nc.vector.tensor_copy if k < 2 else nc.scalar.copy
             engine_copy(
                 out=y_words[:].rearrange("p c t -> p (c t)").bitcast(word).rearrange("p (c u) -> p c u", u=2),
                 in_=pairs[k][:].rearrange("p u c e -> p (u c e)").bitcast(word).rearrange("p (u c) -> p c u", u=2),
             )
-            y_codes = sb.tile([P, CHUNK], U32, name=f"y_codes{k}", align_bytes=64)
-            cols = slice(CHUNK * k, CHUNK * (k + 1))
+            y_codes = sb.tile([P, width], U32, name=f"y_codes{k}", align_bytes=64)
+            cols = slice(first, first + width)
             nc.vector.quantize_mx(
                 out=y_codes[:].bitcast(E4M3), scales=y_scales[:, cols], in_=y_words[:].rearrange("p c t -> p (c t)")
             )

@@ -19,9 +19,10 @@ LANES = 4
 D = 512
 R = 512
 SLOTS = 512
+HALF = SLOTS // 2
 T = 2048
 CHUNKS = ((0, 512), (512, 512), (1024, 512), (1536, 256), (1792, 256))
-G_SPLIT = 416
+VECTOR_CHUNKS = 2
 
 FLOPS = 2 * 2 * D * R * SLOTS
 
@@ -32,39 +33,52 @@ def tile_attend_grbf_pl_kernel(tc, xT, cT, hx, cs, cd, dp, us, wt, offs, out_0, 
         sb = ctx.enter_context(tc.tile_pool(name="sb", bufs=1))
         ps = ctx.enter_context(tc.psum_pool(name="ps", bufs=1))
 
-        def quantize(name, src, fmt, tag=""):
-            codes = sb.tile([P, 512], U32, name=name + "_codes", tag=tag, align_bytes=64)
-            scales = sb.tile([P, 512], U8, name=name + "_scales", align_bytes=64)
-            nc.vector.quantize_mx(out=codes[:].bitcast(fmt), scales=scales[:], in_=src)
+        def mx_tiles(name, width):
+            codes = sb.tile([P, width], U32, name=name + "_codes", align_bytes=64)
+            scales = sb.tile([P, width], U8, name=name + "_scales", align_bytes=64)
             return codes, scales
 
-        def column(name, src):
+        def column(name, src, queue):
             col = sb.tile([P, LANES], F32, name=name)
-            nc.scalar.dma_start(out=col[:], in_=src)
+            queue.dma_start(out=col[:], in_=src)
             return col
 
-        def spread_sums(name, turned, row, scale):
-            for b in range(turned.shape[1]):
+        def turn_and_add(turned, plane, first, last):
+            for b in range(2):
+                nc.tensor.matmul(
+                    turned[b], plane[:, P * b : P * (b + 1)], ident[:], is_transpose=True, start=first[b], stop=last[b]
+                )
+
+        def slot_sums(name, turned, scale):
+            cols = []
+            for b in range(2):
                 col = sb.tile([P, 1], F32, name=f"{name}_col{b}")
                 summed = sb.tile([P, P], F32, name=f"{name}_summed{b}")
-                nc.scalar.activation(summed[:], turned[:, b, :], ACT.Identity, scale=scale, accum_out=col[:])
+                nc.scalar.activation(summed[:], turned[b], ACT.Identity, scale=scale, accum_out=col[:])
+                cols.append(col)
+            return cols
+
+        def spread(row, cols):
+            for b, col in enumerate(cols):
                 nc.tensor.transpose(row[:, P * b : P * (b + 1)], col[:].to_broadcast([P, P]), ident[:])
+
+        halves = [slice(HALF * u, HALF * (u + 1)) for u in range(2)]
 
         x_raw = sb.tile([P, LANES, R], F32, name="x_raw")
         nc.sync.dma_start(out=x_raw[:], in_=xT.rearrange("(p j) r -> p j r", j=LANES))
         offsets = sb.tile([P, SLOTS // 16], U16, name="offsets")
         nc.sync.dma_start(offsets[:], offs)
-        cs_col = column("cs_col", cs[0, :].rearrange("(p j) -> p j", j=LANES))
-        us_col = column("us_col", us.rearrange("(s t) o -> s (t o)", t=LANES))
-        hx_col = column("hx_col", hx.rearrange("(s t) o -> s (t o)", t=LANES))
-        wt_col = column("wt_col", wt.rearrange("(s t) o -> s (t o)", t=LANES))
-        cd_col = column("cd_col", cd.rearrange("(p j) o -> p (j o)", j=LANES))
+        cs_col = column("cs_col", cs[0, :].rearrange("(p j) -> p j", j=LANES), nc.scalar)
+        hx_col = column("hx_col", hx.rearrange("(s t) o -> s (t o)", t=LANES), nc.scalar)
         cT_planes = cT.rearrange("(p j) c -> j p c", j=LANES)
         table = []
         for j in range(LANES):
             plane = sb.tile([P, T], F32, name=f"table{j}")
             nc.sync.dma_start(out=plane[:], in_=cT_planes[j])
             table.append(plane)
+        us_col = column("us_col", us.rearrange("(s t) o -> s (t o)", t=LANES), nc.sync)
+        wt_col = column("wt_col", wt.rearrange("(s t) o -> s (t o)", t=LANES), nc.sync)
+        cd_col = column("cd_col", cd.rearrange("(p j) o -> p (j o)", j=LANES), nc.sync)
         dp_sb = sb.tile([P, LANES, SLOTS], F32, name="dp_sb")
         nc.sync.dma_start(out=dp_sb[:], in_=dp.rearrange("(s t) i -> s t i", t=LANES))
 
@@ -72,146 +86,208 @@ def tile_attend_grbf_pl_kernel(tc, xT, cT, hx, cs, cd, dp, us, wt, offs, out_0, 
         make_identity(nc, ident[:])
         ident_bf = sb.tile([P, P], BF16, name="ident_bf")
         make_identity(nc, ident_bf[:])
-        windows = []
-        for j in range(2):
+
+        early = []
+        for j in range(2, LANES):
             window = sb.tile([P, T], F32, name=f"window{j}")
             nc.vector.memset(window[:], 0.0)
-            windows.append(window)
-        neg_hx = sb.tile([P, LANES], F32, name="neg_hx")
-        nc.gpsimd.tensor_scalar(neg_hx[:], hx_col[:], -1.0, 0.0, ALU.mult, ALU.add)
-        neg_cd = sb.tile([P, LANES], F32, name="neg_cd")
-        nc.gpsimd.tensor_scalar(neg_cd[:], cd_col[:], -1.0, 0.0, ALU.mult, ALU.add)
-        neg_cd2 = sb.tile([P, LANES], F32, name="neg_cd2")
-        nc.gpsimd.tensor_tensor(neg_cd2[:], neg_cd[:], cd_col[:], ALU.mult)
-        us_wt = sb.tile([P, LANES], F32, name="us_wt")
-        nc.gpsimd.tensor_tensor(us_wt[:], us_col[:], wt_col[:], ALU.mult)
+            early.append(window)
 
         xd = sb.tile([P, LANES, P, LANES], BF16, name="xd", align_bytes=64)
         nc.vector.tensor_copy(
             out=xd[:].rearrange("p t s j -> p s j t"),
             in_=x_raw[:].rearrange("p j (s t) -> p s j t", t=LANES),
         )
-        xd_codes, xd_scales = quantize("xd", xd[:].rearrange("p t s j -> p (t s j)"), E4M3)
+        xd_codes, xd_scales = mx_tiles("xd", R)
+        nc.vector.quantize_mx(
+            out=xd_codes[:].bitcast(E4M3), scales=xd_scales[:], in_=xd[:].rearrange("p t s j -> p (t s j)")
+        )
 
         xr = sb.tile([P, LANES, P, LANES], BF16, name="xr", align_bytes=64)
         for j in range(LANES):
-            turned = ps.tile([P, LANES, P], BF16, name=f"x_turned{j}", tag=f"big{j}")
+            turned = ps.tile([P, LANES, P], BF16, name=f"x_turned{j}", tag=f"bank{j}")
             for t in range(LANES):
                 nc.tensor.transpose(turned[:, t, :], xd[:, t, :, j], ident_bf[:])
             nc.scalar.copy(out=xr[:, j, :, :], in_=turned[:].rearrange("s t p -> s p t"))
+        xr_codes, xr_scales = mx_tiles("xr", D)
+        nc.vector.quantize_mx(
+            out=xr_codes[:].bitcast(E4M3), scales=xr_scales[:], in_=xr[:].rearrange("s j p t -> s (j p t)")
+        )
 
-        c_pairs = [sb.tile([P, 2, SLOTS], F32, name=f"c_pair{u}") for u in range(2)]
+        c_pairs = [
+            sb.tile([P, 2, SLOTS], F32, name=f"c_pair{u}", tag=("c_pair0", "xr")[u], align_bytes=64) for u in range(2)
+        ]
         c_planes = [c_pairs[j // 2][:, j % 2, :] for j in range(LANES)]
-        c_words = sb.tile([P, SLOTS, LANES], BF16, name="c_words", tag="late2", align_bytes=64)
-        n2_turned = [ps.tile([P, 2, P], F32, name=f"n2_turned{u}", tag=f"side{2 + u}") for u in range(2)]
-        for j in range(LANES):
-            square = sb.tile([P, SLOTS], F32, name=f"square{j}", tag=f"square{j}", align_bytes=64)
-            parts = 2 if j == LANES - 1 else 1
-            width = SLOTS // parts
-            for part in range(parts):
-                cols = slice(width * part, width * (part + 1))
-                listed = offsets[:, width // 16 * part : width // 16 * (part + 1)]
-                nc.vector.tensor_copy(c_planes[j][:, cols], table[j][:].indirect(listed))
-                nc.scalar.activation(square[:, cols], c_planes[j][:, cols], ACT.Square, scale=cs_col[:, j : j + 1])
-            for b in range(LANES):
-                nc.tensor.matmul(
-                    n2_turned[b // 2][:, b % 2, :], square[:, P * b : P * (b + 1)], ident[:], is_transpose=True,
-                    start=(j == 0 and b % 2 == 0), stop=(j == LANES - 1 and b % 2 == 1),
-                )
+        c_words = [sb.tile([P, HALF, LANES], BF16, name=f"c_words{u}", align_bytes=64) for u in range(2)]
+        n2_turned = [
+            [ps.tile([P, P], F32, name=f"n2_turned{u}{b}", tag=f"bank{4 + 2 * u + b}")[:] for b in range(2)]
+            for u in range(2)
+        ]
+        for j in range(LANES - 1):
+            square = sb.tile([P, SLOTS], F32, name=f"square{j}")
+            nc.vector.tensor_copy(c_planes[j], table[j][:].indirect(offsets[:]))
+            nc.scalar.activation(square[:], c_planes[j], ACT.Square, scale=cs_col[:, j : j + 1])
+            for u in range(2):
+                turn_and_add(n2_turned[u], square[:, halves[u]], (j == 0, j == 0), (False, False))
             if j == 1:
-                nc.scalar.copy(out=c_words[:, :, 0:2], in_=c_pairs[0][:].rearrange("p e i -> p i e"))
-        nc.vector.tensor_copy(out=c_words[:, :, 2:4], in_=c_pairs[1][:].rearrange("p e i -> p i e"))
-        c_codes, c_scales = quantize("c", c_words[:].rearrange("p i t -> p (i t)"), E4M3)
-        xr_codes, xr_scales = quantize("xr", xr[:].rearrange("s j p t -> s (j p t)"), E4M3, tag="square3")
-        n2_row = sb.tile([P, SLOTS], F32, name="n2_row")
-        n2_row_ps = [ps.tile([P, 2 * P], F32, name=f"n2_row_ps{u}", tag=f"side{u}") for u in range(2)]
+                for u in range(2):
+                    nc.scalar.copy(
+                        out=c_words[u][:, :, 0:2], in_=c_pairs[0][:, :, halves[u]].rearrange("p e i -> p i e")
+                    )
+        c_mx, n2_rows = [], []
+        last = LANES - 1
         for u in range(2):
-            spread_sums(f"n2_{u}", n2_turned[u], n2_row_ps[u], 0.5)
+            listed = offsets[:, HALF // 16 * u : HALF // 16 * (u + 1)]
+            nc.vector.tensor_copy(c_planes[last][:, halves[u]], table[last][:].indirect(listed))
+            square = sb.tile([P, HALF], F32, name=f"square{last}_{u}")
+            nc.scalar.activation(square[:], c_planes[last][:, halves[u]], ACT.Square, scale=cs_col[:, last:])
+            turn_and_add(n2_turned[u], square[:], (False, False), (True, True))
         for u in range(2):
-            nc.scalar.copy(out=n2_row[:, 2 * P * u : 2 * P * (u + 1)], in_=n2_row_ps[u][:])
+            nc.vector.tensor_copy(
+                out=c_words[u][:, :, 2:4], in_=c_pairs[1][:, :, halves[u]].rearrange("p e i -> p i e")
+            )
+        for u in range(2):
+            codes, scales = mx_tiles(f"c{u}", HALF)
+            nc.vector.quantize_mx(
+                out=codes[:].bitcast(E4M3), scales=scales[:], in_=c_words[u][:].rearrange("p i t -> p (i t)")
+            )
+            c_mx.append((codes, scales))
+            n2_row_ps = ps.tile([P, HALF], F32, name=f"n2_row_ps{u}", tag=f"bank{u}")
+            spread(n2_row_ps, slot_sums(f"n2_{u}", n2_turned[u], 0.5))
+            n2_row = sb.tile([P, HALF], F32, name=f"n2_row{u}")
+            nc.scalar.copy(out=n2_row[:], in_=n2_row_ps[:])
+            n2_rows.append(n2_row)
 
-        g_planes = sb.tile([P, LANES, SLOTS], BF16, name="g_planes")
-        sh_turned = ps.tile([P, LANES, P], F32, name="sh_turned", tag="big0")
-        probs = []
-        for t in range(LANES):
-            a = ps.tile([P, SLOTS], F32, name=f"a{t}", tag=("side3", "side2", "side0", "side1")[t])
-            cols = slice(P * t, P * (t + 1))
-            nc.tensor.matmul_mx(
-                out=a[:], lhsT=xd_codes[:, cols].bitcast(E4M3), lhsT_scale=xd_scales[:, cols],
-                rhs=c_codes[:].bitcast(E4M3), rhs_scale=c_scales[:], start=True, stop=True,
-            )
-            expo = sb.tile([P, SLOTS], F32, name=f"expo{t}", tag="late3" if t == 0 else f"expo{t}", align_bytes=64)
-            nc.vector.scalar_tensor_tensor(expo[:], a[:], us_col[:, t : t + 1], n2_row[:], ALU.mult, ALU.subtract)
-            prob = sb.tile([P, SLOTS], F32, name=f"prob{t}")
-            nc.scalar.activation(prob[:], expo[:], ACT.Exp, bias=neg_hx[:, t : t + 1])
-            probs.append(prob)
-        for j in range(2, LANES):
-            window = sb.tile([P, T], F32, name=f"window{j}", tag=f"late{j}", align_bytes=64)
-            nc.gpsimd.memset(window[:], 0.0)
-            windows.append(window)
-        for t in range(LANES):
-            h = sb.tile([P, SLOTS], F32, name=f"h{t}")
-            nc.vector.scalar_tensor_tensor(h[:], probs[t][:], wt_col[:, t : t + 1], dp_sb[:, t, :], ALU.mult, ALU.mult)
-            for b in range(LANES):
-                nc.tensor.matmul(
-                    sh_turned[:, b, :], h[:, P * b : P * (b + 1)], ident[:], is_transpose=True,
-                    start=(t == 0 and b == 0), stop=(t == LANES - 1 and b == LANES - 1),
-                )
-            if t < LANES - 1:
-                nc.scalar.activation(g_planes[:, t, :], h[:], ACT.Copy, scale=us_col[:, t : t + 1])
-            else:
+        neg_hx = sb.tile([P, LANES], F32, name="neg_hx")
+        nc.gpsimd.tensor_scalar(neg_hx[:], hx_col[:], -1.0, 0.0, ALU.mult, ALU.add)
+
+        probs = {}
+        for u in range(2):
+            codes, scales = c_mx[u]
+            for v in range(2):
+                a = ps.tile([P, 2, HALF], F32, name=f"a{u}{v}", tag=f"bank{4 + 2 * u + v}")
+                for e in range(2):
+                    cols = slice(P * (2 * v + e), P * (2 * v + e + 1))
+                    nc.tensor.matmul_mx(
+                        out=a[:, e, :], lhsT=xd_codes[:, cols].bitcast(E4M3), lhsT_scale=xd_scales[:, cols],
+                        rhs=codes[:].bitcast(E4M3), rhs_scale=scales[:], start=True, stop=True,
+                    )
+                for e in range(2):
+                    t = 2 * v + e
+                    expo = sb.tile([P, HALF], F32, name=f"expo{u}{t}", align_bytes=64)
+                    nc.vector.scalar_tensor_tensor(
+                        expo[:], a[:, e, :], us_col[:, t : t + 1], n2_rows[u][:], ALU.mult, ALU.subtract
+                    )
+                    prob = sb.tile([P, HALF], F32, name=f"prob{u}{t}")
+                    nc.scalar.activation(prob[:], expo[:], ACT.Exp, bias=neg_hx[:, t : t + 1])
+                    probs[u, t] = prob
+        cd2 = sb.tile([P, LANES], F32, name="cd2", tag="expo01", align_bytes=64)
+        nc.gpsimd.tensor_tensor(cd2[:], cd_col[:], cd_col[:], ALU.mult)
+        g_planes = []
+        sh_row = ps.tile([P, SLOTS], F32, name="sh_row", tag="bank0")
+        for u in range(2):
+            planes = sb.tile([P, LANES, HALF], BF16, name=f"g_planes{u}")
+            sh_bank = ps.tile([P, 2, P], F32, name=f"sh_turned{u}", tag=f"bank{2 + u}")
+            sh_turned = [sh_bank[:, b, :] for b in range(2)]
+            for t in range(LANES):
+                h = sb.tile([P, HALF], F32, name=f"h{u}{t}")
                 nc.vector.scalar_tensor_tensor(
-                    g_planes[:, t, :], probs[t][:], us_wt[:, t : t + 1], dp_sb[:, t, :], ALU.mult, ALU.mult
+                    h[:], probs[u, t][:], wt_col[:, t : t + 1], dp_sb[:, t, halves[u]], ALU.mult, ALU.mult
                 )
-        g_words = sb.tile([P, SLOTS, LANES], BF16, name="g_words", align_bytes=64)
-        for engine_copy, cols in ((nc.vector.tensor_copy, slice(0, G_SPLIT)), (nc.scalar.copy, slice(G_SPLIT, SLOTS))):
-            engine_copy(
-                out=g_words[:, cols, :].rearrange("s (c i) t -> s c t i", i=4),
-                in_=g_planes[:, :, cols].rearrange("s t (c i) -> s c t i", i=4),
+                nc.scalar.activation(planes[:, t, :], h[:], ACT.Copy, scale=us_col[:, t : t + 1])
+                turn_and_add(sh_turned, h[:], (t == 0, False), (False, t == last))
+            g_planes.append(planes)
+            spread(sh_row[:, halves[u]], slot_sums(f"sh{u}", sh_turned, 1.0))
+        g_codes, g_scales = mx_tiles("g", SLOTS)
+        g_words = [sb.tile([P, HALF, LANES], BF16, name=f"g_words{u}", align_bytes=64) for u in range(2)]
+        for u in range(2):
+            nc.vector.tensor_copy(
+                out=g_words[u][:].rearrange("s (c i) t -> s c t i", i=4),
+                in_=g_planes[u][:].rearrange("s t (c i) -> s c t i", i=4),
             )
-        sh_row = ps.tile([P, SLOTS], F32, name="sh_row", tag="big1")
-        spread_sums("sh", sh_turned, sh_row, 1.0)
-        g_codes, g_scales = quantize("g", g_words[:].rearrange("s i t -> s (i t)"), E5M2)
+        for u in range(2):
+            nc.vector.quantize_mx(
+                out=g_codes[:, halves[u]].bitcast(E5M2), scales=g_scales[:, halves[u]],
+                in_=g_words[u][:].rearrange("s i t -> s (i t)"),
+            )
+
+        windows = []
+        for j in range(LANES):
+            if j < 2:
+                window = sb.tile([P, T], F32, name=f"window{j}", tag=("expo00", "c_words1")[j], align_bytes=64)
+                nc.gpsimd.memset(window[:], 0.0)
+            else:
+                window = early[j - 2]
+            windows.append(window)
 
         out_planes = out_0.rearrange("(p j) c -> j p c", j=LANES)
-        pairs = [sb.tile([P, 2, width, 2], BF16, name=f"pairs{k}") for k, (first, width) in enumerate(CHUNKS)]
-        for j in range(LANES):
-            xg_ps = ps.tile([P, SLOTS], F32, name=f"xg{j}", tag=("big0", "big2", "big3", "side0")[j])
+        def product(j):
+            xg_ps = ps.tile([P, SLOTS], F32, name=f"xg{j}", tag=f"bank{7 - j}")
             cols = slice(P * j, P * (j + 1))
             nc.tensor.matmul_mx(
                 out=xg_ps[:], lhsT=xr_codes[:, cols].bitcast(E4M3), lhsT_scale=xr_scales[:, cols],
                 rhs=g_codes[:].bitcast(E5M2), rhs_scale=g_scales[:], start=True, stop=True,
             )
-            xg = sb.tile([P, SLOTS], F32, name=f"xg_sb{j}")
-            nc.scalar.copy(out=xg[:], in_=xg_ps[:])
-            pull = sb.tile([P, SLOTS], F32, name=f"pull{j}")
-            nc.vector.scalar_tensor_tensor(pull[:], c_planes[j], neg_cd2[:, j : j + 1], sh_row[:], ALU.mult, ALU.mult)
-            nc.vector.tensor_tensor(windows[j][:].indirect(offsets[:]), xg[:], pull[:], ALU.add)
+            return xg_ps
+
+        def scatter(j, dc):
+            nc.vector.tensor_copy(windows[j][:].indirect(offsets[:]), dc)
             nc.sync.dma_start(out=out_planes[j], in_=windows[j][:])
-        for j in range(LANES):
+
+        xg_ps = product(last)
+        pull = sb.tile([P, SLOTS], F32, name="pull_first")
+        nc.vector.scalar_tensor_tensor(pull[:], c_planes[last], cd2[:, last:], sh_row[:], ALU.mult, ALU.mult)
+        dc = sb.tile([P, SLOTS], F32, name="dc_first")
+        nc.vector.tensor_tensor(dc[:], xg_ps[:], pull[:], ALU.subtract)
+        scatter(last, dc[:])
+        for group, centres in (((2,), c_pairs[1][:, 0:1, :]), ((0, 1), c_pairs[0][:])):
+            shape = [P, len(group), SLOTS]
+            factor = sb.tile(shape, F32, name=f"factor{group[0]}")
+            xg = sb.tile(shape, F32, name=f"xg_sb{group[0]}")
+            for e, j in enumerate(group):
+                nc.scalar.activation(factor[:, e, :], sh_row[:], ACT.Copy, scale=cd2[:, j : j + 1])
+            for e, j in enumerate(group):
+                nc.scalar.copy(out=xg[:, e, :], in_=product(j)[:])
+            pull = sb.tile(shape, F32, name=f"pull{group[0]}", tag="pull")
+            nc.gpsimd.tensor_tensor(pull[:], centres, factor[:], ALU.mult)
+            for e, j in reversed(list(enumerate(group))):
+                dc = sb.tile([P, SLOTS], F32, name=f"dc{j}")
+                nc.gpsimd.tensor_tensor(dc[:], xg[:, e, :], pull[:, e, :], ALU.subtract)
+                scatter(j, dc[:])
+
+        pairs = [sb.tile([P, 2, width, 2], BF16, name=f"pairs{k}") for k, (first, width) in enumerate(CHUNKS)]
+        for j in reversed(range(LANES)):
             for k, (first, width) in enumerate(CHUNKS):
                 src = windows[j][:, first : first + width]
-                if j == 2 and k < 2:
-                    nc.scalar.copy(out=pairs[k][:, 1, :, :], in_=src.unsqueeze(2).to_broadcast([P, width, 2]))
-                elif j == 3 and k < 2:
-                    nc.vector.tensor_copy(out=pairs[k][:, 1, :, 1], in_=src)
-                else:
+                if j == 1 and k < VECTOR_CHUNKS:
+                    engine_copy = nc.gpsimd.tensor_copy if k == 0 else nc.scalar.copy
+                    engine_copy(out=pairs[k][:, 0, :, :], in_=src.unsqueeze(2).to_broadcast([P, width, 2]))
+                elif j == 0 and k < VECTOR_CHUNKS:
+                    nc.vector.tensor_copy(out=pairs[k][:, 0, :, 0], in_=src)
+                elif j > 0:
                     nc.scalar.copy(out=pairs[k][:, j // 2, :, j % 2], in_=src)
 
+        y_words = []
+        for k, (first, width) in enumerate(CHUNKS):
+            words = sb.tile([P, width, LANES], BF16, name=f"y_words{k}", align_bytes=64)
+            on_vector = k < VECTOR_CHUNKS
+            word = I32 if on_vector else U32
+            engine_copy = nc.vector.tensor_copy if on_vector else nc.scalar.copy
+            if not on_vector:
+                nc.scalar.copy(out=pairs[k][:, 0, :, 0], in_=windows[0][:, first : first + width])
+            engine_copy(
+                out=words[:].rearrange("p c t -> p (c t)").bitcast(word).rearrange("p (c u) -> p c u", u=2),
+                in_=pairs[k][:].rearrange("p u c e -> p (u c e)").bitcast(word).rearrange("p (u c) -> p c u", u=2),
+            )
+            y_words.append(words)
         y_scales = sb.tile([P, T], U8, name="y_scales", align_bytes=64)
         words_out = out_1[0].rearrange("p c l -> p (c l)").bitcast(I32)
         for k, (first, width) in enumerate(CHUNKS):
-            y_words = sb.tile([P, width, LANES], BF16, name=f"y_words{k}", align_bytes=64)
-            word = I32 if k < 2 else U32
-            engine_copy = nc.vector.tensor_copy if k < 2 else nc.scalar.copy
-            engine_copy(
-                out=y_words[:].rearrange("p c t -> p (c t)").bitcast(word).rearrange("p (c u) -> p c u", u=2),
-                in_=pairs[k][:].rearrange("p u c e -> p (u c e)").bitcast(word).rearrange("p (u c) -> p c u", u=2),
-            )
             y_codes = sb.tile([P, width], U32, name=f"y_codes{k}", align_bytes=64)
             cols = slice(first, first + width)
             nc.vector.quantize_mx(
-                out=y_codes[:].bitcast(E4M3), scales=y_scales[:, cols], in_=y_words[:].rearrange("p c t -> p (c t)")
+                out=y_codes[:].bitcast(E4M3), scales=y_scales[:, cols],
+                in_=y_words[k][:].rearrange("p c t -> p (c t)"),
             )
             nc.sync.dma_start(out=words_out[:, cols], in_=y_codes[:].bitcast(I32))
         scales_out = out_2[0].bitcast(I32)

@@ -23,6 +23,7 @@ HALF = SLOTS // 2
 T = 2048
 CHUNKS = ((0, 512), (512, 512), (1024, 512), (1536, 256), (1792, 256))
 VECTOR_CHUNKS = 2
+PAIR_WIDTHS = (1024, 512, 256, 256)
 
 FLOPS = 2 * 2 * D * R * SLOTS
 
@@ -136,9 +137,9 @@ def tile_attend_grbf_pl_kernel(tc, xT, cT, hx, cs, cd, dp, us, wt, offs, out_0, 
                     )
         c_mx, n2_rows = [], []
         last = LANES - 1
+        listed = [offsets[:, HALF // 16 * u : HALF // 16 * (u + 1)] for u in range(2)]
         for u in range(2):
-            listed = offsets[:, HALF // 16 * u : HALF // 16 * (u + 1)]
-            nc.vector.tensor_copy(c_planes[last][:, halves[u]], table[last][:].indirect(listed))
+            nc.vector.tensor_copy(c_planes[last][:, halves[u]], table[last][:].indirect(listed[u]))
             square = sb.tile([P, HALF], F32, name=f"square{last}_{u}")
             nc.scalar.activation(square[:], c_planes[last][:, halves[u]], ACT.Square, scale=cs_col[:, last:])
             turn_and_add(n2_turned[u], square[:], (False, False), (True, True))
@@ -183,6 +184,9 @@ def tile_attend_grbf_pl_kernel(tc, xT, cT, hx, cs, cd, dp, us, wt, offs, out_0, 
                     probs[u, t] = prob
         cd2 = sb.tile([P, LANES], F32, name="cd2", tag="expo01", align_bytes=64)
         nc.gpsimd.tensor_tensor(cd2[:], cd_col[:], cd_col[:], ALU.mult)
+        cd2_second = sb.tile([P, 1], F32, name="cd2_second", tag="expo02", align_bytes=64)
+        nc.gpsimd.tensor_tensor(cd2_second[:], cd_col[:, 2:3], cd_col[:, 2:3], ALU.mult)
+        cd2_of = {0: cd2[:, 0:1], 1: cd2[:, 1:2], 2: cd2_second[:]}
         g_planes = []
         sh_row = ps.tile([P, SLOTS], F32, name="sh_row", tag="bank0")
         for u in range(2):
@@ -234,38 +238,55 @@ def tile_attend_grbf_pl_kernel(tc, xT, cT, hx, cs, cd, dp, us, wt, offs, out_0, 
             nc.vector.tensor_copy(windows[j][:].indirect(offsets[:]), dc)
             nc.sync.dma_start(out=out_planes[j], in_=windows[j][:])
 
+        def scaled_sh(factor, j):
+            nc.scalar.activation(factor, sh_row[:], ACT.Copy, scale=cd2_of[j])
+
+        factors = {2: sb.tile([P, 1, SLOTS], F32, name="factor2", align_bytes=64), 0: sb.tile([P, 2, SLOTS], F32, name="factor0")}
         xg_ps = product(last)
         pull = sb.tile([P, SLOTS], F32, name="pull_first")
         nc.vector.scalar_tensor_tensor(pull[:], c_planes[last], cd2[:, last:], sh_row[:], ALU.mult, ALU.mult)
-        dc = sb.tile([P, SLOTS], F32, name="dc_first")
-        nc.vector.tensor_tensor(dc[:], xg_ps[:], pull[:], ALU.subtract)
-        scatter(last, dc[:])
+        dc_halves = [sb.tile([P, HALF], F32, name=f"dc_first{u}") for u in range(2)]
+        for u in range(2):
+            nc.vector.tensor_tensor(dc_halves[u][:], xg_ps[:, halves[u]], pull[:, halves[u]], ALU.subtract)
+        for u in range(2):
+            nc.vector.tensor_copy(windows[last][:].indirect(listed[u]), dc_halves[u][:])
+        nc.sync.dma_start(out=out_planes[last], in_=windows[last][:])
         for group, centres in (((2,), c_pairs[1][:, 0:1, :]), ((0, 1), c_pairs[0][:])):
             shape = [P, len(group), SLOTS]
-            factor = sb.tile(shape, F32, name=f"factor{group[0]}")
-            xg = sb.tile(shape, F32, name=f"xg_sb{group[0]}")
+            factor = factors[group[0]]
+            xg = sb.tile(
+                shape, F32, name=f"xg_sb{group[0]}", tag="expo02" if group[0] == 2 else "factor2", align_bytes=64
+            )
             for e, j in enumerate(group):
-                nc.scalar.activation(factor[:, e, :], sh_row[:], ACT.Copy, scale=cd2[:, j : j + 1])
-            for e, j in enumerate(group):
+                scaled_sh(factor[:, e, :], j)
+            for e, j in reversed(list(enumerate(group))):
                 nc.scalar.copy(out=xg[:, e, :], in_=product(j)[:])
             pull = sb.tile(shape, F32, name=f"pull{group[0]}", tag="pull")
             nc.gpsimd.tensor_tensor(pull[:], centres, factor[:], ALU.mult)
             for e, j in reversed(list(enumerate(group))):
-                dc = sb.tile([P, SLOTS], F32, name=f"dc{j}")
+                dc = sb.tile([P, SLOTS], F32, name=f"dc{j}", tag="pull_first" if j == 2 else f"dc{j}")
                 nc.gpsimd.tensor_tensor(dc[:], xg[:, e, :], pull[:, e, :], ALU.subtract)
                 scatter(j, dc[:])
 
-        pairs = [sb.tile([P, 2, width, 2], BF16, name=f"pairs{k}") for k, (first, width) in enumerate(CHUNKS)]
-        for j in reversed(range(LANES)):
+        pair_tiles = [
+            sb.tile([P, 2, width, 2], BF16, name=f"pairs{k}", align_bytes=64) for k, width in enumerate(PAIR_WIDTHS)
+        ]
+        pairs = []
+        for k, (first, width) in enumerate(CHUNKS):
+            if k < VECTOR_CHUNKS:
+                pairs.append(pair_tiles[0][:, :, first : first + width, :])
+            else:
+                pairs.append(pair_tiles[k - VECTOR_CHUNKS + 1][:])
+        for j in (3, 2):
             for k, (first, width) in enumerate(CHUNKS):
-                src = windows[j][:, first : first + width]
-                if j == 1 and k < VECTOR_CHUNKS:
-                    engine_copy = nc.gpsimd.tensor_copy if k == 0 else nc.scalar.copy
-                    engine_copy(out=pairs[k][:, 0, :, :], in_=src.unsqueeze(2).to_broadcast([P, width, 2]))
-                elif j == 0 and k < VECTOR_CHUNKS:
-                    nc.vector.tensor_copy(out=pairs[k][:, 0, :, 0], in_=src)
-                elif j > 0:
-                    nc.scalar.copy(out=pairs[k][:, j // 2, :, j % 2], in_=src)
+                nc.scalar.copy(out=pairs[k][:, 1, :, j % 2], in_=windows[j][:, first : first + width])
+        src = windows[1][:, 0 : PAIR_WIDTHS[0]]
+        nc.gpsimd.tensor_copy(out=pair_tiles[0][:, 0, :, :], in_=src.unsqueeze(2).to_broadcast([P, PAIR_WIDTHS[0], 2]))
+        for k, (first, width) in enumerate(CHUNKS):
+            if k >= VECTOR_CHUNKS:
+                nc.scalar.copy(out=pairs[k][:, 0, :, 1], in_=windows[1][:, first : first + width])
+        for k, (first, width) in enumerate(CHUNKS[:VECTOR_CHUNKS]):
+            nc.vector.tensor_copy(out=pairs[k][:, 0, :, 0], in_=windows[0][:, first : first + width])
 
         y_words = []
         for k, (first, width) in enumerate(CHUNKS):
@@ -277,13 +298,14 @@ def tile_attend_grbf_pl_kernel(tc, xT, cT, hx, cs, cd, dp, us, wt, offs, out_0, 
                 nc.scalar.copy(out=pairs[k][:, 0, :, 0], in_=windows[0][:, first : first + width])
             engine_copy(
                 out=words[:].rearrange("p c t -> p (c t)").bitcast(word).rearrange("p (c u) -> p c u", u=2),
-                in_=pairs[k][:].rearrange("p u c e -> p (u c e)").bitcast(word).rearrange("p (u c) -> p c u", u=2),
+                in_=pairs[k].bitcast(word).rearrange("p u c o -> p (c o) u"),
             )
             y_words.append(words)
         y_scales = sb.tile([P, T], U8, name="y_scales", align_bytes=64)
         words_out = out_1[0].rearrange("p c l -> p (c l)").bitcast(I32)
         for k, (first, width) in enumerate(CHUNKS):
-            y_codes = sb.tile([P, width], U32, name=f"y_codes{k}", align_bytes=64)
+            freed = ("y_codes0", "y_codes1", "pairs0", "y_words0", "y_words1")[k]
+            y_codes = sb.tile([P, width], U32, name=f"y_codes{k}", tag=freed, align_bytes=64)
             cols = slice(first, first + width)
             nc.vector.quantize_mx(
                 out=y_codes[:].bitcast(E4M3), scales=y_scales[:, cols],

@@ -140,7 +140,7 @@ def tile_attend_grbf_pl_kernel(tc, xT, cT, hx, cs, cd, dp, us, wt, offs, out_0, 
         listed = [offsets[:, HALF // 16 * u : HALF // 16 * (u + 1)] for u in range(2)]
         for u in range(2):
             nc.vector.tensor_copy(c_planes[last][:, halves[u]], table[last][:].indirect(listed[u]))
-            square = sb.tile([P, HALF], F32, name=f"square{last}_{u}")
+            square = sb.tile([P, HALF], F32, name=f"square{last}_{u}", align_bytes=64)
             nc.scalar.activation(square[:], c_planes[last][:, halves[u]], ACT.Square, scale=cs_col[:, last:])
             turn_and_add(n2_turned[u], square[:], (False, False), (True, True))
         for u in range(2):
@@ -162,11 +162,13 @@ def tile_attend_grbf_pl_kernel(tc, xT, cT, hx, cs, cd, dp, us, wt, offs, out_0, 
         neg_hx = sb.tile([P, LANES], F32, name="neg_hx")
         nc.gpsimd.tensor_scalar(neg_hx[:], hx_col[:], -1.0, 0.0, ALU.mult, ALU.add)
 
-        probs = {}
+        g_planes = []
+        sh_row = ps.tile([P, SLOTS], F32, name="sh_row", tag="bank4")
         for u in range(2):
             codes, scales = c_mx[u]
+            probs = []
             for v in range(2):
-                a = ps.tile([P, 2, HALF], F32, name=f"a{u}{v}", tag=f"bank{4 + 2 * u + v}")
+                a = ps.tile([P, 2, HALF], F32, name=f"a{u}{v}", tag=f"bank{((6, 7), (0, 1))[u][v]}")
                 for e in range(2):
                     cols = slice(P * (2 * v + e), P * (2 * v + e + 1))
                     nc.tensor.matmul_mx(
@@ -181,27 +183,24 @@ def tile_attend_grbf_pl_kernel(tc, xT, cT, hx, cs, cd, dp, us, wt, offs, out_0, 
                     )
                     prob = sb.tile([P, HALF], F32, name=f"prob{u}{t}")
                     nc.scalar.activation(prob[:], expo[:], ACT.Exp, bias=neg_hx[:, t : t + 1])
-                    probs[u, t] = prob
-        cd2 = sb.tile([P, LANES], F32, name="cd2", tag="expo01", align_bytes=64)
-        nc.gpsimd.tensor_tensor(cd2[:], cd_col[:], cd_col[:], ALU.mult)
-        cd2_second = sb.tile([P, 1], F32, name="cd2_second", tag="expo02", align_bytes=64)
-        nc.gpsimd.tensor_tensor(cd2_second[:], cd_col[:, 2:3], cd_col[:, 2:3], ALU.mult)
-        cd2_of = {0: cd2[:, 0:1], 1: cd2[:, 1:2], 2: cd2_second[:]}
-        g_planes = []
-        sh_row = ps.tile([P, SLOTS], F32, name="sh_row", tag="bank0")
-        for u in range(2):
+                    probs.append(prob)
             planes = sb.tile([P, LANES, HALF], BF16, name=f"g_planes{u}")
             sh_bank = ps.tile([P, 2, P], F32, name=f"sh_turned{u}", tag=f"bank{2 + u}")
             sh_turned = [sh_bank[:, b, :] for b in range(2)]
             for t in range(LANES):
                 h = sb.tile([P, HALF], F32, name=f"h{u}{t}")
                 nc.vector.scalar_tensor_tensor(
-                    h[:], probs[u, t][:], wt_col[:, t : t + 1], dp_sb[:, t, halves[u]], ALU.mult, ALU.mult
+                    h[:], probs[t][:], wt_col[:, t : t + 1], dp_sb[:, t, halves[u]], ALU.mult, ALU.mult
                 )
                 nc.scalar.activation(planes[:, t, :], h[:], ACT.Copy, scale=us_col[:, t : t + 1])
                 turn_and_add(sh_turned, h[:], (t == 0, False), (False, t == last))
             g_planes.append(planes)
             spread(sh_row[:, halves[u]], slot_sums(f"sh{u}", sh_turned, 1.0))
+        cd2 = sb.tile([P, LANES], F32, name="cd2", tag="c_words0", align_bytes=64)
+        nc.vector.tensor_tensor(cd2[:], cd_col[:], cd_col[:], ALU.mult)
+        cd2_second = sb.tile([P, 1], F32, name="cd2_second", tag="square3_0", align_bytes=64)
+        nc.vector.tensor_tensor(cd2_second[:], cd_col[:, 2:3], cd_col[:, 2:3], ALU.mult)
+        cd2_of = {0: cd2[:, 0:1], 1: cd2[:, 1:2], 2: cd2_second[:]}
         g_codes, g_scales = mx_tiles("g", SLOTS)
         g_words = [sb.tile([P, HALF, LANES], BF16, name=f"g_words{u}", align_bytes=64) for u in range(2)]
         for u in range(2):
@@ -226,7 +225,7 @@ def tile_attend_grbf_pl_kernel(tc, xT, cT, hx, cs, cd, dp, us, wt, offs, out_0, 
 
         out_planes = out_0.rearrange("(p j) c -> j p c", j=LANES)
         def product(j):
-            xg_ps = ps.tile([P, SLOTS], F32, name=f"xg{j}", tag=f"bank{7 - j}")
+            xg_ps = ps.tile([P, SLOTS], F32, name=f"xg{j}", tag=f"bank{(1, 0, 7, 6)[j]}")
             cols = slice(P * j, P * (j + 1))
             nc.tensor.matmul_mx(
                 out=xg_ps[:], lhsT=xr_codes[:, cols].bitcast(E4M3), lhsT_scale=xr_scales[:, cols],
@@ -255,7 +254,7 @@ def tile_attend_grbf_pl_kernel(tc, xT, cT, hx, cs, cd, dp, us, wt, offs, out_0, 
             shape = [P, len(group), SLOTS]
             factor = factors[group[0]]
             xg = sb.tile(
-                shape, F32, name=f"xg_sb{group[0]}", tag="expo02" if group[0] == 2 else "factor2", align_bytes=64
+                shape, F32, name=f"xg_sb{group[0]}", tag="square3_0" if group[0] == 2 else "factor2", align_bytes=64
             )
             for e, j in enumerate(group):
                 scaled_sh(factor[:, e, :], j)

@@ -300,18 +300,19 @@ def tile_attend_grbf_pl_kernel(tc, xT, cT, hx, cs, cd, dp, us, wt, offs, out_0, 
                 in_=pairs[k].bitcast(word).rearrange("p u c o -> p (c o) u"),
             )
             y_words.append(words)
-        y_scales = sb.tile([P, T], U8, name="y_scales", align_bytes=64)
+        y_scales = sb.tile([P, T // 2], U8, name="y_scales", align_bytes=64)
         words_out = out_1[0].rearrange("p c l -> p (c l)").bitcast(I32)
         for k, (first, width) in enumerate(CHUNKS):
             freed = ("y_codes0", "y_codes1", "pairs0", "y_words0", "y_words1")[k]
             y_codes = sb.tile([P, width], U32, name=f"y_codes{k}", tag=freed, align_bytes=64)
             cols = slice(first, first + width)
+            upper, place = divmod(first, T // 2)
             nc.vector.quantize_mx(
-                out=y_codes[:].bitcast(E4M3), scales=y_scales[:, cols],
+                out=y_codes[:].bitcast(E4M3), scales=y_scales[4 * upper :, place : place + width],
                 in_=y_words[k][:].rearrange("p c t -> p (c t)"),
             )
             nc.sync.dma_start(out=words_out[:, cols], in_=y_codes[:].bitcast(I32))
-        scales_out = out_2[0].bitcast(I32)
+        scales_out = out_2[0].bitcast(I32).rearrange("f (h c) -> h f c", h=2)
         for q in range(4):
             queue = nc.scalar if q < 2 else nc.sync
-            queue.dma_start(out=scales_out[4 * q : 4 * q + 4, :], in_=y_scales[32 * q : 32 * q + 4, :].bitcast(I32))
+            queue.dma_start(out=scales_out[:, 4 * q : 4 * q + 4, :], in_=y_scales[32 * q : 32 * q + 8, :].bitcast(I32))

@@ -195,13 +195,20 @@ def tile_attend_grbf_pl_kernel(tc, xT, cT, hx, cs, cd, dp, us, wt, offs, out_0, 
                 nc.scalar.activation(planes[:, t, :], h[:], ACT.Copy, scale=us_col[:, t : t + 1])
                 turn_and_add(sh_turned, h[:], (t == 0, False), (False, t == last))
             g_planes.append(planes)
-            spread(sh_row[:, halves[u]], slot_sums(f"sh{u}", sh_turned, 1.0))
+            sh_cols = slot_sums(f"sh{u}", sh_turned, 1.0)
+            if u == 0:
+                sh_first = ps.tile([P, HALF], F32, name="sh_first", tag="bank2")
+                spread(sh_first, sh_cols)
+            spread(sh_row[:, halves[u]], sh_cols)
         cd2 = sb.tile([P, LANES], F32, name="cd2", tag="c_words0", align_bytes=64)
         nc.vector.tensor_tensor(cd2[:], cd_col[:], cd_col[:], ALU.mult)
         cd2_second = sb.tile([P, 1], F32, name="cd2_second", tag="square3_0", align_bytes=64)
         nc.vector.tensor_tensor(cd2_second[:], cd_col[:, 2:3], cd_col[:, 2:3], ALU.mult)
         cd2_of = {0: cd2[:, 0:1], 1: cd2[:, 1:2], 2: cd2_second[:]}
-        g_codes, g_scales = mx_tiles("g", SLOTS)
+        g_all_codes, g_all_scales = mx_tiles("g", HALF + SLOTS)
+        nc.gpsimd.memset(g_all_codes[:, :HALF], 0)
+        nc.gpsimd.memset(g_all_scales[:, :HALF], 0)
+        g_codes, g_scales = g_all_codes[:, HALF:], g_all_scales[:, HALF:]
         g_words = [sb.tile([P, HALF, LANES], BF16, name=f"g_words{u}", align_bytes=64) for u in range(2)]
         for u in range(2):
             nc.vector.tensor_copy(
@@ -229,7 +236,7 @@ def tile_attend_grbf_pl_kernel(tc, xT, cT, hx, cs, cd, dp, us, wt, offs, out_0, 
             cols = slice(P * j, P * (j + 1))
             nc.tensor.matmul_mx(
                 out=xg_ps[:], lhsT=xr_codes[:, cols].bitcast(E4M3), lhsT_scale=xr_scales[:, cols],
-                rhs=g_codes[:].bitcast(E5M2), rhs_scale=g_scales[:], start=True, stop=True,
+                rhs=g_codes.bitcast(E5M2), rhs_scale=g_scales, start=True, stop=True,
             )
             return xg_ps
 
@@ -241,14 +248,22 @@ def tile_attend_grbf_pl_kernel(tc, xT, cT, hx, cs, cd, dp, us, wt, offs, out_0, 
             nc.scalar.activation(factor, sh_row[:], ACT.Copy, scale=cd2_of[j])
 
         factors = {2: sb.tile([P, 1, SLOTS], F32, name="factor2", align_bytes=64), 0: sb.tile([P, 2, SLOTS], F32, name="factor0")}
-        xg_ps = product(last)
-        pull = sb.tile([P, SLOTS], F32, name="pull_first")
-        nc.vector.scalar_tensor_tensor(pull[:], c_planes[last], cd2[:, last:], sh_row[:], ALU.mult, ALU.mult)
-        dc_halves = [sb.tile([P, HALF], F32, name=f"dc_first{u}") for u in range(2)]
+        early_ps = ps.tile([P, SLOTS], F32, name="xg_early", tag="bank5")
+        nc.tensor.matmul_mx(
+            out=early_ps[:], lhsT=xr_codes[:, P * last :].bitcast(E4M3), lhsT_scale=xr_scales[:, P * last :],
+            rhs=g_all_codes[:, :SLOTS].bitcast(E5M2), rhs_scale=g_all_scales[:, :SLOTS], start=True, stop=True,
+        )
+        xg_halves = [early_ps[:, HALF:], product(last)[:, HALF:]]
         for u in range(2):
-            nc.vector.tensor_tensor(dc_halves[u][:], xg_ps[:, halves[u]], pull[:, halves[u]], ALU.subtract)
-        for u in range(2):
-            nc.vector.tensor_copy(windows[last][:].indirect(listed[u]), dc_halves[u][:])
+            pull = sb.tile([P, HALF], F32, name=f"pull_first{u}")
+            nc.vector.scalar_tensor_tensor(
+                pull[:], c_planes[last][:, halves[u]], cd2[:, last:], (sh_first[:], sh_row[:, HALF:])[u], ALU.mult, ALU.mult
+            )
+            dc = sb.tile([P, HALF], F32, name=f"dc_first{u}", tag="g_words1", align_bytes=64)
+            nc.vector.tensor_tensor(dc[:], xg_halves[u], pull[:], ALU.subtract)
+            nc.vector.tensor_copy(windows[last][:].indirect(listed[u]), dc[:])
+            if u == 0:
+                scaled_sh(factors[2][:, 0, :], 2)
         nc.sync.dma_start(out=out_planes[last], in_=windows[last][:])
         for group, centres in (((2,), c_pairs[1][:, 0:1, :]), ((0, 1), c_pairs[0][:])):
             shape = [P, len(group), SLOTS]
@@ -257,13 +272,14 @@ def tile_attend_grbf_pl_kernel(tc, xT, cT, hx, cs, cd, dp, us, wt, offs, out_0, 
                 shape, F32, name=f"xg_sb{group[0]}", tag="square3_0" if group[0] == 2 else "factor2", align_bytes=64
             )
             for e, j in enumerate(group):
-                scaled_sh(factor[:, e, :], j)
+                if j < 2:
+                    scaled_sh(factor[:, e, :], j)
             for e, j in reversed(list(enumerate(group))):
                 nc.scalar.copy(out=xg[:, e, :], in_=product(j)[:])
             pull = sb.tile(shape, F32, name=f"pull{group[0]}", tag="pull")
             nc.gpsimd.tensor_tensor(pull[:], centres, factor[:], ALU.mult)
             for e, j in reversed(list(enumerate(group))):
-                dc = sb.tile([P, SLOTS], F32, name=f"dc{j}", tag="pull_first" if j == 2 else f"dc{j}")
+                dc = sb.tile([P, SLOTS], F32, name=f"dc{j}", tag="pull_first0" if j == 2 else f"dc{j}")
                 nc.gpsimd.tensor_tensor(dc[:], xg[:, e, :], pull[:, e, :], ALU.subtract)
                 scatter(j, dc[:])
 

@@ -188,7 +188,7 @@ def tile_attend_grbf_pl_kernel(tc, xT, cT, hx, cs, cd, dp, us, wt, offs, out_0, 
             sh_bank = ps.tile([P, 2, P], F32, name=f"sh_turned{u}", tag=f"bank{2 + u}")
             sh_turned = [sh_bank[:, b, :] for b in range(2)]
             for t in range(LANES):
-                h = sb.tile([P, HALF], F32, name=f"h{u}{t}")
+                h = sb.tile([P, HALF], F32, name=f"h{u}{t}", align_bytes=64)
                 nc.vector.scalar_tensor_tensor(
                     h[:], probs[t][:], wt_col[:, t : t + 1], dp_sb[:, t, halves[u]], ALU.mult, ALU.mult
                 )
@@ -259,7 +259,7 @@ def tile_attend_grbf_pl_kernel(tc, xT, cT, hx, cs, cd, dp, us, wt, offs, out_0, 
             nc.vector.scalar_tensor_tensor(
                 pull[:], c_planes[last][:, halves[u]], cd2[:, last:], (sh_first[:], sh_row[:, HALF:])[u], ALU.mult, ALU.mult
             )
-            dc = sb.tile([P, HALF], F32, name=f"dc_first{u}", tag="g_words1", align_bytes=64)
+            dc = sb.tile([P, HALF], F32, name=f"dc_first{u}", tag=("h13", "dc_first1")[u], align_bytes=64)
             nc.vector.tensor_tensor(dc[:], xg_halves[u], pull[:], ALU.subtract)
             nc.vector.tensor_copy(windows[last][:].indirect(listed[u]), dc[:])
             if u == 0:

@@ -23,6 +23,7 @@ HALF = SLOTS // 2
 T = 2048
 CHUNKS = ((0, 512), (512, 512), (1024, 512), (1536, 256), (1792, 256))
 VECTOR_CHUNKS = 2
+SCORE_BANKS = ((((0,), 6), ((1,), 7), ((2, 3), 0)), (((0, 1), 6), ((2, 3), 7)))
 PAIR_WIDTHS = (1024, 512, 256, 256)
 
 FLOPS = 2 * 2 * D * R * SLOTS
@@ -135,7 +136,14 @@ def tile_attend_grbf_pl_kernel(tc, xT, cT, hx, cs, cd, dp, us, wt, offs, out_0, 
                     nc.scalar.copy(
                         out=c_words[u][:, :, 0:2], in_=c_pairs[0][:, :, halves[u]].rearrange("p e i -> p i e")
                     )
-        c_mx, n2_rows = [], []
+        def n2_as_row(u):
+            n2_row_ps = ps.tile([P, HALF], F32, name=f"n2_row_ps{u}", tag=f"bank{u}")
+            spread(n2_row_ps, n2_cols[u])
+            row = sb.tile([P, HALF], F32, name=f"n2_row{u}")
+            nc.scalar.copy(out=row[:], in_=n2_row_ps[:])
+            return row
+
+        c_mx, n2_cols = [], []
         last = LANES - 1
         listed = [offsets[:, HALF // 16 * u : HALF // 16 * (u + 1)] for u in range(2)]
         for u in range(2):
@@ -153,11 +161,9 @@ def tile_attend_grbf_pl_kernel(tc, xT, cT, hx, cs, cd, dp, us, wt, offs, out_0, 
                 out=codes[:].bitcast(E4M3), scales=scales[:], in_=c_words[u][:].rearrange("p i t -> p (i t)")
             )
             c_mx.append((codes, scales))
-            n2_row_ps = ps.tile([P, HALF], F32, name=f"n2_row_ps{u}", tag=f"bank{u}")
-            spread(n2_row_ps, slot_sums(f"n2_{u}", n2_turned[u], 0.5))
-            n2_row = sb.tile([P, HALF], F32, name=f"n2_row{u}")
-            nc.scalar.copy(out=n2_row[:], in_=n2_row_ps[:])
-            n2_rows.append(n2_row)
+            n2_cols.append(slot_sums(f"n2_{u}", n2_turned[u], 0.5))
+            if u == 0:
+                n2_row = n2_as_row(u)
 
         neg_hx = sb.tile([P, LANES], F32, name="neg_hx")
         nc.gpsimd.tensor_scalar(neg_hx[:], hx_col[:], -1.0, 0.0, ALU.mult, ALU.add)
@@ -166,20 +172,21 @@ def tile_attend_grbf_pl_kernel(tc, xT, cT, hx, cs, cd, dp, us, wt, offs, out_0, 
         sh_row = ps.tile([P, SLOTS], F32, name="sh_row", tag="bank4")
         for u in range(2):
             codes, scales = c_mx[u]
+            if u == 1:
+                n2_row = n2_as_row(u)
             probs = []
-            for v in range(2):
-                a = ps.tile([P, 2, HALF], F32, name=f"a{u}{v}", tag=f"bank{((6, 7), (0, 1))[u][v]}")
-                for e in range(2):
-                    cols = slice(P * (2 * v + e), P * (2 * v + e + 1))
+            for group, bank in SCORE_BANKS[u]:
+                a = ps.tile([P, len(group), HALF], F32, name=f"a{u}{group[0]}", tag=f"bank{bank}")
+                for e, t in enumerate(group):
+                    cols = slice(P * t, P * (t + 1))
                     nc.tensor.matmul_mx(
                         out=a[:, e, :], lhsT=xd_codes[:, cols].bitcast(E4M3), lhsT_scale=xd_scales[:, cols],
                         rhs=codes[:].bitcast(E4M3), rhs_scale=scales[:], start=True, stop=True,
                     )
-                for e in range(2):
-                    t = 2 * v + e
+                for e, t in enumerate(group):
                     expo = sb.tile([P, HALF], F32, name=f"expo{u}{t}", align_bytes=64)
                     nc.vector.scalar_tensor_tensor(
-                        expo[:], a[:, e, :], us_col[:, t : t + 1], n2_rows[u][:], ALU.mult, ALU.subtract
+                        expo[:], a[:, e, :], us_col[:, t : t + 1], n2_row[:], ALU.mult, ALU.subtract
                     )
                     prob = sb.tile([P, HALF], F32, name=f"prob{u}{t}")
                     nc.scalar.activation(prob[:], expo[:], ACT.Exp, bias=neg_hx[:, t : t + 1])
@@ -204,7 +211,9 @@ def tile_attend_grbf_pl_kernel(tc, xT, cT, hx, cs, cd, dp, us, wt, offs, out_0, 
         nc.vector.tensor_tensor(cd2[:], cd_col[:], cd_col[:], ALU.mult)
         cd2_second = sb.tile([P, 1], F32, name="cd2_second", tag="square3_0", align_bytes=64)
         nc.vector.tensor_tensor(cd2_second[:], cd_col[:, 2:3], cd_col[:, 2:3], ALU.mult)
-        cd2_of = {0: cd2[:, 0:1], 1: cd2[:, 1:2], 2: cd2_second[:]}
+        neg_cd2 = sb.tile([P, 1], F32, name="neg_cd2")
+        nc.vector.tensor_scalar_mul(neg_cd2[:], cd2[:, 1:2], -1.0)
+        cd2_of = {0: cd2[:, 0:1], 1: neg_cd2[:], 2: cd2_second[:]}
         g_all_codes, g_all_scales = mx_tiles("g", HALF + SLOTS)
         nc.gpsimd.memset(g_all_codes[:, :HALF], 0)
         nc.gpsimd.memset(g_all_scales[:, :HALF], 0)
@@ -232,7 +241,7 @@ def tile_attend_grbf_pl_kernel(tc, xT, cT, hx, cs, cd, dp, us, wt, offs, out_0, 
 
         out_planes = out_0.rearrange("(p j) c -> j p c", j=LANES)
         def product(j):
-            xg_ps = ps.tile([P, SLOTS], F32, name=f"xg{j}", tag=f"bank{(1, 0, 7, 6)[j]}")
+            xg_ps = ps.tile([P, SLOTS], F32, name=f"xg{j}", tag=f"bank{(6, 7, 1, 0)[j]}")
             cols = slice(P * j, P * (j + 1))
             nc.tensor.matmul_mx(
                 out=xg_ps[:], lhsT=xr_codes[:, cols].bitcast(E4M3), lhsT_scale=xr_scales[:, cols],
@@ -253,7 +262,8 @@ def tile_attend_grbf_pl_kernel(tc, xT, cT, hx, cs, cd, dp, us, wt, offs, out_0, 
             out=early_ps[:], lhsT=xr_codes[:, P * last :].bitcast(E4M3), lhsT_scale=xr_scales[:, P * last :],
             rhs=g_all_codes[:, :SLOTS].bitcast(E5M2), rhs_scale=g_all_scales[:, :SLOTS], start=True, stop=True,
         )
-        xg_halves = [early_ps[:, HALF:], product(last)[:, HALF:]]
+        products = {j: product(j) for j in (2, 3, 1, 0)}
+        xg_halves = [early_ps[:, HALF:], products[last][:, HALF:]]
         for u in range(2):
             pull = sb.tile([P, HALF], F32, name=f"pull_first{u}")
             nc.vector.scalar_tensor_tensor(
@@ -275,13 +285,17 @@ def tile_attend_grbf_pl_kernel(tc, xT, cT, hx, cs, cd, dp, us, wt, offs, out_0, 
                 if j < 2:
                     scaled_sh(factor[:, e, :], j)
             for e, j in reversed(list(enumerate(group))):
-                nc.scalar.copy(out=xg[:, e, :], in_=product(j)[:])
+                nc.scalar.copy(out=xg[:, e, :], in_=products[j][:])
             pull = sb.tile(shape, F32, name=f"pull{group[0]}", tag="pull")
             nc.gpsimd.tensor_tensor(pull[:], centres, factor[:], ALU.mult)
             for e, j in reversed(list(enumerate(group))):
-                dc = sb.tile([P, SLOTS], F32, name=f"dc{j}", tag="pull_first0" if j == 2 else f"dc{j}")
-                nc.gpsimd.tensor_tensor(dc[:], xg[:, e, :], pull[:, e, :], ALU.subtract)
-                scatter(j, dc[:])
+                if j == 1:
+                    nc.vector.tensor_tensor(windows[j][:].indirect(offsets[:]), xg[:, e, :], pull[:, e, :], ALU.add)
+                    nc.sync.dma_start(out=out_planes[j], in_=windows[j][:])
+                else:
+                    dc = sb.tile([P, SLOTS], F32, name=f"dc{j}", tag="pull_first0" if j == 2 else f"dc{j}")
+                    nc.gpsimd.tensor_tensor(dc[:], xg[:, e, :], pull[:, e, :], ALU.subtract)
+                    scatter(j, dc[:])
 
         pair_tiles = [
             sb.tile([P, 2, width, 2], BF16, name=f"pairs{k}", align_bytes=64) for k, width in enumerate(PAIR_WIDTHS)

@@ -211,9 +211,7 @@ def tile_attend_grbf_pl_kernel(tc, xT, cT, hx, cs, cd, dp, us, wt, offs, out_0, 
         nc.vector.tensor_tensor(cd2[:], cd_col[:], cd_col[:], ALU.mult)
         cd2_second = sb.tile([P, 1], F32, name="cd2_second", tag="square3_0", align_bytes=64)
         nc.vector.tensor_tensor(cd2_second[:], cd_col[:, 2:3], cd_col[:, 2:3], ALU.mult)
-        neg_cd2 = sb.tile([P, 1], F32, name="neg_cd2")
-        nc.vector.tensor_scalar_mul(neg_cd2[:], cd2[:, 1:2], -1.0)
-        cd2_of = {0: cd2[:, 0:1], 1: neg_cd2[:], 2: cd2_second[:]}
+        cd2_of = {0: cd2[:, 0:1], 1: cd2[:, 1:2], 2: cd2_second[:]}
         g_all_codes, g_all_scales = mx_tiles("g", HALF + SLOTS)
         nc.gpsimd.memset(g_all_codes[:, :HALF], 0)
         nc.gpsimd.memset(g_all_scales[:, :HALF], 0)
@@ -256,7 +254,7 @@ def tile_attend_grbf_pl_kernel(tc, xT, cT, hx, cs, cd, dp, us, wt, offs, out_0, 
         def scaled_sh(factor, j):
             nc.scalar.activation(factor, sh_row[:], ACT.Copy, scale=cd2_of[j])
 
-        factors = {2: sb.tile([P, 1, SLOTS], F32, name="factor2", align_bytes=64), 0: sb.tile([P, 2, SLOTS], F32, name="factor0")}
+        factors = {2: sb.tile([P, SLOTS], F32, name="factor2", align_bytes=64)}
         early_ps = ps.tile([P, SLOTS], F32, name="xg_early", tag="bank5")
         nc.tensor.matmul_mx(
             out=early_ps[:], lhsT=xr_codes[:, P * last :].bitcast(E4M3), lhsT_scale=xr_scales[:, P * last :],
@@ -273,29 +271,22 @@ def tile_attend_grbf_pl_kernel(tc, xT, cT, hx, cs, cd, dp, us, wt, offs, out_0, 
             nc.vector.tensor_tensor(dc[:], xg_halves[u], pull[:], ALU.subtract)
             nc.vector.tensor_copy(windows[last][:].indirect(listed[u]), dc[:])
             if u == 0:
-                scaled_sh(factors[2][:, 0, :], 2)
+                scaled_sh(factors[2][:], 2)
         nc.sync.dma_start(out=out_planes[last], in_=windows[last][:])
-        for group, centres in (((2,), c_pairs[1][:, 0:1, :]), ((0, 1), c_pairs[0][:])):
-            shape = [P, len(group), SLOTS]
-            factor = factors[group[0]]
-            xg = sb.tile(
-                shape, F32, name=f"xg_sb{group[0]}", tag="square3_0" if group[0] == 2 else "factor2", align_bytes=64
-            )
-            for e, j in enumerate(group):
-                if j < 2:
-                    scaled_sh(factor[:, e, :], j)
-            for e, j in reversed(list(enumerate(group))):
-                nc.scalar.copy(out=xg[:, e, :], in_=products[j][:])
-            pull = sb.tile(shape, F32, name=f"pull{group[0]}", tag="pull")
-            nc.gpsimd.tensor_tensor(pull[:], centres, factor[:], ALU.mult)
-            for e, j in reversed(list(enumerate(group))):
-                if j == 1:
-                    nc.vector.tensor_tensor(windows[j][:].indirect(offsets[:]), xg[:, e, :], pull[:, e, :], ALU.add)
-                    nc.sync.dma_start(out=out_planes[j], in_=windows[j][:])
-                else:
-                    dc = sb.tile([P, SLOTS], F32, name=f"dc{j}", tag="pull_first0" if j == 2 else f"dc{j}")
-                    nc.gpsimd.tensor_tensor(dc[:], xg[:, e, :], pull[:, e, :], ALU.subtract)
-                    scatter(j, dc[:])
+        for j in (2, 1, 0):
+            if j < 2:
+                factors[j] = sb.tile([P, SLOTS], F32, name=f"factor{j}")
+                scaled_sh(factors[j][:], j)
+            xg = sb.tile([P, SLOTS], F32, name=f"xg_sb{j}", tag=("xg_sb0", "factor2", "square3_0")[j], align_bytes=64)
+            nc.scalar.copy(out=xg[:], in_=products[j][:])
+            pull = sb.tile([P, SLOTS], F32, name=f"pull{j}", tag="pull")
+            dc = sb.tile([P, SLOTS], F32, name=f"dc{j}", tag="pull_first0" if j == 2 else f"dc{j}")
+            parts = halves if j == 0 else [slice(0, SLOTS)]
+            for part in parts:
+                nc.gpsimd.tensor_tensor(pull[:, part], c_planes[j][:, part], factors[j][:, part], ALU.mult)
+            for part in parts:
+                nc.gpsimd.tensor_tensor(dc[:, part], xg[:, part], pull[:, part], ALU.subtract)
+            scatter(j, dc[:])
 
         pair_tiles = [
             sb.tile([P, 2, width, 2], BF16, name=f"pairs{k}", align_bytes=64) for k, width in enumerate(PAIR_WIDTHS)
@@ -317,14 +308,15 @@ def tile_attend_grbf_pl_kernel(tc, xT, cT, hx, cs, cd, dp, us, wt, offs, out_0, 
         for k, (first, width) in enumerate(CHUNKS[:VECTOR_CHUNKS]):
             nc.vector.tensor_copy(out=pairs[k][:, 0, :, 0], in_=windows[0][:, first : first + width])
 
+        for k, (first, width) in enumerate(CHUNKS):
+            if k >= VECTOR_CHUNKS:
+                nc.scalar.copy(out=pairs[k][:, 0, :, 0], in_=windows[0][:, first : first + width])
         y_words = []
         for k, (first, width) in enumerate(CHUNKS):
             words = sb.tile([P, width, LANES], BF16, name=f"y_words{k}", align_bytes=64)
             on_vector = k < VECTOR_CHUNKS
             word = I32 if on_vector else U32
             engine_copy = nc.vector.tensor_copy if on_vector else nc.scalar.copy
-            if not on_vector:
-                nc.scalar.copy(out=pairs[k][:, 0, :, 0], in_=windows[0][:, first : first + width])
             engine_copy(
                 out=words[:].rearrange("p c t -> p (c t)").bitcast(word).rearrange("p (c u) -> p c u", u=2),
                 in_=pairs[k].bitcast(word).rearrange("p u c o -> p (c o) u"),

@@ -16,15 +16,19 @@ ALU = mybir.AluOpType
 
 P = 128
 LANES = 4
+LAST = LANES - 1
 D = 512
 R = 512
 SLOTS = 512
 HALF = SLOTS // 2
 T = 2048
+
 CHUNKS = ((0, 512), (512, 512), (1024, 512), (1536, 256), (1792, 256))
 VECTOR_CHUNKS = 2
-SCORE_BANKS = ((((0,), 6), ((1,), 7), ((2, 3), 0)), (((0, 1), 6), ((2, 3), 7)))
 PAIR_WIDTHS = (1024, 512, 256, 256)
+SCALAR_MIDDLE = 256
+SCORE_BANKS = ((((0,), 6), ((1,), 7), ((2, 3), 0)), (((0, 1), 6), ((2, 3), 7)))
+PRODUCT_BANKS = (6, 7, 1, 0)
 
 FLOPS = 2 * 2 * D * R * SLOTS
 
@@ -40,29 +44,29 @@ def tile_attend_grbf_pl_kernel(tc, xT, cT, hx, cs, cd, dp, us, wt, offs, out_0, 
             scales = sb.tile([P, width], U8, name=name + "_scales", align_bytes=64)
             return codes, scales
 
-        def column(name, src, queue):
-            col = sb.tile([P, LANES], F32, name=name)
-            queue.dma_start(out=col[:], in_=src)
-            return col
+        def by_lane(name, src, queue):
+            vector = sb.tile([P, LANES], F32, name=name)
+            queue.dma_start(out=vector[:], in_=src)
+            return vector
 
-        def turn_and_add(turned, plane, first, last):
+        def turn_and_add(turned, plane, start, stop):
             for b in range(2):
                 nc.tensor.matmul(
-                    turned[b], plane[:, P * b : P * (b + 1)], ident[:], is_transpose=True, start=first[b], stop=last[b]
+                    turned[b], plane[:, P * b : P * (b + 1)], ident[:], is_transpose=True, start=start[b], stop=stop[b]
                 )
 
         def slot_sums(name, turned, scale):
-            cols = []
+            sums = []
             for b in range(2):
-                col = sb.tile([P, 1], F32, name=f"{name}_col{b}")
-                summed = sb.tile([P, P], F32, name=f"{name}_summed{b}")
-                nc.scalar.activation(summed[:], turned[b], ACT.Identity, scale=scale, accum_out=col[:])
-                cols.append(col)
-            return cols
+                total = sb.tile([P, 1], F32, name=f"{name}_col{b}")
+                terms = sb.tile([P, P], F32, name=f"{name}_summed{b}")
+                nc.scalar.activation(terms[:], turned[b], ACT.Identity, scale=scale, accum_out=total[:])
+                sums.append(total)
+            return sums
 
-        def spread(row, cols):
-            for b, col in enumerate(cols):
-                nc.tensor.transpose(row[:, P * b : P * (b + 1)], col[:].to_broadcast([P, P]), ident[:])
+        def spread(row, sums):
+            for b, total in enumerate(sums):
+                nc.tensor.transpose(row[:, P * b : P * (b + 1)], total[:].to_broadcast([P, P]), ident[:])
 
         halves = [slice(HALF * u, HALF * (u + 1)) for u in range(2)]
 
@@ -70,17 +74,17 @@ def tile_attend_grbf_pl_kernel(tc, xT, cT, hx, cs, cd, dp, us, wt, offs, out_0, 
         nc.sync.dma_start(out=x_raw[:], in_=xT.rearrange("(p j) r -> p j r", j=LANES))
         offsets = sb.tile([P, SLOTS // 16], U16, name="offsets")
         nc.sync.dma_start(offsets[:], offs)
-        cs_col = column("cs_col", cs[0, :].rearrange("(p j) -> p j", j=LANES), nc.scalar)
-        hx_col = column("hx_col", hx.rearrange("(s t) o -> s (t o)", t=LANES), nc.scalar)
+        cs_col = by_lane("cs_col", cs[0, :].rearrange("(p j) -> p j", j=LANES), nc.scalar)
+        hx_col = by_lane("hx_col", hx.rearrange("(s t) o -> s (t o)", t=LANES), nc.scalar)
         cT_planes = cT.rearrange("(p j) c -> j p c", j=LANES)
         table = []
         for j in range(LANES):
             plane = sb.tile([P, T], F32, name=f"table{j}")
             nc.sync.dma_start(out=plane[:], in_=cT_planes[j])
             table.append(plane)
-        us_col = column("us_col", us.rearrange("(s t) o -> s (t o)", t=LANES), nc.sync)
-        wt_col = column("wt_col", wt.rearrange("(s t) o -> s (t o)", t=LANES), nc.sync)
-        cd_col = column("cd_col", cd.rearrange("(p j) o -> p (j o)", j=LANES), nc.sync)
+        us_col = by_lane("us_col", us.rearrange("(s t) o -> s (t o)", t=LANES), nc.sync)
+        wt_col = by_lane("wt_col", wt.rearrange("(s t) o -> s (t o)", t=LANES), nc.sync)
+        cd_col = by_lane("cd_col", cd.rearrange("(p j) o -> p (j o)", j=LANES), nc.sync)
         dp_sb = sb.tile([P, LANES, SLOTS], F32, name="dp_sb")
         nc.sync.dma_start(out=dp_sb[:], in_=dp.rearrange("(s t) i -> s t i", t=LANES))
 
@@ -89,11 +93,10 @@ def tile_attend_grbf_pl_kernel(tc, xT, cT, hx, cs, cd, dp, us, wt, offs, out_0, 
         ident_bf = sb.tile([P, P], BF16, name="ident_bf")
         make_identity(nc, ident_bf[:])
 
-        early = []
-        for j in range(2, LANES):
-            window = sb.tile([P, T], F32, name=f"window{j}")
-            nc.vector.memset(window[:], 0.0)
-            early.append(window)
+        windows = {}
+        for j in (2, 3):
+            windows[j] = sb.tile([P, T], F32, name=f"window{j}")
+            nc.vector.memset(windows[j][:], 0.0)
 
         xd = sb.tile([P, LANES, P, LANES], BF16, name="xd", align_bytes=64)
         nc.vector.tensor_copy(
@@ -125,7 +128,7 @@ def tile_attend_grbf_pl_kernel(tc, xT, cT, hx, cs, cd, dp, us, wt, offs, out_0, 
             [ps.tile([P, P], F32, name=f"n2_turned{u}{b}", tag=f"bank{4 + 2 * u + b}")[:] for b in range(2)]
             for u in range(2)
         ]
-        for j in range(LANES - 1):
+        for j in range(LAST):
             square = sb.tile([P, SLOTS], F32, name=f"square{j}")
             nc.vector.tensor_copy(c_planes[j], table[j][:].indirect(offsets[:]))
             nc.scalar.activation(square[:], c_planes[j], ACT.Square, scale=cs_col[:, j : j + 1])
@@ -136,37 +139,39 @@ def tile_attend_grbf_pl_kernel(tc, xT, cT, hx, cs, cd, dp, us, wt, offs, out_0, 
                     nc.scalar.copy(
                         out=c_words[u][:, :, 0:2], in_=c_pairs[0][:, :, halves[u]].rearrange("p e i -> p i e")
                     )
-        def n2_as_row(u):
-            n2_row_ps = ps.tile([P, HALF], F32, name=f"n2_row_ps{u}", tag=f"bank{u}")
-            spread(n2_row_ps, n2_cols[u])
-            row = sb.tile([P, HALF], F32, name=f"n2_row{u}")
-            nc.scalar.copy(out=row[:], in_=n2_row_ps[:])
-            return row
-
-        c_mx, n2_cols = [], []
-        last = LANES - 1
-        listed = [offsets[:, HALF // 16 * u : HALF // 16 * (u + 1)] for u in range(2)]
+        half_lists = [offsets[:, HALF // 16 * u : HALF // 16 * (u + 1)] for u in range(2)]
         for u in range(2):
-            nc.vector.tensor_copy(c_planes[last][:, halves[u]], table[last][:].indirect(listed[u]))
-            square = sb.tile([P, HALF], F32, name=f"square{last}_{u}", align_bytes=64)
-            nc.scalar.activation(square[:], c_planes[last][:, halves[u]], ACT.Square, scale=cs_col[:, last:])
+            nc.vector.tensor_copy(c_planes[LAST][:, halves[u]], table[LAST][:].indirect(half_lists[u]))
+            square = sb.tile([P, HALF], F32, name=f"square{LAST}_{u}", align_bytes=64)
+            nc.scalar.activation(square[:], c_planes[LAST][:, halves[u]], ACT.Square, scale=cs_col[:, LAST:])
             turn_and_add(n2_turned[u], square[:], (False, False), (True, True))
         for u in range(2):
             nc.vector.tensor_copy(
                 out=c_words[u][:, :, 2:4], in_=c_pairs[1][:, :, halves[u]].rearrange("p e i -> p i e")
             )
+
+        def n2_as_row(u):
+            spread_ps = ps.tile([P, HALF], F32, name=f"n2_row_ps{u}", tag=f"bank{u}")
+            spread(spread_ps, n2_sums[u])
+            row = sb.tile([P, HALF], F32, name=f"n2_row{u}")
+            nc.scalar.copy(out=row[:], in_=spread_ps[:])
+            return row
+
+        c_mx, n2_sums = [], []
         for u in range(2):
             codes, scales = mx_tiles(f"c{u}", HALF)
             nc.vector.quantize_mx(
                 out=codes[:].bitcast(E4M3), scales=scales[:], in_=c_words[u][:].rearrange("p i t -> p (i t)")
             )
             c_mx.append((codes, scales))
-            n2_cols.append(slot_sums(f"n2_{u}", n2_turned[u], 0.5))
+            n2_sums.append(slot_sums(f"n2_{u}", n2_turned[u], 0.5))
             if u == 0:
                 n2_row = n2_as_row(u)
 
         neg_hx = sb.tile([P, LANES], F32, name="neg_hx")
         nc.gpsimd.tensor_scalar(neg_hx[:], hx_col[:], -1.0, 0.0, ALU.mult, ALU.add)
+        us_wt = sb.tile([P, 1], F32, name="us_wt", tag="square3_1", align_bytes=64)
+        nc.vector.tensor_tensor(us_wt[:], us_col[:, LAST:], wt_col[:, LAST:], ALU.mult)
 
         g_planes = []
         sh_row = ps.tile([P, SLOTS], F32, name="sh_row", tag="bank4")
@@ -191,7 +196,7 @@ def tile_attend_grbf_pl_kernel(tc, xT, cT, hx, cs, cd, dp, us, wt, offs, out_0, 
                     prob = sb.tile([P, HALF], F32, name=f"prob{u}{t}")
                     nc.scalar.activation(prob[:], expo[:], ACT.Exp, bias=neg_hx[:, t : t + 1])
                     probs.append(prob)
-            planes = sb.tile([P, LANES, HALF], BF16, name=f"g_planes{u}")
+            g_half = sb.tile([P, LANES, HALF], BF16, name=f"g_planes{u}")
             sh_bank = ps.tile([P, 2, P], F32, name=f"sh_turned{u}", tag=f"bank{2 + u}")
             sh_turned = [sh_bank[:, b, :] for b in range(2)]
             for t in range(LANES):
@@ -199,19 +204,26 @@ def tile_attend_grbf_pl_kernel(tc, xT, cT, hx, cs, cd, dp, us, wt, offs, out_0, 
                 nc.vector.scalar_tensor_tensor(
                     h[:], probs[t][:], wt_col[:, t : t + 1], dp_sb[:, t, halves[u]], ALU.mult, ALU.mult
                 )
-                nc.scalar.activation(planes[:, t, :], h[:], ACT.Copy, scale=us_col[:, t : t + 1])
-                turn_and_add(sh_turned, h[:], (t == 0, False), (False, t == last))
-            g_planes.append(planes)
-            sh_cols = slot_sums(f"sh{u}", sh_turned, 1.0)
+                if (u, t) == (1, LAST):
+                    nc.vector.scalar_tensor_tensor(
+                        g_half[:, t, :], probs[t][:], us_wt[:], dp_sb[:, t, halves[u]], ALU.mult, ALU.mult
+                    )
+                else:
+                    nc.scalar.activation(g_half[:, t, :], h[:], ACT.Copy, scale=us_col[:, t : t + 1])
+                turn_and_add(sh_turned, h[:], (t == 0, False), (False, t == LAST))
+            g_planes.append(g_half)
+            sh_sums = slot_sums(f"sh{u}", sh_turned, 1.0)
             if u == 0:
                 sh_first = ps.tile([P, HALF], F32, name="sh_first", tag="bank2")
-                spread(sh_first, sh_cols)
-            spread(sh_row[:, halves[u]], sh_cols)
+                spread(sh_first, sh_sums)
+            spread(sh_row[:, halves[u]], sh_sums)
+
         cd2 = sb.tile([P, LANES], F32, name="cd2", tag="c_words0", align_bytes=64)
         nc.vector.tensor_tensor(cd2[:], cd_col[:], cd_col[:], ALU.mult)
-        cd2_second = sb.tile([P, 1], F32, name="cd2_second", tag="square3_0", align_bytes=64)
-        nc.vector.tensor_tensor(cd2_second[:], cd_col[:, 2:3], cd_col[:, 2:3], ALU.mult)
-        cd2_of = {0: cd2[:, 0:1], 1: cd2[:, 1:2], 2: cd2_second[:]}
+        cd2_plane2 = sb.tile([P, 1], F32, name="cd2_plane2", tag="square3_0", align_bytes=64)
+        nc.vector.tensor_tensor(cd2_plane2[:], cd_col[:, 2:3], cd_col[:, 2:3], ALU.mult)
+        cd2_of = {0: cd2[:, 0:1], 1: cd2[:, 1:2], 2: cd2_plane2[:]}
+
         g_all_codes, g_all_scales = mx_tiles("g", HALF + SLOTS)
         nc.gpsimd.memset(g_all_codes[:, :HALF], 0)
         nc.gpsimd.memset(g_all_scales[:, :HALF], 0)
@@ -228,18 +240,14 @@ def tile_attend_grbf_pl_kernel(tc, xT, cT, hx, cs, cd, dp, us, wt, offs, out_0, 
                 in_=g_words[u][:].rearrange("s i t -> s (i t)"),
             )
 
-        windows = []
-        for j in range(LANES):
-            if j < 2:
-                window = sb.tile([P, T], F32, name=f"window{j}", tag=("expo00", "c_words1")[j], align_bytes=64)
-                nc.gpsimd.memset(window[:], 0.0)
-            else:
-                window = early[j - 2]
-            windows.append(window)
+        for j, freed in ((0, "expo00"), (1, "c_words1")):
+            windows[j] = sb.tile([P, T], F32, name=f"window{j}", tag=freed, align_bytes=64)
+            nc.gpsimd.memset(windows[j][:], 0.0)
 
         out_planes = out_0.rearrange("(p j) c -> j p c", j=LANES)
+
         def product(j):
-            xg_ps = ps.tile([P, SLOTS], F32, name=f"xg{j}", tag=f"bank{(6, 7, 1, 0)[j]}")
+            xg_ps = ps.tile([P, SLOTS], F32, name=f"xg{j}", tag=f"bank{PRODUCT_BANKS[j]}")
             cols = slice(P * j, P * (j + 1))
             nc.tensor.matmul_mx(
                 out=xg_ps[:], lhsT=xr_codes[:, cols].bitcast(E4M3), lhsT_scale=xr_scales[:, cols],
@@ -247,46 +255,48 @@ def tile_attend_grbf_pl_kernel(tc, xT, cT, hx, cs, cd, dp, us, wt, offs, out_0, 
             )
             return xg_ps
 
-        def scatter(j, dc):
-            nc.vector.tensor_copy(windows[j][:].indirect(offsets[:]), dc)
-            nc.sync.dma_start(out=out_planes[j], in_=windows[j][:])
-
-        def scaled_sh(factor, j):
+        def sh_factor(factor, j):
             nc.scalar.activation(factor, sh_row[:], ACT.Copy, scale=cd2_of[j])
 
         factors = {2: sb.tile([P, SLOTS], F32, name="factor2", align_bytes=64)}
         early_ps = ps.tile([P, SLOTS], F32, name="xg_early", tag="bank5")
         nc.tensor.matmul_mx(
-            out=early_ps[:], lhsT=xr_codes[:, P * last :].bitcast(E4M3), lhsT_scale=xr_scales[:, P * last :],
+            out=early_ps[:], lhsT=xr_codes[:, P * LAST :].bitcast(E4M3), lhsT_scale=xr_scales[:, P * LAST :],
             rhs=g_all_codes[:, :SLOTS].bitcast(E5M2), rhs_scale=g_all_scales[:, :SLOTS], start=True, stop=True,
         )
         products = {j: product(j) for j in (2, 3, 1, 0)}
-        xg_halves = [early_ps[:, HALF:], products[last][:, HALF:]]
-        for u in range(2):
+
+        xg_halves = [early_ps[:, HALF:], products[LAST][:, HALF:]]
+        for u, parts in enumerate(([slice(0, HALF)], [slice(0, P), slice(P, HALF)])):
             pull = sb.tile([P, HALF], F32, name=f"pull_first{u}")
-            nc.vector.scalar_tensor_tensor(
-                pull[:], c_planes[last][:, halves[u]], cd2[:, last:], (sh_first[:], sh_row[:, HALF:])[u], ALU.mult, ALU.mult
-            )
+            centres, sh_half = c_planes[LAST][:, halves[u]], (sh_first[:], sh_row[:, HALF:])[u]
+            for part in parts:
+                nc.vector.scalar_tensor_tensor(
+                    pull[:, part], centres[:, part], cd2[:, LAST:], sh_half[:, part], ALU.mult, ALU.mult
+                )
             dc = sb.tile([P, HALF], F32, name=f"dc_first{u}", tag=("h13", "dc_first1")[u], align_bytes=64)
-            nc.vector.tensor_tensor(dc[:], xg_halves[u], pull[:], ALU.subtract)
-            nc.vector.tensor_copy(windows[last][:].indirect(listed[u]), dc[:])
+            for part in parts:
+                nc.vector.tensor_tensor(dc[:, part], xg_halves[u][:, part], pull[:, part], ALU.subtract)
+            nc.vector.tensor_copy(windows[LAST][:].indirect(half_lists[u]), dc[:])
             if u == 0:
-                scaled_sh(factors[2][:], 2)
-        nc.sync.dma_start(out=out_planes[last], in_=windows[last][:])
+                sh_factor(factors[2][:], 2)
+        nc.sync.dma_start(out=out_planes[LAST], in_=windows[LAST][:])
+
         for j in (2, 1, 0):
             if j < 2:
                 factors[j] = sb.tile([P, SLOTS], F32, name=f"factor{j}")
-                scaled_sh(factors[j][:], j)
+                sh_factor(factors[j][:], j)
             xg = sb.tile([P, SLOTS], F32, name=f"xg_sb{j}", tag=("xg_sb0", "factor2", "square3_0")[j], align_bytes=64)
             nc.scalar.copy(out=xg[:], in_=products[j][:])
-            pull = sb.tile([P, SLOTS], F32, name=f"pull{j}", tag="pull")
+            pull = sb.tile([P, SLOTS], F32, name=f"pull{j}", tag="g_words1", align_bytes=64)
             dc = sb.tile([P, SLOTS], F32, name=f"dc{j}", tag="pull_first0" if j == 2 else f"dc{j}")
             parts = halves if j == 0 else [slice(0, SLOTS)]
             for part in parts:
                 nc.gpsimd.tensor_tensor(pull[:, part], c_planes[j][:, part], factors[j][:, part], ALU.mult)
             for part in parts:
                 nc.gpsimd.tensor_tensor(dc[:, part], xg[:, part], pull[:, part], ALU.subtract)
-            scatter(j, dc[:])
+            nc.vector.tensor_copy(windows[j][:].indirect(offsets[:]), dc[:])
+            nc.sync.dma_start(out=out_planes[j], in_=windows[j][:])
 
         pair_tiles = [
             sb.tile([P, 2, width, 2], BF16, name=f"pairs{k}", align_bytes=64) for k, width in enumerate(PAIR_WIDTHS)
@@ -298,43 +308,48 @@ def tile_attend_grbf_pl_kernel(tc, xT, cT, hx, cs, cd, dp, us, wt, offs, out_0, 
             else:
                 pairs.append(pair_tiles[k - VECTOR_CHUNKS + 1][:])
         for j in (3, 2):
-            for k, (first, width) in enumerate(CHUNKS):
-                nc.scalar.copy(out=pairs[k][:, 1, :, j % 2], in_=windows[j][:, first : first + width])
-        src = windows[1][:, 0 : PAIR_WIDTHS[0]]
-        nc.gpsimd.tensor_copy(out=pair_tiles[0][:, 0, :, :], in_=src.unsqueeze(2).to_broadcast([P, PAIR_WIDTHS[0], 2]))
-        for k, (first, width) in enumerate(CHUNKS):
-            if k >= VECTOR_CHUNKS:
-                nc.scalar.copy(out=pairs[k][:, 0, :, 1], in_=windows[1][:, first : first + width])
+            first = 0
+            for tile, width in zip(pair_tiles, PAIR_WIDTHS):
+                nc.scalar.copy(out=tile[:, 1, :, j % 2], in_=windows[j][:, first : first + width])
+                first += width
+        outer = (PAIR_WIDTHS[0] - SCALAR_MIDDLE) // 2
+        step = outer + SCALAR_MIDDLE
+        src = windows[1][:, 0 : 2 * step].rearrange("p (a c) -> p a c", a=2)[:, :, 0:outer]
+        dst = pair_tiles[0][:].rearrange("p u c e -> p (u c) e")[:, 0 : 2 * step, :]
+        dst = dst.rearrange("p (a c) e -> p a c e", a=2)[:, :, 0:outer, :]
+        nc.gpsimd.tensor_copy(out=dst, in_=src.unsqueeze(3).to_broadcast([P, 2, outer, 2]))
+        src = windows[1][:, outer:step]
+        nc.scalar.copy(out=pair_tiles[0][:, 0, outer:step, :], in_=src.unsqueeze(2).to_broadcast([P, SCALAR_MIDDLE, 2]))
+        scalar_chunks = list(enumerate(CHUNKS))[VECTOR_CHUNKS:]
+        for k, (first, width) in scalar_chunks:
+            nc.scalar.copy(out=pairs[k][:, 0, :, 1], in_=windows[1][:, first : first + width])
         for k, (first, width) in enumerate(CHUNKS[:VECTOR_CHUNKS]):
             nc.vector.tensor_copy(out=pairs[k][:, 0, :, 0], in_=windows[0][:, first : first + width])
+        for k, (first, width) in scalar_chunks:
+            nc.scalar.copy(out=pairs[k][:, 0, :, 0], in_=windows[0][:, first : first + width])
 
-        for k, (first, width) in enumerate(CHUNKS):
-            if k >= VECTOR_CHUNKS:
-                nc.scalar.copy(out=pairs[k][:, 0, :, 0], in_=windows[0][:, first : first + width])
         y_words = []
         for k, (first, width) in enumerate(CHUNKS):
             words = sb.tile([P, width, LANES], BF16, name=f"y_words{k}", align_bytes=64)
-            on_vector = k < VECTOR_CHUNKS
-            word = I32 if on_vector else U32
-            engine_copy = nc.vector.tensor_copy if on_vector else nc.scalar.copy
+            raw, engine_copy = (I32, nc.vector.tensor_copy) if k < VECTOR_CHUNKS else (U32, nc.scalar.copy)
             engine_copy(
-                out=words[:].rearrange("p c t -> p (c t)").bitcast(word).rearrange("p (c u) -> p c u", u=2),
-                in_=pairs[k].bitcast(word).rearrange("p u c o -> p (c o) u"),
+                out=words[:].rearrange("p c t -> p (c t)").bitcast(raw).rearrange("p (c u) -> p c u", u=2),
+                in_=pairs[k].bitcast(raw).rearrange("p u c o -> p (c o) u"),
             )
             y_words.append(words)
+
         y_scales = sb.tile([P, T // 2], U8, name="y_scales", align_bytes=64)
         words_out = out_1[0].rearrange("p c l -> p (c l)").bitcast(I32)
+        code_buffers = ("y_codes0", "y_codes1", "pairs0", "y_words0", "y_words1")
         for k, (first, width) in enumerate(CHUNKS):
-            freed = ("y_codes0", "y_codes1", "pairs0", "y_words0", "y_words1")[k]
-            y_codes = sb.tile([P, width], U32, name=f"y_codes{k}", tag=freed, align_bytes=64)
-            cols = slice(first, first + width)
+            y_codes = sb.tile([P, width], U32, name=f"y_codes{k}", tag=code_buffers[k], align_bytes=64)
             upper, place = divmod(first, T // 2)
             nc.vector.quantize_mx(
                 out=y_codes[:].bitcast(E4M3), scales=y_scales[4 * upper :, place : place + width],
                 in_=y_words[k][:].rearrange("p c t -> p (c t)"),
             )
-            nc.sync.dma_start(out=words_out[:, cols], in_=y_codes[:].bitcast(I32))
-        scales_out = out_2[0].bitcast(I32).rearrange("f (h c) -> h f c", h=2)
+            nc.sync.dma_start(out=words_out[:, first : first + width], in_=y_codes[:].bitcast(I32))
+        scales_out = out_2[0].bitcast(I32).rearrange("f (upper c) -> upper f c", upper=2)
         for q in range(4):
             queue = nc.scalar if q < 2 else nc.sync
             queue.dma_start(out=scales_out[:, 4 * q : 4 * q + 4, :], in_=y_scales[32 * q : 32 * q + 8, :].bitcast(I32))

@@ -26,7 +26,6 @@ T = 2048
 CHUNKS = ((0, 512), (512, 512), (1024, 512), (1536, 256), (1792, 256))
 VECTOR_CHUNKS = 2
 PAIR_WIDTHS = (1024, 512, 256, 256)
-SCALAR_MIDDLE = 256
 SCORE_BANKS = ((((0,), 6), ((1,), 7), ((2, 3), 0)), (((0, 1), 6), ((2, 3), 7)))
 PRODUCT_BANKS = (6, 7, 1, 0)
 
@@ -170,8 +169,6 @@ def tile_attend_grbf_pl_kernel(tc, xT, cT, hx, cs, cd, dp, us, wt, offs, out_0, 
 
         neg_hx = sb.tile([P, LANES], F32, name="neg_hx")
         nc.gpsimd.tensor_scalar(neg_hx[:], hx_col[:], -1.0, 0.0, ALU.mult, ALU.add)
-        us_wt = sb.tile([P, 1], F32, name="us_wt", tag="square3_1", align_bytes=64)
-        nc.vector.tensor_tensor(us_wt[:], us_col[:, LAST:], wt_col[:, LAST:], ALU.mult)
 
         g_planes = []
         sh_row = ps.tile([P, SLOTS], F32, name="sh_row", tag="bank4")
@@ -204,12 +201,7 @@ def tile_attend_grbf_pl_kernel(tc, xT, cT, hx, cs, cd, dp, us, wt, offs, out_0, 
                 nc.vector.scalar_tensor_tensor(
                     h[:], probs[t][:], wt_col[:, t : t + 1], dp_sb[:, t, halves[u]], ALU.mult, ALU.mult
                 )
-                if (u, t) == (1, LAST):
-                    nc.vector.scalar_tensor_tensor(
-                        g_half[:, t, :], probs[t][:], us_wt[:], dp_sb[:, t, halves[u]], ALU.mult, ALU.mult
-                    )
-                else:
-                    nc.scalar.activation(g_half[:, t, :], h[:], ACT.Copy, scale=us_col[:, t : t + 1])
+                nc.scalar.activation(g_half[:, t, :], h[:], ACT.Copy, scale=us_col[:, t : t + 1])
                 turn_and_add(sh_turned, h[:], (t == 0, False), (False, t == LAST))
             g_planes.append(g_half)
             sh_sums = slot_sums(f"sh{u}", sh_turned, 1.0)
@@ -288,7 +280,7 @@ def tile_attend_grbf_pl_kernel(tc, xT, cT, hx, cs, cd, dp, us, wt, offs, out_0, 
                 sh_factor(factors[j][:], j)
             xg = sb.tile([P, SLOTS], F32, name=f"xg_sb{j}", tag=("xg_sb0", "factor2", "square3_0")[j], align_bytes=64)
             nc.scalar.copy(out=xg[:], in_=products[j][:])
-            pull = sb.tile([P, SLOTS], F32, name=f"pull{j}", tag="g_words1", align_bytes=64)
+            pull = sb.tile([P, SLOTS], F32, name=f"pull{j}", tag="pull")
             dc = sb.tile([P, SLOTS], F32, name=f"dc{j}", tag="pull_first0" if j == 2 else f"dc{j}")
             parts = halves if j == 0 else [slice(0, SLOTS)]
             for part in parts:
@@ -312,14 +304,8 @@ def tile_attend_grbf_pl_kernel(tc, xT, cT, hx, cs, cd, dp, us, wt, offs, out_0, 
             for tile, width in zip(pair_tiles, PAIR_WIDTHS):
                 nc.scalar.copy(out=tile[:, 1, :, j % 2], in_=windows[j][:, first : first + width])
                 first += width
-        outer = (PAIR_WIDTHS[0] - SCALAR_MIDDLE) // 2
-        step = outer + SCALAR_MIDDLE
-        src = windows[1][:, 0 : 2 * step].rearrange("p (a c) -> p a c", a=2)[:, :, 0:outer]
-        dst = pair_tiles[0][:].rearrange("p u c e -> p (u c) e")[:, 0 : 2 * step, :]
-        dst = dst.rearrange("p (a c) e -> p a c e", a=2)[:, :, 0:outer, :]
-        nc.gpsimd.tensor_copy(out=dst, in_=src.unsqueeze(3).to_broadcast([P, 2, outer, 2]))
-        src = windows[1][:, outer:step]
-        nc.scalar.copy(out=pair_tiles[0][:, 0, outer:step, :], in_=src.unsqueeze(2).to_broadcast([P, SCALAR_MIDDLE, 2]))
+        src = windows[1][:, 0 : PAIR_WIDTHS[0]]
+        nc.gpsimd.tensor_copy(out=pair_tiles[0][:, 0, :, :], in_=src.unsqueeze(2).to_broadcast([P, PAIR_WIDTHS[0], 2]))
         scalar_chunks = list(enumerate(CHUNKS))[VECTOR_CHUNKS:]
         for k, (first, width) in scalar_chunks:
             nc.scalar.copy(out=pairs[k][:, 0, :, 1], in_=windows[1][:, first : first + width])

@@ -23,11 +23,11 @@ SLOTS = 512
 HALF = SLOTS // 2
 T = 2048
 
-CHUNKS = ((0, 512), (512, 512), (1024, 512), (1536, 256), (1792, 256))
-VECTOR_CHUNKS = 2
-PAIR_WIDTHS = (1024, 512, 256, 256)
+VECTOR_COLUMNS = 1280
+CHUNKS = ((0, 512), (512, 512), (1024, 256), (1280, 256), (1536, 256), (1792, 256))
+CODE_STORES = (((0, 1), "y_codes0"), ((2, 3), "vector_pairs"), ((4,), "y_words0"), ((5,), "y_words1"))
 SCORE_BANKS = ((((0,), 6), ((1,), 7), ((2, 3), 0)), (((0, 1), 6), ((2, 3), 7)))
-PRODUCT_BANKS = (6, 7, 1, 0)
+PRODUCT_BANKS = ({3: 5, 2: 1, 1: 1, 0: 0}, {3: 6, 2: 7, 1: 7, 0: 3})
 
 FLOPS = 2 * 2 * D * R * SLOTS
 
@@ -170,13 +170,12 @@ def tile_attend_grbf_pl_kernel(tc, xT, cT, hx, cs, cd, dp, us, wt, offs, out_0, 
         neg_hx = sb.tile([P, LANES], F32, name="neg_hx")
         nc.gpsimd.tensor_scalar(neg_hx[:], hx_col[:], -1.0, 0.0, ALU.mult, ALU.add)
 
-        g_planes = []
-        sh_row = ps.tile([P, SLOTS], F32, name="sh_row", tag="bank4")
-        for u in range(2):
+        neg_cd2 = sb.tile([P, LANES], F32, name="neg_cd2", align_bytes=64)
+        out_planes = out_0.rearrange("(p j) c -> j p c", j=LANES)
+        probs, g_planes, sh_turned, sh_rows, g_words, g_mx, products = {}, {}, {}, {}, {}, {}, {}
+
+        def exponents(u, n2_row):
             codes, scales = c_mx[u]
-            if u == 1:
-                n2_row = n2_as_row(u)
-            probs = []
             for group, bank in SCORE_BANKS[u]:
                 a = ps.tile([P, len(group), HALF], F32, name=f"a{u}{group[0]}", tag=f"bank{bank}")
                 for e, t in enumerate(group):
@@ -190,134 +189,130 @@ def tile_attend_grbf_pl_kernel(tc, xT, cT, hx, cs, cd, dp, us, wt, offs, out_0, 
                     nc.vector.scalar_tensor_tensor(
                         expo[:], a[:, e, :], us_col[:, t : t + 1], n2_row[:], ALU.mult, ALU.subtract
                     )
-                    prob = sb.tile([P, HALF], F32, name=f"prob{u}{t}")
-                    nc.scalar.activation(prob[:], expo[:], ACT.Exp, bias=neg_hx[:, t : t + 1])
-                    probs.append(prob)
-            g_half = sb.tile([P, LANES, HALF], BF16, name=f"g_planes{u}")
-            sh_bank = ps.tile([P, 2, P], F32, name=f"sh_turned{u}", tag=f"bank{2 + u}")
-            sh_turned = [sh_bank[:, b, :] for b in range(2)]
-            for t in range(LANES):
+                    probs[u, t] = sb.tile([P, HALF], F32, name=f"prob{u}{t}")
+                    nc.scalar.activation(probs[u, t][:], expo[:], ACT.Exp, bias=neg_hx[:, t : t + 1])
+
+        def weights(u, planes):
+            if u not in g_planes:
+                g_planes[u] = sb.tile([P, LANES, HALF], BF16, name=f"g_planes{u}")
+                sh_turned[u] = ps.tile([P, 2, P], F32, name=f"sh_turned{u}", tag=f"bank{2 + u}")
+            for t in planes:
                 h = sb.tile([P, HALF], F32, name=f"h{u}{t}", align_bytes=64)
                 nc.vector.scalar_tensor_tensor(
-                    h[:], probs[t][:], wt_col[:, t : t + 1], dp_sb[:, t, halves[u]], ALU.mult, ALU.mult
+                    h[:], probs[u, t][:], wt_col[:, t : t + 1], dp_sb[:, t, halves[u]], ALU.mult, ALU.mult
                 )
-                nc.scalar.activation(g_half[:, t, :], h[:], ACT.Copy, scale=us_col[:, t : t + 1])
-                turn_and_add(sh_turned, h[:], (t == 0, False), (False, t == LAST))
-            g_planes.append(g_half)
-            sh_sums = slot_sums(f"sh{u}", sh_turned, 1.0)
-            if u == 0:
-                sh_first = ps.tile([P, HALF], F32, name="sh_first", tag="bank2")
-                spread(sh_first, sh_sums)
-            spread(sh_row[:, halves[u]], sh_sums)
+                nc.scalar.activation(g_planes[u][:, t, :], h[:], ACT.Copy, scale=us_col[:, t : t + 1])
+                turn_and_add([sh_turned[u][:, b, :] for b in range(2)], h[:], (t == 0, False), (False, t == LAST))
 
-        cd2 = sb.tile([P, LANES], F32, name="cd2", tag="c_words0", align_bytes=64)
-        nc.vector.tensor_tensor(cd2[:], cd_col[:], cd_col[:], ALU.mult)
-        cd2_plane2 = sb.tile([P, 1], F32, name="cd2_plane2", tag="square3_0", align_bytes=64)
-        nc.vector.tensor_tensor(cd2_plane2[:], cd_col[:, 2:3], cd_col[:, 2:3], ALU.mult)
-        cd2_of = {0: cd2[:, 0:1], 1: cd2[:, 1:2], 2: cd2_plane2[:]}
+        def sh_as_row(u):
+            sums = slot_sums(f"sh{u}", [sh_turned[u][:, b, :] for b in range(2)], 1.0)
+            sh_rows[u] = ps.tile([P, HALF], F32, name=f"sh_row{u}", tag=("bank2", "bank4")[u])
+            spread(sh_rows[u], sums)
 
-        g_all_codes, g_all_scales = mx_tiles("g", HALF + SLOTS)
-        nc.gpsimd.memset(g_all_codes[:, :HALF], 0)
-        nc.gpsimd.memset(g_all_scales[:, :HALF], 0)
-        g_codes, g_scales = g_all_codes[:, HALF:], g_all_scales[:, HALF:]
-        g_words = [sb.tile([P, HALF, LANES], BF16, name=f"g_words{u}", align_bytes=64) for u in range(2)]
-        for u in range(2):
+        def weave_g(u):
+            g_words[u] = sb.tile([P, HALF, LANES], BF16, name=f"g_words{u}", tag=("g_words0", "pull03")[u], align_bytes=64)
             nc.vector.tensor_copy(
                 out=g_words[u][:].rearrange("s (c i) t -> s c t i", i=4),
                 in_=g_planes[u][:].rearrange("s t (c i) -> s c t i", i=4),
             )
-        for u in range(2):
-            nc.vector.quantize_mx(
-                out=g_codes[:, halves[u]].bitcast(E5M2), scales=g_scales[:, halves[u]],
-                in_=g_words[u][:].rearrange("s i t -> s (i t)"),
-            )
 
+        def quantise_g(u):
+            g_mx[u] = mx_tiles(f"g{u}", HALF)
+            codes, scales = g_mx[u]
+            nc.vector.quantize_mx(
+                out=codes[:].bitcast(E5M2), scales=scales[:], in_=g_words[u][:].rearrange("s i t -> s (i t)")
+            )
+            banks = {}
+            for j in (3, 2, 1, 0):
+                bank = PRODUCT_BANKS[u][j]
+                tenants = [k for k in (3, 2, 1, 0) if PRODUCT_BANKS[u][k] == bank]
+                if bank not in banks:
+                    banks[bank] = ps.tile([P, len(tenants), HALF], F32, name=f"xg{u}{j}", tag=f"bank{bank}")
+                products[u, j] = banks[bank][:, tenants.index(j), :]
+                cols = slice(P * j, P * (j + 1))
+                nc.tensor.matmul_mx(
+                    out=products[u, j], lhsT=xr_codes[:, cols].bitcast(E4M3), lhsT_scale=xr_scales[:, cols],
+                    rhs=codes[:].bitcast(E5M2), rhs_scale=scales[:], start=True, stop=True,
+                )
+
+        def gradient(u, j, pull, tag=None):
+            dc = sb.tile([P, HALF], F32, name=f"dc{u}{j}", tag=tag or f"dc{u}{j}", align_bytes=64)
+            nc.vector.scalar_tensor_tensor(dc[:], pull, neg_cd2[:, j : j + 1], products[u, j], ALU.mult, ALU.add)
+            return dc
+
+        def scalar_scatter(u, j, dc):
+            nc.scalar.activation(windows[j][:].indirect(half_lists[u]), dc[:], ACT.Copy)
+
+        def vector_scatter(u, j, dc):
+            nc.vector.tensor_copy(windows[j][:].indirect(half_lists[u]), dc[:])
+
+        def store(j):
+            nc.sync.dma_start(out=out_planes[j], in_=windows[j][:])
+
+        exponents(0, n2_row)
+        weights(0, range(LANES))
         for j, freed in ((0, "expo00"), (1, "c_words1")):
             windows[j] = sb.tile([P, T], F32, name=f"window{j}", tag=freed, align_bytes=64)
             nc.gpsimd.memset(windows[j][:], 0.0)
-
-        out_planes = out_0.rearrange("(p j) c -> j p c", j=LANES)
-
-        def product(j):
-            xg_ps = ps.tile([P, SLOTS], F32, name=f"xg{j}", tag=f"bank{PRODUCT_BANKS[j]}")
-            cols = slice(P * j, P * (j + 1))
-            nc.tensor.matmul_mx(
-                out=xg_ps[:], lhsT=xr_codes[:, cols].bitcast(E4M3), lhsT_scale=xr_scales[:, cols],
-                rhs=g_codes.bitcast(E5M2), rhs_scale=g_scales, start=True, stop=True,
-            )
-            return xg_ps
-
-        def sh_factor(factor, j):
-            nc.scalar.activation(factor, sh_row[:], ACT.Copy, scale=cd2_of[j])
-
-        factors = {2: sb.tile([P, SLOTS], F32, name="factor2", align_bytes=64)}
-        early_ps = ps.tile([P, SLOTS], F32, name="xg_early", tag="bank5")
-        nc.tensor.matmul_mx(
-            out=early_ps[:], lhsT=xr_codes[:, P * LAST :].bitcast(E4M3), lhsT_scale=xr_scales[:, P * LAST :],
-            rhs=g_all_codes[:, :SLOTS].bitcast(E5M2), rhs_scale=g_all_scales[:, :SLOTS], start=True, stop=True,
-        )
-        products = {j: product(j) for j in (2, 3, 1, 0)}
-
-        xg_halves = [early_ps[:, HALF:], products[LAST][:, HALF:]]
-        for u, parts in enumerate(([slice(0, HALF)], [slice(0, P), slice(P, HALF)])):
-            pull = sb.tile([P, HALF], F32, name=f"pull_first{u}")
-            centres, sh_half = c_planes[LAST][:, halves[u]], (sh_first[:], sh_row[:, HALF:])[u]
-            for part in parts:
-                nc.vector.scalar_tensor_tensor(
-                    pull[:, part], centres[:, part], cd2[:, LAST:], sh_half[:, part], ALU.mult, ALU.mult
-                )
-            dc = sb.tile([P, HALF], F32, name=f"dc_first{u}", tag=("h13", "dc_first1")[u], align_bytes=64)
-            for part in parts:
-                nc.vector.tensor_tensor(dc[:, part], xg_halves[u][:, part], pull[:, part], ALU.subtract)
-            nc.vector.tensor_copy(windows[LAST][:].indirect(half_lists[u]), dc[:])
+        sh_as_row(0)
+        exponents(1, n2_as_row(1))
+        nc.vector.scalar_tensor_tensor(neg_cd2[:], cd_col[:], -1.0, cd_col[:], ALU.mult, ALU.mult)
+        weave_g(0)
+        weights(1, (0, 1))
+        quantise_g(0)
+        weights(1, (2, 3))
+        sh_as_row(1)
+        pulls = {0: {}, 1: {}}
+        sh_sb = []
+        for u in range(2):
+            pull = sb.tile([P, HALF], F32, name=f"pull{u}3", align_bytes=64)
+            nc.vector.tensor_tensor(pull[:], c_planes[3][:, halves[u]], sh_rows[u][:], ALU.mult)
+            row = sb.tile([P, HALF], F32, name=f"sh_sb{u}")
+            nc.scalar.copy(out=row[:], in_=sh_rows[u][:])
+            sh_sb.append(row)
+            scalar_scatter(u, 3, gradient(u, 3, pull[:]))
             if u == 0:
-                sh_factor(factors[2][:], 2)
-        nc.sync.dma_start(out=out_planes[LAST], in_=windows[LAST][:])
+                weave_g(1)
+                quantise_g(1)
+        store(3)
+        for u, j in ((0, 2), (0, 1), (1, 2), (1, 1), (0, 0), (1, 0)):
+            pull = sb.tile([P, HALF], F32, name=f"pull{u}{j}", tag="pull03" if (u, j) == (0, 2) else f"pull{u}{j}", align_bytes=64)
+            nc.gpsimd.tensor_tensor(pull[:], c_planes[j][:, halves[u]], sh_sb[u][:], ALU.mult)
+            pulls[u][j] = pull[:]
+        vector_scatter(0, 2, gradient(0, 2, pulls[0][2], tag="pull13"))
+        scalar_scatter(0, 1, gradient(0, 1, pulls[0][1]))
+        dc_12 = gradient(1, 2, pulls[1][2])
+        dc_11 = gradient(1, 1, pulls[1][1])
+        vector_scatter(1, 2, dc_12)
+        store(2)
+        scalar_scatter(1, 1, dc_11)
+        store(1)
+        dc_00 = gradient(0, 0, pulls[0][0], tag="dc12")
+        dc_10 = gradient(1, 0, pulls[1][0])
+        vector_scatter(0, 0, dc_00)
+        scalar_scatter(1, 0, dc_10)
+        store(0)
 
-        for j in (2, 1, 0):
-            if j < 2:
-                factors[j] = sb.tile([P, SLOTS], F32, name=f"factor{j}")
-                sh_factor(factors[j][:], j)
-            xg = sb.tile([P, SLOTS], F32, name=f"xg_sb{j}", tag=("xg_sb0", "factor2", "square3_0")[j], align_bytes=64)
-            nc.scalar.copy(out=xg[:], in_=products[j][:])
-            pull = sb.tile([P, SLOTS], F32, name=f"pull{j}", tag="pull")
-            dc = sb.tile([P, SLOTS], F32, name=f"dc{j}", tag="pull_first0" if j == 2 else f"dc{j}")
-            parts = halves if j == 0 else [slice(0, SLOTS)]
-            for part in parts:
-                nc.gpsimd.tensor_tensor(pull[:, part], c_planes[j][:, part], factors[j][:, part], ALU.mult)
-            for part in parts:
-                nc.gpsimd.tensor_tensor(dc[:, part], xg[:, part], pull[:, part], ALU.subtract)
-            nc.vector.tensor_copy(windows[j][:].indirect(offsets[:]), dc[:])
-            nc.sync.dma_start(out=out_planes[j], in_=windows[j][:])
-
-        pair_tiles = [
-            sb.tile([P, 2, width, 2], BF16, name=f"pairs{k}", align_bytes=64) for k, width in enumerate(PAIR_WIDTHS)
-        ]
+        vector_pairs = sb.tile([P, 2, VECTOR_COLUMNS, 2], BF16, name="vector_pairs", align_bytes=64)
+        scalar_pairs = sb.tile([P, 2, T - VECTOR_COLUMNS, 2], BF16, name="scalar_pairs", tag="dc11", align_bytes=64)
+        src = windows[3][:, :VECTOR_COLUMNS]
+        nc.gpsimd.tensor_copy(out=vector_pairs[:, 1, :, :], in_=src.unsqueeze(2).to_broadcast([P, VECTOR_COLUMNS, 2]))
+        for j in (1, 2, 0):
+            nc.vector.tensor_copy(out=vector_pairs[:, j // 2, :, j % 2], in_=windows[j][:, :VECTOR_COLUMNS])
+        for j in (3, 2, 1):
+            nc.scalar.copy(out=scalar_pairs[:, j // 2, :, j % 2], in_=windows[j][:, VECTOR_COLUMNS:])
         pairs = []
-        for k, (first, width) in enumerate(CHUNKS):
-            if k < VECTOR_CHUNKS:
-                pairs.append(pair_tiles[0][:, :, first : first + width, :])
+        for first, width in CHUNKS:
+            if first < VECTOR_COLUMNS:
+                pairs.append(vector_pairs[:, :, first : first + width, :])
             else:
-                pairs.append(pair_tiles[k - VECTOR_CHUNKS + 1][:])
-        for j in (3, 2):
-            first = 0
-            for tile, width in zip(pair_tiles, PAIR_WIDTHS):
-                nc.scalar.copy(out=tile[:, 1, :, j % 2], in_=windows[j][:, first : first + width])
-                first += width
-        src = windows[1][:, 0 : PAIR_WIDTHS[0]]
-        nc.gpsimd.tensor_copy(out=pair_tiles[0][:, 0, :, :], in_=src.unsqueeze(2).to_broadcast([P, PAIR_WIDTHS[0], 2]))
-        scalar_chunks = list(enumerate(CHUNKS))[VECTOR_CHUNKS:]
-        for k, (first, width) in scalar_chunks:
-            nc.scalar.copy(out=pairs[k][:, 0, :, 1], in_=windows[1][:, first : first + width])
-        for k, (first, width) in enumerate(CHUNKS[:VECTOR_CHUNKS]):
-            nc.vector.tensor_copy(out=pairs[k][:, 0, :, 0], in_=windows[0][:, first : first + width])
-        for k, (first, width) in scalar_chunks:
-            nc.scalar.copy(out=pairs[k][:, 0, :, 0], in_=windows[0][:, first : first + width])
+                pairs.append(scalar_pairs[:, :, first - VECTOR_COLUMNS : first - VECTOR_COLUMNS + width, :])
+                nc.scalar.copy(out=pairs[-1][:, 0, :, 0], in_=windows[0][:, first : first + width])
 
         y_words = []
         for k, (first, width) in enumerate(CHUNKS):
             words = sb.tile([P, width, LANES], BF16, name=f"y_words{k}", align_bytes=64)
-            raw, engine_copy = (I32, nc.vector.tensor_copy) if k < VECTOR_CHUNKS else (U32, nc.scalar.copy)
+            raw, engine_copy = (I32, nc.vector.tensor_copy) if first < VECTOR_COLUMNS else (U32, nc.scalar.copy)
             engine_copy(
                 out=words[:].rearrange("p c t -> p (c t)").bitcast(raw).rearrange("p (c u) -> p c u", u=2),
                 in_=pairs[k].bitcast(raw).rearrange("p u c o -> p (c o) u"),
@@ -326,15 +321,19 @@ def tile_attend_grbf_pl_kernel(tc, xT, cT, hx, cs, cd, dp, us, wt, offs, out_0, 
 
         y_scales = sb.tile([P, T // 2], U8, name="y_scales", align_bytes=64)
         words_out = out_1[0].rearrange("p c l -> p (c l)").bitcast(I32)
-        code_buffers = ("y_codes0", "y_codes1", "pairs0", "y_words0", "y_words1")
-        for k, (first, width) in enumerate(CHUNKS):
-            y_codes = sb.tile([P, width], U32, name=f"y_codes{k}", tag=code_buffers[k], align_bytes=64)
-            upper, place = divmod(first, T // 2)
-            nc.vector.quantize_mx(
-                out=y_codes[:].bitcast(E4M3), scales=y_scales[4 * upper :, place : place + width],
-                in_=y_words[k][:].rearrange("p c t -> p (c t)"),
-            )
-            nc.sync.dma_start(out=words_out[:, first : first + width], in_=y_codes[:].bitcast(I32))
+        for group, freed in CODE_STORES:
+            start = CHUNKS[group[0]][0]
+            span = sum(CHUNKS[k][1] for k in group)
+            y_codes = sb.tile([P, span], U32, name=f"y_codes{group[0]}", tag=freed, align_bytes=64)
+            for k in group:
+                first, width = CHUNKS[k]
+                upper, place = divmod(first, T // 2)
+                nc.vector.quantize_mx(
+                    out=y_codes[:, first - start : first - start + width].bitcast(E4M3),
+                    scales=y_scales[4 * upper :, place : place + width],
+                    in_=y_words[k][:].rearrange("p c t -> p (c t)"),
+                )
+            nc.sync.dma_start(out=words_out[:, start : start + span], in_=y_codes[:].bitcast(I32))
         scales_out = out_2[0].bitcast(I32).rearrange("f (upper c) -> upper f c", upper=2)
         for q in range(4):
             queue = nc.scalar if q < 2 else nc.sync

@@ -25,7 +25,8 @@ T = 2048
 
 VECTOR_COLUMNS = 1280
 CHUNKS = ((0, 512), (512, 512), (1024, 256), (1280, 256), (1536, 256), (1792, 256))
-CODE_STORES = (((0, 1), "y_codes0"), ((2, 3), "vector_pairs"), ((4,), "y_words0"), ((5,), "y_words1"))
+PIECES = ((0, 512), (512, 768), (1280, 768))
+CODE_STORES = (((0, 1), "y_codes0"), ((2, 3), "y_words0"), ((4,), "y_words1"), ((5,), "y_words2"))
 SCORE_BANKS = ((((0,), 6), ((1,), 7), ((2, 3), 0)), (((0, 1), 6), ((2, 3), 7)))
 PRODUCT_BANKS = ({3: 5, 2: 1, 1: 1, 0: 0}, {3: 6, 2: 7, 1: 7, 0: 3})
 
@@ -235,16 +236,16 @@ def tile_attend_grbf_pl_kernel(tc, xT, cT, hx, cs, cd, dp, us, wt, offs, out_0, 
                     rhs=codes[:].bitcast(E5M2), rhs_scale=scales[:], start=True, stop=True,
                 )
 
-        def gradient(u, j, pull, tag=None):
-            dc = sb.tile([P, HALF], F32, name=f"dc{u}{j}", tag=tag or f"dc{u}{j}", align_bytes=64)
-            nc.vector.scalar_tensor_tensor(dc[:], pull, neg_cd2[:, j : j + 1], products[u, j], ALU.mult, ALU.add)
+        def gradient(u, j, pull, tag=None, place=None):
+            dc = place if place is not None else sb.tile([P, HALF], F32, name=f"dc{u}{j}", tag=tag or f"dc{u}{j}", align_bytes=64)[:]
+            nc.vector.scalar_tensor_tensor(dc, pull, neg_cd2[:, j : j + 1], products[u, j], ALU.mult, ALU.add)
             return dc
 
         def scalar_scatter(u, j, dc):
-            nc.scalar.activation(windows[j][:].indirect(half_lists[u]), dc[:], ACT.Copy)
+            nc.scalar.activation(windows[j][:].indirect(half_lists[u]), dc, ACT.Copy)
 
         def vector_scatter(u, j, dc):
-            nc.vector.tensor_copy(windows[j][:].indirect(half_lists[u]), dc[:])
+            nc.vector.tensor_copy(windows[j][:].indirect(half_lists[u]), dc)
 
         def store(j):
             nc.sync.dma_start(out=out_planes[j], in_=windows[j][:])
@@ -275,47 +276,40 @@ def tile_attend_grbf_pl_kernel(tc, xT, cT, hx, cs, cd, dp, us, wt, offs, out_0, 
                 weave_g(1)
                 quantise_g(1)
         store(3)
-        for u, j in ((0, 2), (0, 1), (1, 2), (1, 1), (0, 0), (1, 0)):
-            pull = sb.tile([P, HALF], F32, name=f"pull{u}{j}", tag="pull03" if (u, j) == (0, 2) else f"pull{u}{j}", align_bytes=64)
-            nc.gpsimd.tensor_tensor(pull[:], c_planes[j][:, halves[u]], sh_sb[u][:], ALU.mult)
-            pulls[u][j] = pull[:]
-        vector_scatter(0, 2, gradient(0, 2, pulls[0][2], tag="pull13"))
-        scalar_scatter(0, 1, gradient(0, 1, pulls[0][1]))
+        late_pulls = sb.tile([P, 6 * HALF], F32, name="late_pulls", tag="pull03", align_bytes=64)
+        for n, (u, j) in enumerate(((0, 2), (0, 1), (1, 2), (0, 0), (1, 1), (1, 0))):
+            pulls[u][j] = late_pulls[:, HALF * n : HALF * (n + 1)]
+            nc.gpsimd.tensor_tensor(pulls[u][j], c_planes[j][:, halves[u]], sh_sb[u][:], ALU.mult)
+        rounded = []
+        for k, (first, width) in enumerate(PIECES):
+            flat = sb.tile([P, LANES * width], BF16, name=f"rounded{k}", align_bytes=64)
+            rounded.append(flat[:].rearrange("p (t c) -> p t c", t=LANES))
+        dc_02 = gradient(0, 2, pulls[0][2], tag="pull13")
         dc_12 = gradient(1, 2, pulls[1][2])
-        dc_11 = gradient(1, 1, pulls[1][1])
-        vector_scatter(1, 2, dc_12)
+        vector_scatter(0, 2, dc_02)
+        scalar_scatter(1, 2, dc_12)
         store(2)
-        scalar_scatter(1, 1, dc_11)
-        store(1)
-        dc_00 = gradient(0, 0, pulls[0][0], tag="dc12")
-        dc_10 = gradient(1, 0, pulls[1][0])
-        vector_scatter(0, 0, dc_00)
-        scalar_scatter(1, 0, dc_10)
+        scalar_scatter(0, 1, gradient(0, 1, pulls[0][1]))
+        vector_scatter(0, 0, gradient(0, 0, pulls[0][0]))
+        scalar_scatter(1, 1, gradient(1, 1, pulls[1][1], place=rounded[2][:, 2, : 2 * HALF].bitcast(F32)))
+        vector_scatter(1, 0, gradient(1, 0, pulls[1][0], place=rounded[1][:, 2, : 2 * HALF].bitcast(F32)))
         store(0)
+        store(1)
 
-        vector_pairs = sb.tile([P, 2, VECTOR_COLUMNS, 2], BF16, name="vector_pairs", align_bytes=64)
-        scalar_pairs = sb.tile([P, 2, T - VECTOR_COLUMNS, 2], BF16, name="scalar_pairs", tag="dc11", align_bytes=64)
-        src = windows[3][:, :VECTOR_COLUMNS]
-        nc.gpsimd.tensor_copy(out=vector_pairs[:, 1, :, :], in_=src.unsqueeze(2).to_broadcast([P, VECTOR_COLUMNS, 2]))
-        for j in (1, 2, 0):
-            nc.vector.tensor_copy(out=vector_pairs[:, j // 2, :, j % 2], in_=windows[j][:, :VECTOR_COLUMNS])
-        for j in (3, 2, 1):
-            nc.scalar.copy(out=scalar_pairs[:, j // 2, :, j % 2], in_=windows[j][:, VECTOR_COLUMNS:])
-        pairs = []
-        for first, width in CHUNKS:
-            if first < VECTOR_COLUMNS:
-                pairs.append(vector_pairs[:, :, first : first + width, :])
-            else:
-                pairs.append(scalar_pairs[:, :, first - VECTOR_COLUMNS : first - VECTOR_COLUMNS + width, :])
-                nc.scalar.copy(out=pairs[-1][:, 0, :, 0], in_=windows[0][:, first : first + width])
-
+        rounders = {3: "ggg", 2: "gvv", 0: "vvs", 1: "vss"}
+        copies = {"g": nc.gpsimd.tensor_copy, "v": nc.vector.tensor_copy, "s": nc.scalar.copy}
+        for j in (3, 2, 0, 1):
+            for k, (first, width) in enumerate(PIECES):
+                copies[rounders[j][k]](out=rounded[k][:, j, :], in_=windows[j][:, first : first + width])
         y_words = []
         for k, (first, width) in enumerate(CHUNKS):
             words = sb.tile([P, width, LANES], BF16, name=f"y_words{k}", align_bytes=64)
-            raw, engine_copy = (I32, nc.vector.tensor_copy) if first < VECTOR_COLUMNS else (U32, nc.scalar.copy)
+            engine_copy = nc.vector.tensor_copy if first < VECTOR_COLUMNS else nc.scalar.copy
+            piece = max(n for n, (start, span) in enumerate(PIECES) if start <= first)
+            place = first - PIECES[piece][0]
             engine_copy(
-                out=words[:].rearrange("p c t -> p (c t)").bitcast(raw).rearrange("p (c u) -> p c u", u=2),
-                in_=pairs[k].bitcast(raw).rearrange("p u c o -> p (c o) u"),
+                out=words[:].rearrange("p (c i) t -> p c t i", i=4),
+                in_=rounded[piece][:, :, place : place + width].rearrange("p t (c i) -> p c t i", i=4),
             )
             y_words.append(words)
 

@@ -23,10 +23,11 @@ SLOTS = 512
 HALF = SLOTS // 2
 T = 2048
 
-VECTOR_COLUMNS = 1280
-CHUNKS = ((0, 512), (512, 512), (1024, 256), (1280, 256), (1536, 256), (1792, 256))
-PIECES = ((0, 512), (512, 768), (1280, 768))
-CODE_STORES = (((0, 1), "y_codes0"), ((2, 3), "y_words0"), ((4,), "y_words1"), ((5,), "y_words2"))
+VECTOR_COLUMNS = 1152
+PIECES = ((0, 512), (512, 640))
+TURN_BANKS = (2, 4, 5, 6, 1, 0, 7)
+CHUNKS = ((0, 512), (512, 512), (1024, 128), (1152, 256), (1408, 256), (1664, 256), (1920, 128))
+CODE_STORES = (((0,), "y_codes0"), ((1, 2), "y_codes1"), ((3, 4), "y_words0"), ((5, 6), "y_words512"))
 SCORE_BANKS = ((((0,), 6), ((1,), 7), ((2, 3), 0)), (((0, 1), 6), ((2, 3), 7)))
 PRODUCT_BANKS = ({3: 5, 2: 1, 1: 1, 0: 0}, {3: 6, 2: 7, 1: 7, 0: 3})
 
@@ -236,9 +237,9 @@ def tile_attend_grbf_pl_kernel(tc, xT, cT, hx, cs, cd, dp, us, wt, offs, out_0, 
                     rhs=codes[:].bitcast(E5M2), rhs_scale=scales[:], start=True, stop=True,
                 )
 
-        def gradient(u, j, pull, tag=None, place=None):
-            dc = place if place is not None else sb.tile([P, HALF], F32, name=f"dc{u}{j}", tag=tag or f"dc{u}{j}", align_bytes=64)[:]
-            nc.vector.scalar_tensor_tensor(dc, pull, neg_cd2[:, j : j + 1], products[u, j], ALU.mult, ALU.add)
+        def gradient(u, j, place=None):
+            dc = place if place is not None else sb.tile([P, HALF], F32, name=f"dc{u}{j}", align_bytes=64)[:]
+            nc.vector.scalar_tensor_tensor(dc, pulls[u, j], neg_cd2[:, j : j + 1], products[u, j], ALU.mult, ALU.add)
             return dc
 
         def scalar_scatter(u, j, dc):
@@ -263,55 +264,95 @@ def tile_attend_grbf_pl_kernel(tc, xT, cT, hx, cs, cd, dp, us, wt, offs, out_0, 
         quantise_g(0)
         weights(1, (2, 3))
         sh_as_row(1)
-        pulls = {0: {}, 1: {}}
-        sh_sb = []
-        for u in range(2):
-            pull = sb.tile([P, HALF], F32, name=f"pull{u}3", align_bytes=64)
-            nc.vector.tensor_tensor(pull[:], c_planes[3][:, halves[u]], sh_rows[u][:], ALU.mult)
-            row = sb.tile([P, HALF], F32, name=f"sh_sb{u}")
+        pulls = {}
+
+        def vector_pull(u, j):
+            pulls[u, j] = sb.tile([P, HALF], F32, name=f"pull{u}{j}", align_bytes=64)[:]
+            nc.vector.tensor_tensor(pulls[u, j], c_planes[j][:, halves[u]], sh_rows[u][:], ALU.mult)
+
+        def sh_to_sbuf(u, tag):
+            row = sb.tile([P, HALF], F32, name=f"sh_sb{u}", tag=tag, align_bytes=64)
             nc.scalar.copy(out=row[:], in_=sh_rows[u][:])
-            sh_sb.append(row)
-            scalar_scatter(u, 3, gradient(u, 3, pull[:]))
-            if u == 0:
-                weave_g(1)
-                quantise_g(1)
+            return row
+
+        vector_pull(0, 3)
+        sh_sb = [sh_to_sbuf(0, "sh_sb0")]
+        scalar_scatter(0, 3, gradient(0, 3))
+        weave_g(1)
+        quantise_g(1)
+        vector_pull(1, 3)
+        vector_pull(1, 2)
+        scalar_scatter(1, 3, gradient(1, 3))
         store(3)
-        late_pulls = sb.tile([P, 6 * HALF], F32, name="late_pulls", tag="pull03", align_bytes=64)
-        for n, (u, j) in enumerate(((0, 2), (0, 1), (1, 2), (0, 0), (1, 1), (1, 0))):
-            pulls[u][j] = late_pulls[:, HALF * n : HALF * (n + 1)]
-            nc.gpsimd.tensor_tensor(pulls[u][j], c_planes[j][:, halves[u]], sh_sb[u][:], ALU.mult)
-        rounded = []
-        for k, (first, width) in enumerate(PIECES):
-            flat = sb.tile([P, LANES * width], BF16, name=f"rounded{k}", align_bytes=64)
-            rounded.append(flat[:].rearrange("p (t c) -> p t c", t=LANES))
-        dc_02 = gradient(0, 2, pulls[0][2], tag="pull13")
-        dc_12 = gradient(1, 2, pulls[1][2])
+        sh_sb.append(sh_to_sbuf(1, "dc13"))
+        late_pulls = sb.tile([P, 5 * HALF], F32, name="late_pulls", tag="pull03", align_bytes=64)
+        for n, (u, j) in enumerate(((0, 2), (0, 1), (0, 0), (1, 1), (1, 0))):
+            pulls[u, j] = late_pulls[:, HALF * n : HALF * (n + 1)]
+            nc.gpsimd.tensor_tensor(pulls[u, j], c_planes[j][:, halves[u]], sh_sb[u][:], ALU.mult)
+        dc_12 = gradient(1, 2)
+        dc_02 = gradient(0, 2, place=pulls[1, 3])
+        scalar_scatter(0, 1, gradient(0, 1, place=pulls[1, 2]))
         vector_scatter(0, 2, dc_02)
         scalar_scatter(1, 2, dc_12)
         store(2)
-        scalar_scatter(0, 1, gradient(0, 1, pulls[0][1]))
-        vector_scatter(0, 0, gradient(0, 0, pulls[0][0]))
-        scalar_scatter(1, 1, gradient(1, 1, pulls[1][1], place=rounded[2][:, 2, : 2 * HALF].bitcast(F32)))
-        vector_scatter(1, 0, gradient(1, 0, pulls[1][0], place=rounded[1][:, 2, : 2 * HALF].bitcast(F32)))
+        dc_00 = gradient(0, 0, place=pulls[0, 2])
+        dc_11 = gradient(1, 1)
+        vector_scatter(0, 0, dc_00)
+        scalar_scatter(1, 1, dc_11)
+        vector_scatter(1, 0, gradient(1, 0))
         store(0)
         store(1)
 
-        rounders = {3: "ggg", 2: "gvv", 0: "vvs", 1: "vss"}
-        copies = {"g": nc.gpsimd.tensor_copy, "v": nc.vector.tensor_copy, "s": nc.scalar.copy}
+        y_words = {}
+        rounded = [
+            sb.tile([P, LANES, width], BF16, name=f"rounded{k}", align_bytes=64) for k, (first, width) in enumerate(PIECES)
+        ]
         for j in (3, 2, 0, 1):
+            engine_copy = nc.gpsimd.tensor_copy if j >= 2 else nc.vector.tensor_copy
             for k, (first, width) in enumerate(PIECES):
-                copies[rounders[j][k]](out=rounded[k][:, j, :], in_=windows[j][:, first : first + width])
-        y_words = []
-        for k, (first, width) in enumerate(CHUNKS):
-            words = sb.tile([P, width, LANES], BF16, name=f"y_words{k}", align_bytes=64)
-            engine_copy = nc.vector.tensor_copy if first < VECTOR_COLUMNS else nc.scalar.copy
-            piece = max(n for n, (start, span) in enumerate(PIECES) if start <= first)
-            place = first - PIECES[piece][0]
-            engine_copy(
-                out=words[:].rearrange("p (c i) t -> p c t i", i=4),
-                in_=rounded[piece][:, :, place : place + width].rearrange("p t (c i) -> p c t i", i=4),
+                engine_copy(out=rounded[k][:, j, :], in_=windows[j][:, first : first + width])
+        for k, (first, width) in enumerate(PIECES):
+            y_words[first] = sb.tile([P, width, LANES], BF16, name=f"y_words{first}", align_bytes=64)
+            nc.vector.tensor_copy(
+                out=y_words[first][:].rearrange("p (c i) t -> p c t i", i=4),
+                in_=rounded[k][:].rearrange("p t (c i) -> p c t i", i=4),
             )
-            y_words.append(words)
+
+        starts = range(VECTOR_COLUMNS, T, P)
+        turned = [ps.tile([P, LANES, P], F32, name=f"y_turned{c}", tag=f"bank{b}") for c, b in zip(starts, TURN_BANKS)]
+        for planes in ((3,), (2,), (1, 0)):
+            for c, bank in zip(starts, turned):
+                for j in planes:
+                    nc.tensor.transpose(bank[:, j, :], windows[j][:, c : c + P], ident[:])
+        rows = []
+
+        def round_block(n):
+            row = sb.tile([P, 2, P, 2], BF16, name=f"y_rows{n}", align_bytes=64)
+            nc.scalar.copy(out=row[:], in_=turned[n][:].rearrange("c (u e) p -> c u p e", u=2))
+            rows.append(row[:].rearrange("c u p e -> c (u p e)").bitcast(F32))
+
+        def turn_back(group):
+            width = P * len(group)
+            back = ps.tile([P, 2, width], F32, name=f"y_back{group[0]}", tag=f"bank{TURN_BANKS[group[0]]}")
+            for e, n in enumerate(group):
+                for u in range(2):
+                    nc.tensor.transpose(back[:, u, P * e : P * (e + 1)], rows[n][:, P * u : P * (u + 1)], ident[:])
+            first = starts[group[0]]
+            y_words[first] = sb.tile([P, width, LANES], BF16, name=f"y_words{first}", align_bytes=64)
+            nc.scalar.copy(
+                out=y_words[first][:].rearrange("p c t -> p (c t)").bitcast(F32).rearrange("p (c u) -> p c u", u=2),
+                in_=back[:].rearrange("p u c -> p c u"),
+            )
+
+        groups = [tuple(range(n, min(n + 2, len(starts)))) for n in range(0, len(starts), 2)]
+        for n in groups[0]:
+            round_block(n)
+        for group, following in zip(groups, groups[1:] + [()]):
+            for n in following[:1]:
+                round_block(n)
+            turn_back(group)
+            for n in following[1:]:
+                round_block(n)
 
         y_scales = sb.tile([P, T // 2], U8, name="y_scales", align_bytes=64)
         words_out = out_1[0].rearrange("p c l -> p (c l)").bitcast(I32)
@@ -322,10 +363,11 @@ def tile_attend_grbf_pl_kernel(tc, xT, cT, hx, cs, cd, dp, us, wt, offs, out_0, 
             for k in group:
                 first, width = CHUNKS[k]
                 upper, place = divmod(first, T // 2)
+                home = max(c for c in y_words if c <= first)
                 nc.vector.quantize_mx(
                     out=y_codes[:, first - start : first - start + width].bitcast(E4M3),
                     scales=y_scales[4 * upper :, place : place + width],
-                    in_=y_words[k][:].rearrange("p c t -> p (c t)"),
+                    in_=y_words[home][:, first - home : first - home + width, :].rearrange("p c t -> p (c t)"),
                 )
             nc.sync.dma_start(out=words_out[:, start : start + span], in_=y_codes[:].bitcast(I32))
         scales_out = out_2[0].bitcast(I32).rearrange("f (upper c) -> upper f c", upper=2)

@@ -25,11 +25,11 @@ T = 2048
 
 VECTOR_COLUMNS = 1152
 PIECES = ((0, 512), (512, 640))
-TURN_BANKS = (2, 4, 5, 6, 1, 0, 7)
+TURN_BANKS = (2, 5, 6, 7, 1, 4, 3)
 CHUNKS = ((0, 512), (512, 512), (1024, 128), (1152, 256), (1408, 256), (1664, 256), (1920, 128))
 CODE_STORES = (((0,), "y_codes0"), ((1, 2), "y_codes1"), ((3, 4), "y_words0"), ((5, 6), "y_words512"))
 SCORE_BANKS = ((((0,), 6), ((1,), 7), ((2, 3), 0)), (((0, 1), 6), ((2, 3), 7)))
-PRODUCT_BANKS = ({3: 5, 2: 1, 1: 1, 0: 0}, {3: 6, 2: 7, 1: 7, 0: 3})
+PRODUCT_BANKS = ({3: 5, 2: 1, 1: 3, 0: 3}, {3: 6, 2: 7, 1: 0, 0: 0})
 
 FLOPS = 2 * 2 * D * R * SLOTS
 
@@ -135,6 +135,9 @@ def tile_attend_grbf_pl_kernel(tc, xT, cT, hx, cs, cd, dp, us, wt, offs, out_0, 
             nc.scalar.activation(square[:], c_planes[j], ACT.Square, scale=cs_col[:, j : j + 1])
             for u in range(2):
                 turn_and_add(n2_turned[u], square[:, halves[u]], (j == 0, j == 0), (False, False))
+            if j == 0:
+                windows[0] = sb.tile([P, T], F32, name="window0", tag="table0")
+                nc.gpsimd.memset(windows[0][:], 0.0)
             if j == 1:
                 for u in range(2):
                     nc.scalar.copy(
@@ -224,13 +227,17 @@ def tile_attend_grbf_pl_kernel(tc, xT, cT, hx, cs, cd, dp, us, wt, offs, out_0, 
             nc.vector.quantize_mx(
                 out=codes[:].bitcast(E5M2), scales=scales[:], in_=g_words[u][:].rearrange("s i t -> s (i t)")
             )
-            banks = {}
-            for j in (3, 2, 1, 0):
+
+        banks = {}
+
+        def multiply(u, planes):
+            codes, scales = g_mx[u]
+            for j in planes:
                 bank = PRODUCT_BANKS[u][j]
                 tenants = [k for k in (3, 2, 1, 0) if PRODUCT_BANKS[u][k] == bank]
-                if bank not in banks:
-                    banks[bank] = ps.tile([P, len(tenants), HALF], F32, name=f"xg{u}{j}", tag=f"bank{bank}")
-                products[u, j] = banks[bank][:, tenants.index(j), :]
+                if (u, bank) not in banks:
+                    banks[u, bank] = ps.tile([P, len(tenants), HALF], F32, name=f"xg{u}{j}", tag=f"bank{bank}")
+                products[u, j] = banks[u, bank][:, tenants.index(j), :]
                 cols = slice(P * j, P * (j + 1))
                 nc.tensor.matmul_mx(
                     out=products[u, j], lhsT=xr_codes[:, cols].bitcast(E4M3), lhsT_scale=xr_scales[:, cols],
@@ -253,7 +260,7 @@ def tile_attend_grbf_pl_kernel(tc, xT, cT, hx, cs, cd, dp, us, wt, offs, out_0, 
 
         exponents(0, n2_row)
         weights(0, range(LANES))
-        for j, freed in ((0, "expo00"), (1, "c_words1")):
+        for j, freed in ((1, "c_words1"),):
             windows[j] = sb.tile([P, T], F32, name=f"window{j}", tag=freed, align_bytes=64)
             nc.gpsimd.memset(windows[j][:], 0.0)
         sh_as_row(0)
@@ -262,6 +269,7 @@ def tile_attend_grbf_pl_kernel(tc, xT, cT, hx, cs, cd, dp, us, wt, offs, out_0, 
         weave_g(0)
         weights(1, (0, 1))
         quantise_g(0)
+        multiply(0, (3, 2))
         weights(1, (2, 3))
         sh_as_row(1)
         pulls = {}
@@ -280,6 +288,9 @@ def tile_attend_grbf_pl_kernel(tc, xT, cT, hx, cs, cd, dp, us, wt, offs, out_0, 
         scalar_scatter(0, 3, gradient(0, 3))
         weave_g(1)
         quantise_g(1)
+        multiply(1, (3, 2))
+        multiply(0, (1, 0))
+        multiply(1, (1, 0))
         vector_pull(1, 3)
         vector_pull(1, 2)
         scalar_scatter(1, 3, gradient(1, 3))
@@ -320,13 +331,14 @@ def tile_attend_grbf_pl_kernel(tc, xT, cT, hx, cs, cd, dp, us, wt, offs, out_0, 
 
         starts = range(VECTOR_COLUMNS, T, P)
         turned = [ps.tile([P, LANES, P], F32, name=f"y_turned{c}", tag=f"bank{b}") for c, b in zip(starts, TURN_BANKS)]
-        for planes in ((3,), (2,), (1, 0)):
+        for j in (3, 2):
             for c, bank in zip(starts, turned):
-                for j in planes:
-                    nc.tensor.transpose(bank[:, j, :], windows[j][:, c : c + P], ident[:])
+                nc.tensor.transpose(bank[:, j, :], windows[j][:, c : c + P], ident[:])
         rows = []
 
         def round_block(n):
+            for j in (1, 0):
+                nc.tensor.transpose(turned[n][:, j, :], windows[j][:, starts[n] : starts[n] + P], ident[:])
             row = sb.tile([P, 2, P, 2], BF16, name=f"y_rows{n}", align_bytes=64)
             nc.scalar.copy(out=row[:], in_=turned[n][:].rearrange("c (u e) p -> c u p e", u=2))
             rows.append(row[:].rearrange("c u p e -> c (u p e)").bitcast(F32))

@@ -135,9 +135,6 @@ def tile_attend_grbf_pl_kernel(tc, xT, cT, hx, cs, cd, dp, us, wt, offs, out_0, 
             nc.scalar.activation(square[:], c_planes[j], ACT.Square, scale=cs_col[:, j : j + 1])
             for u in range(2):
                 turn_and_add(n2_turned[u], square[:, halves[u]], (j == 0, j == 0), (False, False))
-            if j == 0:
-                windows[0] = sb.tile([P, T], F32, name="window0", tag="table0")
-                nc.gpsimd.memset(windows[0][:], 0.0)
             if j == 1:
                 for u in range(2):
                     nc.scalar.copy(
@@ -260,7 +257,7 @@ def tile_attend_grbf_pl_kernel(tc, xT, cT, hx, cs, cd, dp, us, wt, offs, out_0, 
 
         exponents(0, n2_row)
         weights(0, range(LANES))
-        for j, freed in ((1, "c_words1"),):
+        for j, freed in ((0, "expo00"), (1, "c_words1")):
             windows[j] = sb.tile([P, T], F32, name=f"window{j}", tag=freed, align_bytes=64)
             nc.gpsimd.memset(windows[j][:], 0.0)
         sh_as_row(0)

@@ -23,13 +23,13 @@ SLOTS = 512
 HALF = SLOTS // 2
 T = 2048
 
-VECTOR_COLUMNS = 1152
-PIECES = ((0, 512), (512, 640))
-TURN_BANKS = (2, 5, 6, 7, 1, 4, 3)
-CHUNKS = ((0, 512), (512, 512), (1024, 128), (1152, 256), (1408, 256), (1664, 256), (1920, 128))
+VECTOR_COLUMNS = 1280
+PIECES = ((0, 512), (512, 768))
+TURN_BANKS = (2, 5, 6, 7, 1, 4)
+CHUNKS = ((0, 512), (512, 512), (1024, 256), (1280, 256), (1536, 256), (1792, 128), (1920, 128))
 CODE_STORES = (((0,), "y_codes0"), ((1, 2), "y_codes1"), ((3, 4), "y_words0"), ((5, 6), "y_words512"))
 SCORE_BANKS = ((((0,), 6), ((1,), 7), ((2, 3), 0)), (((0, 1), 6), ((2, 3), 7)))
-PRODUCT_BANKS = ({3: 5, 2: 1, 1: 3, 0: 3}, {3: 6, 2: 7, 1: 0, 0: 0})
+PRODUCT_BANKS = ({3: 5, 0: 1, 1: 0, 2: 0}, {3: 6, 0: 7, 1: 3, 2: 3})
 
 FLOPS = 2 * 2 * D * R * SLOTS
 
@@ -266,7 +266,7 @@ def tile_attend_grbf_pl_kernel(tc, xT, cT, hx, cs, cd, dp, us, wt, offs, out_0, 
         weave_g(0)
         weights(1, (0, 1))
         quantise_g(0)
-        multiply(0, (3, 2))
+        multiply(0, (3, 0, 1, 2))
         weights(1, (2, 3))
         sh_as_row(1)
         pulls = {}
@@ -285,38 +285,35 @@ def tile_attend_grbf_pl_kernel(tc, xT, cT, hx, cs, cd, dp, us, wt, offs, out_0, 
         scalar_scatter(0, 3, gradient(0, 3))
         weave_g(1)
         quantise_g(1)
-        multiply(1, (3, 2))
-        multiply(0, (1, 0))
-        multiply(1, (1, 0))
+        multiply(1, (3, 0, 2, 1))
         vector_pull(1, 3)
-        vector_pull(1, 2)
+        vector_pull(1, 0)
         scalar_scatter(1, 3, gradient(1, 3))
         store(3)
         sh_sb.append(sh_to_sbuf(1, "dc13"))
         late_pulls = sb.tile([P, 5 * HALF], F32, name="late_pulls", tag="pull03", align_bytes=64)
-        for n, (u, j) in enumerate(((0, 2), (0, 1), (0, 0), (1, 1), (1, 0))):
+        for n, (u, j) in enumerate(((0, 0), (0, 1), (0, 2), (1, 2), (1, 1))):
             pulls[u, j] = late_pulls[:, HALF * n : HALF * (n + 1)]
             nc.gpsimd.tensor_tensor(pulls[u, j], c_planes[j][:, halves[u]], sh_sb[u][:], ALU.mult)
-        dc_12 = gradient(1, 2)
-        dc_02 = gradient(0, 2, place=pulls[1, 3])
-        scalar_scatter(0, 1, gradient(0, 1, place=pulls[1, 2]))
-        vector_scatter(0, 2, dc_02)
-        scalar_scatter(1, 2, dc_12)
-        store(2)
-        dc_00 = gradient(0, 0, place=pulls[0, 2])
-        dc_11 = gradient(1, 1)
+        dc_10 = gradient(1, 0)
+        dc_00 = gradient(0, 0, place=pulls[1, 3])
+        scalar_scatter(0, 1, gradient(0, 1, place=pulls[1, 0]))
         vector_scatter(0, 0, dc_00)
-        scalar_scatter(1, 1, dc_11)
-        vector_scatter(1, 0, gradient(1, 0))
+        scalar_scatter(0, 2, gradient(0, 2, place=pulls[0, 0]))
+        vector_scatter(1, 0, dc_10)
         store(0)
+        dc_11 = gradient(1, 1)
+        scalar_scatter(1, 2, gradient(1, 2))
+        vector_scatter(1, 1, dc_11)
         store(1)
+        store(2)
 
         y_words = {}
         rounded = [
             sb.tile([P, LANES, width], BF16, name=f"rounded{k}", align_bytes=64) for k, (first, width) in enumerate(PIECES)
         ]
-        for j in (3, 2, 0, 1):
-            engine_copy = nc.gpsimd.tensor_copy if j >= 2 else nc.vector.tensor_copy
+        for j in (3, 0, 1, 2):
+            engine_copy = nc.gpsimd.tensor_copy if j in (3, 0) else nc.vector.tensor_copy
             for k, (first, width) in enumerate(PIECES):
                 engine_copy(out=rounded[k][:, j, :], in_=windows[j][:, first : first + width])
         for k, (first, width) in enumerate(PIECES):
@@ -328,14 +325,13 @@ def tile_attend_grbf_pl_kernel(tc, xT, cT, hx, cs, cd, dp, us, wt, offs, out_0, 
 
         starts = range(VECTOR_COLUMNS, T, P)
         turned = [ps.tile([P, LANES, P], F32, name=f"y_turned{c}", tag=f"bank{b}") for c, b in zip(starts, TURN_BANKS)]
-        for j in (3, 2):
+        for planes in ((3,), (0,), (2, 1)):
             for c, bank in zip(starts, turned):
-                nc.tensor.transpose(bank[:, j, :], windows[j][:, c : c + P], ident[:])
+                for j in planes:
+                    nc.tensor.transpose(bank[:, j, :], windows[j][:, c : c + P], ident[:])
         rows = []
 
         def round_block(n):
-            for j in (1, 0):
-                nc.tensor.transpose(turned[n][:, j, :], windows[j][:, starts[n] : starts[n] + P], ident[:])
             row = sb.tile([P, 2, P, 2], BF16, name=f"y_rows{n}", align_bytes=64)
             nc.scalar.copy(out=row[:], in_=turned[n][:].rearrange("c (u e) p -> c u p e", u=2))
             rows.append(row[:].rearrange("c u p e -> c (u p e)").bitcast(F32))
@@ -353,15 +349,13 @@ def tile_attend_grbf_pl_kernel(tc, xT, cT, hx, cs, cd, dp, us, wt, offs, out_0, 
                 in_=back[:].rearrange("p u c -> p c u"),
             )
 
-        groups = [tuple(range(n, min(n + 2, len(starts)))) for n in range(0, len(starts), 2)]
-        for n in groups[0]:
+        for n in range(4):
             round_block(n)
-        for group, following in zip(groups, groups[1:] + [()]):
-            for n in following[:1]:
-                round_block(n)
+        turn_back((0, 1))
+        for n in (4, 5):
+            round_block(n)
+        for group in ((2, 3), (4,), (5,)):
             turn_back(group)
-            for n in following[1:]:
-                round_block(n)
 
         y_scales = sb.tile([P, T // 2], U8, name="y_scales", align_bytes=64)
         words_out = out_1[0].rearrange("p c l -> p (c l)").bitcast(I32)

@@ -26,8 +26,8 @@ T = 2048
 VECTOR_COLUMNS = 1280
 PIECES = ((0, 512), (512, 768))
 TURN_BANKS = (2, 5, 6, 7, 1, 4)
-CHUNKS = ((0, 512), (512, 512), (1024, 256), (1280, 256), (1536, 256), (1792, 128), (1920, 128))
-CODE_STORES = (((0,), "y_codes0"), ((1, 2), "y_codes1"), ((3, 4), "y_words0"), ((5, 6), "y_words512"))
+CHUNKS = tuple((first, 256) for first in range(0, 1792, 256)) + ((1792, 128), (1920, 128))
+CODE_STORES = (((0, 1), "y_codes0"), ((2, 3, 4), "y_codes1"), ((5, 6), "y_words0"), ((7, 8), "y_words512"))
 SCORE_BANKS = ((((0,), 6), ((1,), 7), ((2, 3), 0)), (((0, 1), 6), ((2, 3), 7)))
 PRODUCT_BANKS = ({3: 5, 0: 1, 1: 0, 2: 0}, {3: 6, 0: 7, 1: 3, 2: 3})
 
@@ -111,10 +111,10 @@ def tile_attend_grbf_pl_kernel(tc, xT, cT, hx, cs, cd, dp, us, wt, offs, out_0, 
 
         xr = sb.tile([P, LANES, P, LANES], BF16, name="xr", align_bytes=64)
         for j in range(LANES):
-            turned = ps.tile([P, LANES, P], BF16, name=f"x_turned{j}", tag=f"bank{j}")
+            x_turned = ps.tile([P, LANES, P], BF16, name=f"x_turned{j}", tag=f"bank{j}")
             for t in range(LANES):
-                nc.tensor.transpose(turned[:, t, :], xd[:, t, :, j], ident_bf[:])
-            nc.scalar.copy(out=xr[:, j, :, :], in_=turned[:].rearrange("s t p -> s p t"))
+                nc.tensor.transpose(x_turned[:, t, :], xd[:, t, :, j], ident_bf[:])
+            nc.scalar.copy(out=xr[:, j, :, :], in_=x_turned[:].rearrange("s t p -> s p t"))
         xr_codes, xr_scales = mx_tiles("xr", D)
         nc.vector.quantize_mx(
             out=xr_codes[:].bitcast(E4M3), scales=xr_scales[:], in_=xr[:].rearrange("s j p t -> s (j p t)")
@@ -174,7 +174,8 @@ def tile_attend_grbf_pl_kernel(tc, xT, cT, hx, cs, cd, dp, us, wt, offs, out_0, 
 
         neg_cd2 = sb.tile([P, LANES], F32, name="neg_cd2", align_bytes=64)
         out_planes = out_0.rearrange("(p j) c -> j p c", j=LANES)
-        probs, g_planes, sh_turned, sh_rows, g_words, g_mx, products = {}, {}, {}, {}, {}, {}, {}
+        probs, g_planes, sh_turned, sh_rows, g_words, g_mx = {}, {}, {}, {}, {}, {}
+        product_banks, products, pulls = {}, {}, {}
 
         def exponents(u, n2_row):
             codes, scales = c_mx[u]
@@ -212,7 +213,8 @@ def tile_attend_grbf_pl_kernel(tc, xT, cT, hx, cs, cd, dp, us, wt, offs, out_0, 
             spread(sh_rows[u], sums)
 
         def weave_g(u):
-            g_words[u] = sb.tile([P, HALF, LANES], BF16, name=f"g_words{u}", tag=("g_words0", "pull03")[u], align_bytes=64)
+            buffer = ("g_words0", "pull03")[u]
+            g_words[u] = sb.tile([P, HALF, LANES], BF16, name=f"g_words{u}", tag=buffer, align_bytes=64)
             nc.vector.tensor_copy(
                 out=g_words[u][:].rearrange("s (c i) t -> s c t i", i=4),
                 in_=g_planes[u][:].rearrange("s t (c i) -> s c t i", i=4),
@@ -225,21 +227,28 @@ def tile_attend_grbf_pl_kernel(tc, xT, cT, hx, cs, cd, dp, us, wt, offs, out_0, 
                 out=codes[:].bitcast(E5M2), scales=scales[:], in_=g_words[u][:].rearrange("s i t -> s (i t)")
             )
 
-        banks = {}
-
         def multiply(u, planes):
             codes, scales = g_mx[u]
             for j in planes:
                 bank = PRODUCT_BANKS[u][j]
                 tenants = [k for k in (3, 2, 1, 0) if PRODUCT_BANKS[u][k] == bank]
-                if (u, bank) not in banks:
-                    banks[u, bank] = ps.tile([P, len(tenants), HALF], F32, name=f"xg{u}{j}", tag=f"bank{bank}")
-                products[u, j] = banks[u, bank][:, tenants.index(j), :]
+                if (u, bank) not in product_banks:
+                    product_banks[u, bank] = ps.tile([P, len(tenants), HALF], F32, name=f"xg{u}{j}", tag=f"bank{bank}")
+                products[u, j] = product_banks[u, bank][:, tenants.index(j), :]
                 cols = slice(P * j, P * (j + 1))
                 nc.tensor.matmul_mx(
                     out=products[u, j], lhsT=xr_codes[:, cols].bitcast(E4M3), lhsT_scale=xr_scales[:, cols],
                     rhs=codes[:].bitcast(E5M2), rhs_scale=scales[:], start=True, stop=True,
                 )
+
+        def vector_pull(u, j):
+            pulls[u, j] = sb.tile([P, HALF], F32, name=f"pull{u}{j}", align_bytes=64)[:]
+            nc.vector.tensor_tensor(pulls[u, j], c_planes[j][:, halves[u]], sh_rows[u][:], ALU.mult)
+
+        def sh_to_sbuf(u, buffer):
+            row = sb.tile([P, HALF], F32, name=f"sh_sb{u}", tag=buffer, align_bytes=64)
+            nc.scalar.copy(out=row[:], in_=sh_rows[u][:])
+            return row
 
         def gradient(u, j, place=None):
             dc = place if place is not None else sb.tile([P, HALF], F32, name=f"dc{u}{j}", align_bytes=64)[:]
@@ -269,16 +278,6 @@ def tile_attend_grbf_pl_kernel(tc, xT, cT, hx, cs, cd, dp, us, wt, offs, out_0, 
         multiply(0, (3, 0, 1, 2))
         weights(1, (2, 3))
         sh_as_row(1)
-        pulls = {}
-
-        def vector_pull(u, j):
-            pulls[u, j] = sb.tile([P, HALF], F32, name=f"pull{u}{j}", align_bytes=64)[:]
-            nc.vector.tensor_tensor(pulls[u, j], c_planes[j][:, halves[u]], sh_rows[u][:], ALU.mult)
-
-        def sh_to_sbuf(u, tag):
-            row = sb.tile([P, HALF], F32, name=f"sh_sb{u}", tag=tag, align_bytes=64)
-            nc.scalar.copy(out=row[:], in_=sh_rows[u][:])
-            return row
 
         vector_pull(0, 3)
         sh_sb = [sh_to_sbuf(0, "sh_sb0")]
@@ -357,7 +356,7 @@ def tile_attend_grbf_pl_kernel(tc, xT, cT, hx, cs, cd, dp, us, wt, offs, out_0, 
         for group in ((2, 3), (4,), (5,)):
             turn_back(group)
 
-        y_scales = sb.tile([P, T // 2], U8, name="y_scales", align_bytes=64)
+        y_scales = sb.tile([P, T // 4], U8, name="y_scales", align_bytes=64)
         words_out = out_1[0].rearrange("p c l -> p (c l)").bitcast(I32)
         for group, freed in CODE_STORES:
             start = CHUNKS[group[0]][0]
@@ -365,15 +364,15 @@ def tile_attend_grbf_pl_kernel(tc, xT, cT, hx, cs, cd, dp, us, wt, offs, out_0, 
             y_codes = sb.tile([P, span], U32, name=f"y_codes{group[0]}", tag=freed, align_bytes=64)
             for k in group:
                 first, width = CHUNKS[k]
-                upper, place = divmod(first, T // 2)
+                quarter, place = divmod(first, T // 4)
                 home = max(c for c in y_words if c <= first)
                 nc.vector.quantize_mx(
                     out=y_codes[:, first - start : first - start + width].bitcast(E4M3),
-                    scales=y_scales[4 * upper :, place : place + width],
+                    scales=y_scales[4 * quarter :, place : place + width],
                     in_=y_words[home][:, first - home : first - home + width, :].rearrange("p c t -> p (c t)"),
                 )
             nc.sync.dma_start(out=words_out[:, start : start + span], in_=y_codes[:].bitcast(I32))
-        scales_out = out_2[0].bitcast(I32).rearrange("f (upper c) -> upper f c", upper=2)
+        scales_out = out_2[0].bitcast(I32).rearrange("f (quarter c) -> quarter f c", quarter=4)
         for q in range(4):
             queue = nc.scalar if q < 2 else nc.sync
-            queue.dma_start(out=scales_out[:, 4 * q : 4 * q + 4, :], in_=y_scales[32 * q : 32 * q + 8, :].bitcast(I32))
+            queue.dma_start(out=scales_out[:, 4 * q : 4 * q + 4, :], in_=y_scales[32 * q : 32 * q + 16, :].bitcast(I32))

@@ -98,6 +98,8 @@ def tile_attend_grbf_pl_kernel(tc, xT, cT, hx, cs, cd, dp, us, wt, offs, out_0, 
         for j in (2, 3):
             windows[j] = sb.tile([P, T], F32, name=f"window{j}")
             nc.vector.memset(windows[j][:], 0.0)
+        windows[1] = sb.tile([P, T], F32, name="window1")
+        nc.gpsimd.memset(windows[1][:], 0.0)
 
         xd = sb.tile([P, LANES, P, LANES], BF16, name="xd", align_bytes=64)
         nc.vector.tensor_copy(
@@ -135,6 +137,9 @@ def tile_attend_grbf_pl_kernel(tc, xT, cT, hx, cs, cd, dp, us, wt, offs, out_0, 
             nc.scalar.activation(square[:], c_planes[j], ACT.Square, scale=cs_col[:, j : j + 1])
             for u in range(2):
                 turn_and_add(n2_turned[u], square[:, halves[u]], (j == 0, j == 0), (False, False))
+            if j == 0:
+                windows[0] = sb.tile([P, T], F32, name="window0", tag="table0")
+                nc.gpsimd.memset(windows[0][:], 0.0)
             if j == 1:
                 for u in range(2):
                     nc.scalar.copy(
@@ -175,11 +180,11 @@ def tile_attend_grbf_pl_kernel(tc, xT, cT, hx, cs, cd, dp, us, wt, offs, out_0, 
         neg_cd2 = sb.tile([P, LANES], F32, name="neg_cd2", align_bytes=64)
         out_planes = out_0.rearrange("(p j) c -> j p c", j=LANES)
         probs, g_planes, sh_turned, sh_rows, g_words, g_mx = {}, {}, {}, {}, {}, {}
-        product_banks, products, pulls = {}, {}, {}
+        product_banks, products, pulls, h_planes, weighted, expos = {}, {}, {}, {}, {}, {}
 
-        def exponents(u, n2_row):
+        def exponents(u, n2_row, groups):
             codes, scales = c_mx[u]
-            for group, bank in SCORE_BANKS[u]:
+            for group, bank in groups:
                 a = ps.tile([P, len(group), HALF], F32, name=f"a{u}{group[0]}", tag=f"bank{bank}")
                 for e, t in enumerate(group):
                     cols = slice(P * t, P * (t + 1))
@@ -192,19 +197,28 @@ def tile_attend_grbf_pl_kernel(tc, xT, cT, hx, cs, cd, dp, us, wt, offs, out_0, 
                     nc.vector.scalar_tensor_tensor(
                         expo[:], a[:, e, :], us_col[:, t : t + 1], n2_row[:], ALU.mult, ALU.subtract
                     )
-                    probs[u, t] = sb.tile([P, HALF], F32, name=f"prob{u}{t}")
-                    nc.scalar.activation(probs[u, t][:], expo[:], ACT.Exp, bias=neg_hx[:, t : t + 1])
+                    expos[u, t] = expo
+
+        def probabilities(u):
+            for t in range(LANES):
+                probs[u, t] = sb.tile([P, HALF], F32, name=f"prob{u}{t}")
+                nc.scalar.activation(probs[u, t][:], expos[u, t][:], ACT.Exp, bias=neg_hx[:, t : t + 1])
 
         def weights(u, planes):
             if u not in g_planes:
-                g_planes[u] = sb.tile([P, LANES, HALF], BF16, name=f"g_planes{u}")
+                g_planes[u] = sb.tile([P, LANES, HALF], BF16, name=f"g_planes{u}", align_bytes=64)
                 sh_turned[u] = ps.tile([P, 2, P], F32, name=f"sh_turned{u}", tag=f"bank{2 + u}")
             for t in planes:
                 h = sb.tile([P, HALF], F32, name=f"h{u}{t}", align_bytes=64)
-                nc.vector.scalar_tensor_tensor(
-                    h[:], probs[u, t][:], wt_col[:, t : t + 1], dp_sb[:, t, halves[u]], ALU.mult, ALU.mult
-                )
-                nc.scalar.activation(g_planes[u][:, t, :], h[:], ACT.Copy, scale=us_col[:, t : t + 1])
+                if (u, t) in weighted:
+                    nc.gpsimd.tensor_tensor(h[:], probs[u, t][:], weighted[u, t], ALU.mult)
+                else:
+                    nc.vector.scalar_tensor_tensor(
+                        h[:], probs[u, t][:], wt_col[:, t : t + 1], dp_sb[:, t, halves[u]], ALU.mult, ALU.mult
+                    )
+                h_planes[u, t] = h
+                if (u, t) != (0, LAST):
+                    nc.scalar.activation(g_planes[u][:, t, :], h[:], ACT.Copy, scale=us_col[:, t : t + 1])
                 turn_and_add([sh_turned[u][:, b, :] for b in range(2)], h[:], (t == 0, False), (False, t == LAST))
 
         def sh_as_row(u):
@@ -213,7 +227,7 @@ def tile_attend_grbf_pl_kernel(tc, xT, cT, hx, cs, cd, dp, us, wt, offs, out_0, 
             spread(sh_rows[u], sums)
 
         def weave_g(u):
-            buffer = ("g_words0", "pull03")[u]
+            buffer = f"g_words{u}"
             g_words[u] = sb.tile([P, HALF, LANES], BF16, name=f"g_words{u}", tag=buffer, align_bytes=64)
             nc.vector.tensor_copy(
                 out=g_words[u][:].rearrange("s (c i) t -> s c t i", i=4),
@@ -264,25 +278,33 @@ def tile_attend_grbf_pl_kernel(tc, xT, cT, hx, cs, cd, dp, us, wt, offs, out_0, 
         def store(j):
             nc.sync.dma_start(out=out_planes[j], in_=windows[j][:])
 
-        exponents(0, n2_row)
+        weighted_dp = sb.tile([P, 2, HALF], F32, name="weighted_dp", tag="c_words1", align_bytes=64)
+        for t in range(2):
+            weighted[0, t] = weighted_dp[:, t, :]
+            nc.gpsimd.tensor_scalar(weighted[0, t], dp_sb[:, t, halves[0]], wt_col[:, t : t + 1], 0.0, ALU.mult, ALU.add)
+        neg_cd = sb.tile([P, LANES], F32, name="neg_cd")
+        nc.gpsimd.tensor_scalar(neg_cd[:], cd_col[:], -1.0, 0.0, ALU.mult, ALU.add)
+        nc.gpsimd.tensor_tensor(neg_cd2[:], neg_cd[:], cd_col[:], ALU.mult)
+        exponents(0, n2_row, SCORE_BANKS[0][:2])
+        second_row = n2_as_row(1)
+        exponents(0, n2_row, SCORE_BANKS[0][2:])
+        exponents(1, second_row, SCORE_BANKS[1])
+        for u in range(2):
+            probabilities(u)
         weights(0, range(LANES))
-        for j, freed in ((0, "expo00"), (1, "c_words1")):
-            windows[j] = sb.tile([P, T], F32, name=f"window{j}", tag=freed, align_bytes=64)
-            nc.gpsimd.memset(windows[j][:], 0.0)
         sh_as_row(0)
-        exponents(1, n2_as_row(1))
-        nc.vector.scalar_tensor_tensor(neg_cd2[:], cd_col[:], -1.0, cd_col[:], ALU.mult, ALU.mult)
+        weights(1, (0,))
+        nc.vector.tensor_scalar(g_planes[0][:, LAST, :], h_planes[0, LAST][:], us_col[:, LAST:], None, ALU.mult)
+        weights(1, (1, 2, 3))
         weave_g(0)
-        weights(1, (0, 1))
         quantise_g(0)
         multiply(0, (3, 0, 1, 2))
-        weights(1, (2, 3))
         sh_as_row(1)
 
         vector_pull(0, 3)
         sh_sb = [sh_to_sbuf(0, "sh_sb0")]
-        scalar_scatter(0, 3, gradient(0, 3))
         weave_g(1)
+        scalar_scatter(0, 3, gradient(0, 3))
         quantise_g(1)
         multiply(1, (3, 0, 2, 1))
         vector_pull(1, 3)
@@ -290,7 +312,7 @@ def tile_attend_grbf_pl_kernel(tc, xT, cT, hx, cs, cd, dp, us, wt, offs, out_0, 
         scalar_scatter(1, 3, gradient(1, 3))
         store(3)
         sh_sb.append(sh_to_sbuf(1, "dc13"))
-        late_pulls = sb.tile([P, 5 * HALF], F32, name="late_pulls", tag="pull03", align_bytes=64)
+        late_pulls = sb.tile([P, 5 * HALF], F32, name="late_pulls", tag="g_words1", align_bytes=64)
         for n, (u, j) in enumerate(((0, 0), (0, 1), (0, 2), (1, 2), (1, 1))):
             pulls[u, j] = late_pulls[:, HALF * n : HALF * (n + 1)]
             nc.gpsimd.tensor_tensor(pulls[u, j], c_planes[j][:, halves[u]], sh_sb[u][:], ALU.mult)

@@ -255,8 +255,8 @@ def tile_attend_grbf_pl_kernel(tc, xT, cT, hx, cs, cd, dp, us, wt, offs, out_0, 
                     rhs=codes[:].bitcast(E5M2), rhs_scale=scales[:], start=True, stop=True,
                 )
 
-        def vector_pull(u, j):
-            pulls[u, j] = sb.tile([P, HALF], F32, name=f"pull{u}{j}", align_bytes=64)[:]
+        def vector_pull(u, j, place=None):
+            pulls[u, j] = place if place is not None else sb.tile([P, HALF], F32, name=f"pull{u}{j}", align_bytes=64)[:]
             nc.vector.tensor_tensor(pulls[u, j], c_planes[j][:, halves[u]], sh_rows[u][:], ALU.mult)
 
         def sh_to_sbuf(u, buffer):
@@ -307,19 +307,26 @@ def tile_attend_grbf_pl_kernel(tc, xT, cT, hx, cs, cd, dp, us, wt, offs, out_0, 
         scalar_scatter(0, 3, gradient(0, 3))
         quantise_g(1)
         multiply(1, (3, 0, 2, 1))
-        vector_pull(1, 3)
+        shared = sb.tile([P, 2 * HALF], F32, name="shared", align_bytes=64)
+        vector_pull(1, 3, place=shared[:, HALF // 2 : 3 * HALF // 2])
         vector_pull(1, 0)
+        sh_sb.append(sh_to_sbuf(1, "sh_sb1"))
         scalar_scatter(1, 3, gradient(1, 3))
         store(3)
-        sh_sb.append(sh_to_sbuf(1, "dc13"))
-        late_pulls = sb.tile([P, 5 * HALF], F32, name="late_pulls", tag="g_words1", align_bytes=64)
-        for n, (u, j) in enumerate(((0, 0), (0, 1), (0, 2), (1, 2), (1, 1))):
-            pulls[u, j] = late_pulls[:, HALF * n : HALF * (n + 1)]
-            nc.gpsimd.tensor_tensor(pulls[u, j], c_planes[j][:, halves[u]], sh_sb[u][:], ALU.mult)
+        late_pulls = sb.tile([P, 3 * HALF], F32, name="late_pulls", tag="g_words1", align_bytes=64)
+
+        def gpsimd_pull(u, j, place):
+            pulls[u, j] = place
+            nc.gpsimd.tensor_tensor(place, c_planes[j][:, halves[u]], sh_sb[u][:], ALU.mult)
+
+        for j in range(3):
+            gpsimd_pull(0, j, late_pulls[:, HALF * j : HALF * (j + 1)])
         dc_10 = gradient(1, 0)
         dc_00 = gradient(0, 0, place=pulls[1, 3])
         scalar_scatter(0, 1, gradient(0, 1, place=pulls[1, 0]))
         vector_scatter(0, 0, dc_00)
+        gpsimd_pull(1, 1, shared[:, :HALF])
+        gpsimd_pull(1, 2, shared[:, HALF:])
         scalar_scatter(0, 2, gradient(0, 2, place=pulls[0, 0]))
         vector_scatter(1, 0, dc_10)
         store(0)
@@ -334,8 +341,10 @@ def tile_attend_grbf_pl_kernel(tc, xT, cT, hx, cs, cd, dp, us, wt, offs, out_0, 
             sb.tile([P, LANES, width], BF16, name=f"rounded{k}", align_bytes=64) for k, (first, width) in enumerate(PIECES)
         ]
         for j in (3, 0, 1, 2):
-            engine_copy = nc.gpsimd.tensor_copy if j in (3, 0) else nc.vector.tensor_copy
             for k, (first, width) in enumerate(PIECES):
+                engine_copy = nc.gpsimd.tensor_copy if j in (3, 0) else nc.vector.tensor_copy
+                if (j, k) == (2, 0):
+                    engine_copy = nc.scalar.copy
                 engine_copy(out=rounded[k][:, j, :], in_=windows[j][:, first : first + width])
         for k, (first, width) in enumerate(PIECES):
             y_words[first] = sb.tile([P, width, LANES], BF16, name=f"y_words{first}", align_bytes=64)

@@ -28,7 +28,7 @@ PIECES = ((0, 512), (512, 768))
 TURN_BANKS = (2, 5, 6, 7, 1, 4)
 CHUNKS = tuple((first, 256) for first in range(0, 1792, 256)) + ((1792, 128), (1920, 128))
 CODE_STORES = (((0, 1), "y_codes0"), ((2, 3, 4), "y_codes1"), ((5, 6), "y_words0"), ((7, 8), "y_words512"))
-SCORE_BANKS = ((((0,), 6), ((1,), 7), ((2, 3), 0)), (((0, 1), 6), ((2, 3), 7)))
+SCORE_BANKS = ((((0,), 5), ((1,), 6), ((2,), 7), ((3,), 0)), (((0,), 5), ((1,), 6), ((2, 3), 7)))
 PRODUCT_BANKS = ({3: 5, 0: 1, 1: 0, 2: 0}, {3: 6, 0: 7, 1: 3, 2: 3})
 
 FLOPS = 2 * 2 * D * R * SLOTS
@@ -285,10 +285,8 @@ def tile_attend_grbf_pl_kernel(tc, xT, cT, hx, cs, cd, dp, us, wt, offs, out_0, 
         neg_cd = sb.tile([P, LANES], F32, name="neg_cd")
         nc.gpsimd.tensor_scalar(neg_cd[:], cd_col[:], -1.0, 0.0, ALU.mult, ALU.add)
         nc.gpsimd.tensor_tensor(neg_cd2[:], neg_cd[:], cd_col[:], ALU.mult)
-        exponents(0, n2_row, SCORE_BANKS[0][:2])
-        second_row = n2_as_row(1)
-        exponents(0, n2_row, SCORE_BANKS[0][2:])
-        exponents(1, second_row, SCORE_BANKS[1])
+        exponents(0, n2_row, SCORE_BANKS[0])
+        exponents(1, n2_as_row(1), SCORE_BANKS[1])
         for u in range(2):
             probabilities(u)
         weights(0, range(LANES))

@@ -28,7 +28,7 @@ PIECES = ((0, 512), (512, 768))
 TURN_BANKS = (2, 5, 6, 7, 1, 4)
 CHUNKS = tuple((first, 256) for first in range(0, 1792, 256)) + ((1792, 128), (1920, 128))
 CODE_STORES = (((0, 1), "y_codes0"), ((2, 3, 4), "y_codes1"), ((5, 6), "y_words0"), ((7, 8), "y_words512"))
-SCORE_BANKS = ((((0,), 5), ((1,), 6), ((2,), 7), ((3,), 0)), (((0,), 5), ((1,), 6), ((2, 3), 7)))
+SCORE_BANKS = ((((0,), 5), ((1,), 6), ((2,), 7), ((3,), 0)), (((0,), 5), ((1,), 6), ((2,), 7), ((3,), 0)))
 PRODUCT_BANKS = ({3: 5, 0: 1, 1: 0, 2: 0}, {3: 6, 0: 7, 1: 3, 2: 3})
 
 FLOPS = 2 * 2 * D * R * SLOTS

@@ -282,9 +282,7 @@ def tile_attend_grbf_pl_kernel(tc, xT, cT, hx, cs, cd, dp, us, wt, offs, out_0, 
         for t in range(2):
             weighted[0, t] = weighted_dp[:, t, :]
             nc.gpsimd.tensor_scalar(weighted[0, t], dp_sb[:, t, halves[0]], wt_col[:, t : t + 1], 0.0, ALU.mult, ALU.add)
-        neg_cd = sb.tile([P, LANES], F32, name="neg_cd")
-        nc.gpsimd.tensor_scalar(neg_cd[:], cd_col[:], -1.0, 0.0, ALU.mult, ALU.add)
-        nc.gpsimd.tensor_tensor(neg_cd2[:], neg_cd[:], cd_col[:], ALU.mult)
+        nc.vector.scalar_tensor_tensor(neg_cd2[:], cd_col[:], -1.0, cd_col[:], ALU.mult, ALU.mult)
         exponents(0, n2_row, SCORE_BANKS[0])
         exponents(1, n2_as_row(1), SCORE_BANKS[1])
         for u in range(2):

@@ -282,7 +282,9 @@ def tile_attend_grbf_pl_kernel(tc, xT, cT, hx, cs, cd, dp, us, wt, offs, out_0, 
         for t in range(2):
             weighted[0, t] = weighted_dp[:, t, :]
             nc.gpsimd.tensor_scalar(weighted[0, t], dp_sb[:, t, halves[0]], wt_col[:, t : t + 1], 0.0, ALU.mult, ALU.add)
-        nc.vector.scalar_tensor_tensor(neg_cd2[:], cd_col[:], -1.0, cd_col[:], ALU.mult, ALU.mult)
+        neg_cd = sb.tile([P, LANES], F32, name="neg_cd")
+        nc.gpsimd.tensor_scalar(neg_cd[:], cd_col[:], -1.0, 0.0, ALU.mult, ALU.add)
+        nc.gpsimd.tensor_tensor(neg_cd2[:], neg_cd[:], cd_col[:], ALU.mult)
         exponents(0, n2_row, SCORE_BANKS[0])
         exponents(1, n2_as_row(1), SCORE_BANKS[1])
         for u in range(2):
@@ -339,9 +341,11 @@ def tile_attend_grbf_pl_kernel(tc, xT, cT, hx, cs, cd, dp, us, wt, offs, out_0, 
         for j in (3, 0, 1, 2):
             for k, (first, width) in enumerate(PIECES):
                 engine_copy = nc.gpsimd.tensor_copy if j in (3, 0) else nc.vector.tensor_copy
+                start = 0
                 if (j, k) == (2, 0):
-                    engine_copy = nc.scalar.copy
-                engine_copy(out=rounded[k][:, j, :], in_=windows[j][:, first : first + width])
+                    start = 256
+                    nc.scalar.copy(out=rounded[k][:, j, :start], in_=windows[j][:, :start])
+                engine_copy(out=rounded[k][:, j, start:], in_=windows[j][:, first + start : first + width])
         for k, (first, width) in enumerate(PIECES):
             y_words[first] = sb.tile([P, width, LANES], BF16, name=f"y_words{first}", align_bytes=64)
             nc.vector.tensor_copy(
@@ -351,7 +355,7 @@ def tile_attend_grbf_pl_kernel(tc, xT, cT, hx, cs, cd, dp, us, wt, offs, out_0, 
 
         starts = range(VECTOR_COLUMNS, T, P)
         turned = [ps.tile([P, LANES, P], F32, name=f"y_turned{c}", tag=f"bank{b}") for c, b in zip(starts, TURN_BANKS)]
-        for planes in ((3,), (0,), (2, 1)):
+        for planes in ((3,), (0,), (1, 2)):
             for c, bank in zip(starts, turned):
                 for j in planes:
                     nc.tensor.transpose(bank[:, j, :], windows[j][:, c : c + P], ident[:])

@@ -25,10 +25,12 @@ T = 2048
 
 VECTOR_COLUMNS = 1280
 PIECES = ((0, 512), (512, 768))
+SCALAR_ROUNDS = 256
 TURN_BANKS = (2, 5, 6, 7, 1, 4)
 CHUNKS = tuple((first, 256) for first in range(0, 1792, 256)) + ((1792, 128), (1920, 128))
 CODE_STORES = (((0, 1), "y_codes0"), ((2, 3, 4), "y_codes1"), ((5, 6), "y_words0"), ((7, 8), "y_words512"))
-SCORE_BANKS = ((((0,), 5), ((1,), 6), ((2,), 7), ((3,), 0)), (((0,), 5), ((1,), 6), ((2,), 7), ((3,), 0)))
+SCORE_BANKS = (5, 6, 7, 0)
+GPSIMD_H_PLANES = 2
 PRODUCT_BANKS = ({3: 5, 0: 1, 1: 0, 2: 0}, {3: 6, 0: 7, 1: 3, 2: 3})
 
 FLOPS = 2 * 2 * D * R * SLOTS
@@ -172,32 +174,29 @@ def tile_attend_grbf_pl_kernel(tc, xT, cT, hx, cs, cd, dp, us, wt, offs, out_0, 
             c_mx.append((codes, scales))
             n2_sums.append(slot_sums(f"n2_{u}", n2_turned[u], 0.5))
             if u == 0:
-                n2_row = n2_as_row(u)
+                first_n2_row = n2_as_row(u)
 
         neg_hx = sb.tile([P, LANES], F32, name="neg_hx")
         nc.gpsimd.tensor_scalar(neg_hx[:], hx_col[:], -1.0, 0.0, ALU.mult, ALU.add)
 
         neg_cd2 = sb.tile([P, LANES], F32, name="neg_cd2", align_bytes=64)
         out_planes = out_0.rearrange("(p j) c -> j p c", j=LANES)
-        probs, g_planes, sh_turned, sh_rows, g_words, g_mx = {}, {}, {}, {}, {}, {}
-        product_banks, products, pulls, h_planes, weighted, expos = {}, {}, {}, {}, {}, {}
+        expos, probs, h_planes, g_planes, g_words, g_mx = {}, {}, {}, {}, {}, {}
+        sh_turned, sh_rows, product_banks, products, pulls = {}, {}, {}, {}, {}
 
-        def exponents(u, n2_row, groups):
+        def exponents(u, n2_row):
             codes, scales = c_mx[u]
-            for group, bank in groups:
-                a = ps.tile([P, len(group), HALF], F32, name=f"a{u}{group[0]}", tag=f"bank{bank}")
-                for e, t in enumerate(group):
-                    cols = slice(P * t, P * (t + 1))
-                    nc.tensor.matmul_mx(
-                        out=a[:, e, :], lhsT=xd_codes[:, cols].bitcast(E4M3), lhsT_scale=xd_scales[:, cols],
-                        rhs=codes[:].bitcast(E4M3), rhs_scale=scales[:], start=True, stop=True,
-                    )
-                for e, t in enumerate(group):
-                    expo = sb.tile([P, HALF], F32, name=f"expo{u}{t}", align_bytes=64)
-                    nc.vector.scalar_tensor_tensor(
-                        expo[:], a[:, e, :], us_col[:, t : t + 1], n2_row[:], ALU.mult, ALU.subtract
-                    )
-                    expos[u, t] = expo
+            for t, bank in enumerate(SCORE_BANKS):
+                a = ps.tile([P, HALF], F32, name=f"a{u}{t}", tag=f"bank{bank}")
+                cols = slice(P * t, P * (t + 1))
+                nc.tensor.matmul_mx(
+                    out=a[:], lhsT=xd_codes[:, cols].bitcast(E4M3), lhsT_scale=xd_scales[:, cols],
+                    rhs=codes[:].bitcast(E4M3), rhs_scale=scales[:], start=True, stop=True,
+                )
+                expos[u, t] = sb.tile([P, HALF], F32, name=f"expo{u}{t}", align_bytes=64)
+                nc.vector.scalar_tensor_tensor(
+                    expos[u, t][:], a[:], us_col[:, t : t + 1], n2_row[:], ALU.mult, ALU.subtract
+                )
 
         def probabilities(u):
             for t in range(LANES):
@@ -207,11 +206,11 @@ def tile_attend_grbf_pl_kernel(tc, xT, cT, hx, cs, cd, dp, us, wt, offs, out_0, 
         def weights(u, planes):
             if u not in g_planes:
                 g_planes[u] = sb.tile([P, LANES, HALF], BF16, name=f"g_planes{u}", align_bytes=64)
-                sh_turned[u] = ps.tile([P, 2, P], F32, name=f"sh_turned{u}", tag=f"bank{2 + u}")
+                sh_turned[u] = ps.tile([P, 2, P], F32, name=f"sh_turned{u}", tag=("bank6", "bank3")[u])
             for t in planes:
                 h = sb.tile([P, HALF], F32, name=f"h{u}{t}", align_bytes=64)
-                if (u, t) in weighted:
-                    nc.gpsimd.tensor_tensor(h[:], probs[u, t][:], weighted[u, t], ALU.mult)
+                if u == 0 and t < GPSIMD_H_PLANES:
+                    nc.gpsimd.tensor_tensor(h[:], probs[u, t][:], weighted_dp[:, t, :], ALU.mult)
                 else:
                     nc.vector.scalar_tensor_tensor(
                         h[:], probs[u, t][:], wt_col[:, t : t + 1], dp_sb[:, t, halves[u]], ALU.mult, ALU.mult
@@ -227,8 +226,7 @@ def tile_attend_grbf_pl_kernel(tc, xT, cT, hx, cs, cd, dp, us, wt, offs, out_0, 
             spread(sh_rows[u], sums)
 
         def weave_g(u):
-            buffer = f"g_words{u}"
-            g_words[u] = sb.tile([P, HALF, LANES], BF16, name=f"g_words{u}", tag=buffer, align_bytes=64)
+            g_words[u] = sb.tile([P, HALF, LANES], BF16, name=f"g_words{u}", align_bytes=64)
             nc.vector.tensor_copy(
                 out=g_words[u][:].rearrange("s (c i) t -> s c t i", i=4),
                 in_=g_planes[u][:].rearrange("s t (c i) -> s c t i", i=4),
@@ -256,13 +254,19 @@ def tile_attend_grbf_pl_kernel(tc, xT, cT, hx, cs, cd, dp, us, wt, offs, out_0, 
                 )
 
         def vector_pull(u, j, place=None):
-            pulls[u, j] = place if place is not None else sb.tile([P, HALF], F32, name=f"pull{u}{j}", align_bytes=64)[:]
-            nc.vector.tensor_tensor(pulls[u, j], c_planes[j][:, halves[u]], sh_rows[u][:], ALU.mult)
+            if place is None:
+                place = sb.tile([P, HALF], F32, name=f"pull{u}{j}", align_bytes=64)[:]
+            pulls[u, j] = place
+            nc.vector.tensor_tensor(place, c_planes[j][:, halves[u]], sh_rows[u][:], ALU.mult)
 
-        def sh_to_sbuf(u, buffer):
-            row = sb.tile([P, HALF], F32, name=f"sh_sb{u}", tag=buffer, align_bytes=64)
+        def sh_to_sbuf(u):
+            row = sb.tile([P, HALF], F32, name=f"sh_sb{u}", align_bytes=64)
             nc.scalar.copy(out=row[:], in_=sh_rows[u][:])
             return row
+
+        def gpsimd_pull(u, j, place):
+            pulls[u, j] = place
+            nc.gpsimd.tensor_tensor(place, c_planes[j][:, halves[u]], sh_sb[u][:], ALU.mult)
 
         def gradient(u, j, place=None):
             dc = place if place is not None else sb.tile([P, HALF], F32, name=f"dc{u}{j}", align_bytes=64)[:]
@@ -278,15 +282,16 @@ def tile_attend_grbf_pl_kernel(tc, xT, cT, hx, cs, cd, dp, us, wt, offs, out_0, 
         def store(j):
             nc.sync.dma_start(out=out_planes[j], in_=windows[j][:])
 
-        weighted_dp = sb.tile([P, 2, HALF], F32, name="weighted_dp", tag="c_words1", align_bytes=64)
-        for t in range(2):
-            weighted[0, t] = weighted_dp[:, t, :]
-            nc.gpsimd.tensor_scalar(weighted[0, t], dp_sb[:, t, halves[0]], wt_col[:, t : t + 1], 0.0, ALU.mult, ALU.add)
+        weighted_dp = sb.tile([P, GPSIMD_H_PLANES, HALF], F32, name="weighted_dp", tag="c_words1", align_bytes=64)
+        for t in range(GPSIMD_H_PLANES):
+            nc.gpsimd.tensor_scalar(
+                weighted_dp[:, t, :], dp_sb[:, t, halves[0]], wt_col[:, t : t + 1], 0.0, ALU.mult, ALU.add
+            )
         neg_cd = sb.tile([P, LANES], F32, name="neg_cd")
         nc.gpsimd.tensor_scalar(neg_cd[:], cd_col[:], -1.0, 0.0, ALU.mult, ALU.add)
         nc.gpsimd.tensor_tensor(neg_cd2[:], neg_cd[:], cd_col[:], ALU.mult)
-        exponents(0, n2_row, SCORE_BANKS[0])
-        exponents(1, n2_as_row(1), SCORE_BANKS[1])
+        exponents(0, first_n2_row)
+        exponents(1, n2_as_row(1))
         for u in range(2):
             probabilities(u)
         weights(0, range(LANES))
@@ -300,31 +305,26 @@ def tile_attend_grbf_pl_kernel(tc, xT, cT, hx, cs, cd, dp, us, wt, offs, out_0, 
         sh_as_row(1)
 
         vector_pull(0, 3)
-        sh_sb = [sh_to_sbuf(0, "sh_sb0")]
+        sh_sb = [sh_to_sbuf(0)]
         weave_g(1)
         scalar_scatter(0, 3, gradient(0, 3))
         quantise_g(1)
         multiply(1, (3, 0, 2, 1))
-        shared = sb.tile([P, 2 * HALF], F32, name="shared", align_bytes=64)
-        vector_pull(1, 3, place=shared[:, HALF // 2 : 3 * HALF // 2])
+        reused = sb.tile([P, 2 * HALF], F32, name="reused", align_bytes=64)
+        vector_pull(1, 3, place=reused[:, HALF // 2 : 3 * HALF // 2])
         vector_pull(1, 0)
-        sh_sb.append(sh_to_sbuf(1, "sh_sb1"))
+        sh_sb.append(sh_to_sbuf(1))
         scalar_scatter(1, 3, gradient(1, 3))
         store(3)
         late_pulls = sb.tile([P, 3 * HALF], F32, name="late_pulls", tag="g_words1", align_bytes=64)
-
-        def gpsimd_pull(u, j, place):
-            pulls[u, j] = place
-            nc.gpsimd.tensor_tensor(place, c_planes[j][:, halves[u]], sh_sb[u][:], ALU.mult)
-
         for j in range(3):
             gpsimd_pull(0, j, late_pulls[:, HALF * j : HALF * (j + 1)])
         dc_10 = gradient(1, 0)
         dc_00 = gradient(0, 0, place=pulls[1, 3])
         scalar_scatter(0, 1, gradient(0, 1, place=pulls[1, 0]))
         vector_scatter(0, 0, dc_00)
-        gpsimd_pull(1, 1, shared[:, :HALF])
-        gpsimd_pull(1, 2, shared[:, HALF:])
+        gpsimd_pull(1, 1, reused[:, :HALF])
+        gpsimd_pull(1, 2, reused[:, HALF:])
         scalar_scatter(0, 2, gradient(0, 2, place=pulls[0, 0]))
         vector_scatter(1, 0, dc_10)
         store(0)
@@ -339,13 +339,13 @@ def tile_attend_grbf_pl_kernel(tc, xT, cT, hx, cs, cd, dp, us, wt, offs, out_0, 
             sb.tile([P, LANES, width], BF16, name=f"rounded{k}", align_bytes=64) for k, (first, width) in enumerate(PIECES)
         ]
         for j in (3, 0, 1, 2):
+            engine_copy = nc.gpsimd.tensor_copy if j in (3, 0) else nc.vector.tensor_copy
+            done = SCALAR_ROUNDS if j == 2 else 0
+            if done:
+                nc.scalar.copy(out=rounded[0][:, j, :done], in_=windows[j][:, :done])
             for k, (first, width) in enumerate(PIECES):
-                engine_copy = nc.gpsimd.tensor_copy if j in (3, 0) else nc.vector.tensor_copy
-                start = 0
-                if (j, k) == (2, 0):
-                    start = 256
-                    nc.scalar.copy(out=rounded[k][:, j, :start], in_=windows[j][:, :start])
-                engine_copy(out=rounded[k][:, j, start:], in_=windows[j][:, first + start : first + width])
+                skip = max(done - first, 0)
+                engine_copy(out=rounded[k][:, j, skip:], in_=windows[j][:, first + skip : first + width])
         for k, (first, width) in enumerate(PIECES):
             y_words[first] = sb.tile([P, width, LANES], BF16, name=f"y_words{first}", align_bytes=64)
             nc.vector.tensor_copy(

@@ -22,16 +22,18 @@ R = 512
 SLOTS = 512
 HALF = SLOTS // 2
 T = 2048
+CS, HX, US, WT, CD = range(5)
 
 VECTOR_COLUMNS = 1280
 PIECES = ((0, 512), (512, 768))
 SCALAR_ROUNDS = 256
-TURN_BANKS = (2, 5, 6, 7, 1, 4)
+TURN_BANKS = (6, 7, 4, 0, 2, 1)
+BACK_BANKS = (5, 3, 6, 7)
 CHUNKS = tuple((first, 256) for first in range(0, 1792, 256)) + ((1792, 128), (1920, 128))
 CODE_STORES = (((0, 1), "y_codes0"), ((2, 3, 4), "y_codes1"), ((5, 6), "y_words0"), ((7, 8), "y_words512"))
-SCORE_BANKS = (5, 6, 7, 0)
+SCORE_BANKS = ((3, 4, 5, 6), (7, 0, 1, 3))
 GPSIMD_H_PLANES = 2
-PRODUCT_BANKS = ({3: 5, 0: 1, 1: 0, 2: 0}, {3: 6, 0: 7, 1: 3, 2: 3})
+PRODUCT_BANKS = ({3: 3, 2: 4, 1: 5, 0: 5}, {3: 0, 2: 2, 1: 3, 0: 3})
 
 FLOPS = 2 * 2 * D * R * SLOTS
 
@@ -42,15 +44,19 @@ def tile_attend_grbf_pl_kernel(tc, xT, cT, hx, cs, cd, dp, us, wt, offs, out_0, 
         sb = ctx.enter_context(tc.tile_pool(name="sb", bufs=1))
         ps = ctx.enter_context(tc.psum_pool(name="ps", bufs=1))
 
-        def mx_tiles(name, width):
-            codes = sb.tile([P, width], U32, name=name + "_codes", align_bytes=64)
-            scales = sb.tile([P, width], U8, name=name + "_scales", align_bytes=64)
-            return codes, scales
+        def buf(name, shape, dtype=F32, tag=None):
+            return sb.tile(shape, dtype, name=name, tag=tag or name, align_bytes=64)
 
-        def by_lane(name, src, queue):
-            vector = sb.tile([P, LANES], F32, name=name)
-            queue.dma_start(out=vector[:], in_=src)
-            return vector
+        def bank(name, shape, number, dtype=F32):
+            return ps.tile(shape, dtype, name=name, tag=f"bank{number}")
+
+        def mx_tiles(name, width, tag=None):
+            return buf(name + "_codes", [P, width], U32, tag), buf(name + "_scales", [P, width], U8)
+
+        def quantise(tiles, words, fmt, cols=None):
+            codes, scales = tiles
+            cols = cols if cols is not None else slice(0, codes.shape[1])
+            nc.vector.quantize_mx(out=codes[:, cols].bitcast(fmt), scales=scales[:, cols], in_=words)
 
         def turn_and_add(turned, plane, start, stop):
             for b in range(2):
@@ -61,8 +67,8 @@ def tile_attend_grbf_pl_kernel(tc, xT, cT, hx, cs, cd, dp, us, wt, offs, out_0, 
         def slot_sums(name, turned, scale):
             sums = []
             for b in range(2):
-                total = sb.tile([P, 1], F32, name=f"{name}_col{b}")
-                terms = sb.tile([P, P], F32, name=f"{name}_summed{b}")
+                total = buf(f"{name}_col{b}", [P, 1])
+                terms = buf(f"{name}_summed{b}", [P, P])
                 nc.scalar.activation(terms[:], turned[b], ACT.Identity, scale=scale, accum_out=total[:])
                 sums.append(total)
             return sums
@@ -73,203 +79,197 @@ def tile_attend_grbf_pl_kernel(tc, xT, cT, hx, cs, cd, dp, us, wt, offs, out_0, 
 
         halves = [slice(HALF * u, HALF * (u + 1)) for u in range(2)]
 
-        x_raw = sb.tile([P, LANES, R], F32, name="x_raw")
-        nc.sync.dma_start(out=x_raw[:], in_=xT.rearrange("(p j) r -> p j r", j=LANES))
         offsets = sb.tile([P, SLOTS // 16], U16, name="offsets")
         nc.sync.dma_start(offsets[:], offs)
-        cs_col = by_lane("cs_col", cs[0, :].rearrange("(p j) -> p j", j=LANES), nc.scalar)
-        hx_col = by_lane("hx_col", hx.rearrange("(s t) o -> s (t o)", t=LANES), nc.scalar)
+        rows = buf("rows", [P, D])
+        nc.gpsimd.memset(rows[:], 0.0)
+        for k, vector in enumerate((cs[0:1, :], hx, us, wt, cd)):
+            nc.scalar.dma_start(out=rows[k : k + 1, :], in_=vector if k == CS else vector.rearrange("r o -> o r"))
         cT_planes = cT.rearrange("(p j) c -> j p c", j=LANES)
         table = []
         for j in range(LANES):
-            plane = sb.tile([P, T], F32, name=f"table{j}")
+            plane = buf(f"table{j}", [P, T])
             nc.sync.dma_start(out=plane[:], in_=cT_planes[j])
             table.append(plane)
-        us_col = by_lane("us_col", us.rearrange("(s t) o -> s (t o)", t=LANES), nc.sync)
-        wt_col = by_lane("wt_col", wt.rearrange("(s t) o -> s (t o)", t=LANES), nc.sync)
-        cd_col = by_lane("cd_col", cd.rearrange("(p j) o -> p (j o)", j=LANES), nc.sync)
-        dp_sb = sb.tile([P, LANES, SLOTS], F32, name="dp_sb")
-        nc.sync.dma_start(out=dp_sb[:], in_=dp.rearrange("(s t) i -> s t i", t=LANES))
+        x_raw = buf("x_raw", [P, LANES, R])
+        nc.sync.dma_start(out=x_raw[:], in_=xT.rearrange("(p j) r -> p j r", j=LANES))
+        dp_rows = dp.rearrange("(s t) i -> s t i", t=LANES)
+        dp_pairs = []
+        for v in range(2):
+            pair = buf(f"dp_pair{v}", [P, 2, SLOTS])
+            nc.sync.dma_start(out=pair[:], in_=dp_rows[:, 2 * v : 2 * v + 2, :])
+            dp_pairs.append(pair)
 
-        ident = sb.tile([P, P], F32, name="ident")
+        def dp_part(u, t):
+            return dp_pairs[t // 2][:, t % 2, halves[u]]
+
+        ident = buf("ident", [P, P])
         make_identity(nc, ident[:])
-        ident_bf = sb.tile([P, P], BF16, name="ident_bf")
-        make_identity(nc, ident_bf[:])
-
         windows = {}
-        for j in (2, 3):
-            windows[j] = sb.tile([P, T], F32, name=f"window{j}")
-            nc.vector.memset(windows[j][:], 0.0)
-        windows[1] = sb.tile([P, T], F32, name="window1")
-        nc.gpsimd.memset(windows[1][:], 0.0)
+        for j in (3, 2, 1, 0):
+            windows[j] = buf(f"window{j}", [P, T])
+            (nc.vector if j > 1 else nc.gpsimd).memset(windows[j][:], 0.0)
 
-        xd = sb.tile([P, LANES, P, LANES], BF16, name="xd", align_bytes=64)
-        nc.vector.tensor_copy(
-            out=xd[:].rearrange("p t s j -> p s j t"),
-            in_=x_raw[:].rearrange("p j (s t) -> p s j t", t=LANES),
-        )
-        xd_codes, xd_scales = mx_tiles("xd", R)
-        nc.vector.quantize_mx(
-            out=xd_codes[:].bitcast(E4M3), scales=xd_scales[:], in_=xd[:].rearrange("p t s j -> p (t s j)")
-        )
-
-        xr = sb.tile([P, LANES, P, LANES], BF16, name="xr", align_bytes=64)
+        cols_ps = bank("cols_ps", [P, LANES, P], 2)
         for j in range(LANES):
-            x_turned = ps.tile([P, LANES, P], BF16, name=f"x_turned{j}", tag=f"bank{j}")
-            for t in range(LANES):
-                nc.tensor.transpose(x_turned[:, t, :], xd[:, t, :, j], ident_bf[:])
-            nc.scalar.copy(out=xr[:, j, :, :], in_=x_turned[:].rearrange("s t p -> s p t"))
-        xr_codes, xr_scales = mx_tiles("xr", D)
-        nc.vector.quantize_mx(
-            out=xr_codes[:].bitcast(E4M3), scales=xr_scales[:], in_=xr[:].rearrange("s j p t -> s (j p t)")
-        )
+            nc.tensor.transpose(cols_ps[:, j, :], rows[:, j : D : LANES], ident[:])
+        cols = buf("cols", [P, LANES, 8])
+        nc.scalar.copy(out=cols[:], in_=cols_ps[:, :, 0:8])
+        neg_hx = buf("neg_hx", [P, LANES])
+        nc.gpsimd.tensor_scalar(neg_hx[:], cols[:, :, HX], -1.0, 0.0, ALU.mult, ALU.add)
+        neg_cd = buf("neg_cd", [P, LANES])
+        nc.gpsimd.tensor_scalar(neg_cd[:], cols[:, :, CD], -1.0, 0.0, ALU.mult, ALU.add)
+        neg_cd2 = buf("neg_cd2", [P, LANES])
+        nc.gpsimd.tensor_tensor(neg_cd2[:], neg_cd[:], cols[:, :, CD], ALU.mult)
 
-        c_pairs = [
-            sb.tile([P, 2, SLOTS], F32, name=f"c_pair{u}", tag=("c_pair0", "xr")[u], align_bytes=64) for u in range(2)
-        ]
+        def col(k, j):
+            return cols[:, j, k : k + 1]
+
+        c_pairs = [buf(f"c_pair{v}", [P, 2, SLOTS]) for v in range(2)]
         c_planes = [c_pairs[j // 2][:, j % 2, :] for j in range(LANES)]
-        c_words = [sb.tile([P, HALF, LANES], BF16, name=f"c_words{u}", align_bytes=64) for u in range(2)]
-        n2_turned = [
-            [ps.tile([P, P], F32, name=f"n2_turned{u}{b}", tag=f"bank{4 + 2 * u + b}")[:] for b in range(2)]
-            for u in range(2)
-        ]
+        c_words = [buf(f"c_words{u}", [P, HALF, LANES], BF16) for u in range(2)]
+        n2_turned = [[bank(f"n2_turned{u}{b}", [P, P], 4 + 2 * u + b)[:] for b in range(2)] for u in range(2)]
+
+        def lay_centres(u, v):
+            nc.vector.tensor_copy(
+                out=c_words[u][:, :, 2 * v : 2 * v + 2], in_=c_pairs[v][:, :, halves[u]].rearrange("p e i -> p i e")
+            )
+
         for j in range(LAST):
-            square = sb.tile([P, SLOTS], F32, name=f"square{j}")
+            square = buf(f"square{j}", [P, SLOTS])
             nc.vector.tensor_copy(c_planes[j], table[j][:].indirect(offsets[:]))
-            nc.scalar.activation(square[:], c_planes[j], ACT.Square, scale=cs_col[:, j : j + 1])
+            nc.scalar.activation(square[:], c_planes[j], ACT.Square, scale=col(CS, j))
             for u in range(2):
                 turn_and_add(n2_turned[u], square[:, halves[u]], (j == 0, j == 0), (False, False))
-            if j == 0:
-                windows[0] = sb.tile([P, T], F32, name="window0", tag="table0")
-                nc.gpsimd.memset(windows[0][:], 0.0)
             if j == 1:
                 for u in range(2):
-                    nc.scalar.copy(
-                        out=c_words[u][:, :, 0:2], in_=c_pairs[0][:, :, halves[u]].rearrange("p e i -> p i e")
-                    )
+                    lay_centres(u, 0)
         half_lists = [offsets[:, HALF // 16 * u : HALF // 16 * (u + 1)] for u in range(2)]
         for u in range(2):
             nc.vector.tensor_copy(c_planes[LAST][:, halves[u]], table[LAST][:].indirect(half_lists[u]))
-            square = sb.tile([P, HALF], F32, name=f"square{LAST}_{u}", align_bytes=64)
-            nc.scalar.activation(square[:], c_planes[LAST][:, halves[u]], ACT.Square, scale=cs_col[:, LAST:])
+            square = buf(f"square{LAST}_{u}", [P, HALF])
+            nc.scalar.activation(square[:], c_planes[LAST][:, halves[u]], ACT.Square, scale=col(CS, LAST))
             turn_and_add(n2_turned[u], square[:], (False, False), (True, True))
         for u in range(2):
-            nc.vector.tensor_copy(
-                out=c_words[u][:, :, 2:4], in_=c_pairs[1][:, :, halves[u]].rearrange("p e i -> p i e")
-            )
-
-        def n2_as_row(u):
-            spread_ps = ps.tile([P, HALF], F32, name=f"n2_row_ps{u}", tag=f"bank{u}")
-            spread(spread_ps, n2_sums[u])
-            row = sb.tile([P, HALF], F32, name=f"n2_row{u}")
-            nc.scalar.copy(out=row[:], in_=spread_ps[:])
-            return row
-
-        c_mx, n2_sums = [], []
+            lay_centres(u, 1)
+        n2_rows = []
         for u in range(2):
-            codes, scales = mx_tiles(f"c{u}", HALF)
-            nc.vector.quantize_mx(
-                out=codes[:].bitcast(E4M3), scales=scales[:], in_=c_words[u][:].rearrange("p i t -> p (i t)")
-            )
-            c_mx.append((codes, scales))
-            n2_sums.append(slot_sums(f"n2_{u}", n2_turned[u], 0.5))
-            if u == 0:
-                first_n2_row = n2_as_row(u)
+            sums = slot_sums(f"n2_{u}", n2_turned[u], 0.5)
+            spread_ps = bank(f"n2_row_ps{u}", [P, HALF], u)
+            spread(spread_ps, sums)
+            row = buf(f"n2_row{u}", [P, HALF])
+            nc.scalar.copy(out=row[:], in_=spread_ps[:])
+            n2_rows.append(row)
 
-        neg_hx = sb.tile([P, LANES], F32, name="neg_hx")
-        nc.gpsimd.tensor_scalar(neg_hx[:], hx_col[:], -1.0, 0.0, ALU.mult, ALU.add)
+        c_mx = [mx_tiles("c0", HALF)]
+        quantise(c_mx[0], c_words[0][:].rearrange("p i t -> p (i t)"), E4M3)
+        xd_all = buf("xd", [P, LANES, P, LANES], BF16, tag=f"square{LAST}_1")
+        xd = [xd_all[:, 2 * v : 2 * v + 2, :, :] for v in range(2)]
+        x_dealt = x_raw[:].rearrange("p j (s t) -> p s j t", t=LANES)
+        for v in range(2):
+            nc.vector.tensor_copy(out=xd[v].rearrange("p t s j -> p s j t"), in_=x_dealt[:, :, :, 2 * v : 2 * v + 2])
+        xd_mx = []
+        for v in range(2):
+            xd_mx.append(mx_tiles(f"xd{v}", 2 * P))
+            quantise(xd_mx[v], xd[v].rearrange("p t s j -> p (t s j)"), E4M3)
+        c_mx.append(mx_tiles("c1", HALF, tag="x_raw"))
+        quantise(c_mx[1], c_words[1][:].rearrange("p i t -> p (i t)"), E4M3)
 
-        neg_cd2 = sb.tile([P, LANES], F32, name="neg_cd2", align_bytes=64)
+        weighted_dp = buf("weighted_dp", [P, GPSIMD_H_PLANES, HALF], tag="c_words1")
+        for t in range(GPSIMD_H_PLANES):
+            nc.gpsimd.tensor_scalar(weighted_dp[:, t, :], dp_part(0, t), col(WT, t), 0.0, ALU.mult, ALU.add)
+
         out_planes = out_0.rearrange("(p j) c -> j p c", j=LANES)
-        expos, probs, h_planes, g_planes, g_words, g_mx = {}, {}, {}, {}, {}, {}
-        sh_turned, sh_rows, product_banks, products, pulls = {}, {}, {}, {}, {}
+        expos, probs, h_tiles, g_words, g_mx, xr, xr_mx = {}, {}, {}, {}, {}, {}, {}
+        sh_turned, sh_rows, sh_sb, product_banks, products, pulls = {}, {}, {}, {}, {}, {}
 
-        def exponents(u, n2_row):
-            codes, scales = c_mx[u]
-            for t, bank in enumerate(SCORE_BANKS):
-                a = ps.tile([P, HALF], F32, name=f"a{u}{t}", tag=f"bank{bank}")
-                cols = slice(P * t, P * (t + 1))
-                nc.tensor.matmul_mx(
-                    out=a[:], lhsT=xd_codes[:, cols].bitcast(E4M3), lhsT_scale=xd_scales[:, cols],
-                    rhs=codes[:].bitcast(E4M3), rhs_scale=scales[:], start=True, stop=True,
-                )
-                expos[u, t] = sb.tile([P, HALF], F32, name=f"expo{u}{t}", align_bytes=64)
-                nc.vector.scalar_tensor_tensor(
-                    expos[u, t][:], a[:], us_col[:, t : t + 1], n2_row[:], ALU.mult, ALU.subtract
-                )
+        def product_pass(out, stationary, b, moving, fmt):
+            (s_codes, s_scales), (m_codes, m_scales) = stationary, moving
+            block = slice(P * b, P * (b + 1))
+            nc.tensor.matmul_mx(
+                out=out, lhsT=s_codes[:, block].bitcast(E4M3), lhsT_scale=s_scales[:, block],
+                rhs=m_codes[:].bitcast(fmt), rhs_scale=m_scales[:], start=True, stop=True,
+            )
 
-        def probabilities(u):
+        for u in range(2):
+            for t, number in enumerate(SCORE_BANKS[u]):
+                a = bank(f"a{u}{t}", [P, HALF], number)
+                product_pass(a[:], xd_mx[t // 2], t % 2, c_mx[u], E4M3)
+                expos[u, t] = buf(f"expo{u}{t}", [P, HALF])
+                nc.vector.scalar_tensor_tensor(expos[u, t][:], a[:], col(US, t), n2_rows[u][:], ALU.mult, ALU.subtract)
+        for u in range(2):
             for t in range(LANES):
-                probs[u, t] = sb.tile([P, HALF], F32, name=f"prob{u}{t}")
+                probs[u, t] = buf(f"prob{u}{t}", [P, HALF])
                 nc.scalar.activation(probs[u, t][:], expos[u, t][:], ACT.Exp, bias=neg_hx[:, t : t + 1])
 
+        def turn_x(v, number):
+            x_turned = bank(f"x_turned{v}", [P, LANES, P], number)
+            for t in range(LANES):
+                pairs = xd[t // 2][:, t % 2, :, :].rearrange("p s j -> p (s j)").bitcast(F32)
+                nc.tensor.transpose(x_turned[:, t, :], pairs[:, v : 2 * P : 2], ident[:])
+            xr[v] = buf(f"xr{v}", [P, 2, P, LANES], BF16)
+            nc.scalar.copy(
+                out=xr[v][:],
+                in_=x_turned[:].rearrange("s t p -> s (t p)").bitcast(BF16).rearrange("s (t p e) -> s e p t", t=LANES, e=2),
+            )
+
+        def quantise_x(v):
+            xr_mx[v] = mx_tiles(f"xr{v}", 2 * P)
+            quantise(xr_mx[v], xr[v][:].rearrange("s e p t -> s (e p t)"), E4M3)
+
         def weights(u, planes):
-            if u not in g_planes:
-                g_planes[u] = sb.tile([P, LANES, HALF], BF16, name=f"g_planes{u}", align_bytes=64)
-                sh_turned[u] = ps.tile([P, 2, P], F32, name=f"sh_turned{u}", tag=("bank6", "bank3")[u])
+            if u not in h_tiles:
+                h_tiles[u] = buf(f"h{u}", [P, LANES, HALF])
+                sh_turned[u] = bank(f"sh_turned{u}", [P, 2, P], (4, 7)[u])
             for t in planes:
-                h = sb.tile([P, HALF], F32, name=f"h{u}{t}", align_bytes=64)
+                h = h_tiles[u][:, t, :]
                 if u == 0 and t < GPSIMD_H_PLANES:
-                    nc.gpsimd.tensor_tensor(h[:], probs[u, t][:], weighted_dp[:, t, :], ALU.mult)
+                    nc.gpsimd.tensor_tensor(h, probs[u, t][:], weighted_dp[:, t, :], ALU.mult)
                 else:
-                    nc.vector.scalar_tensor_tensor(
-                        h[:], probs[u, t][:], wt_col[:, t : t + 1], dp_sb[:, t, halves[u]], ALU.mult, ALU.mult
-                    )
-                h_planes[u, t] = h
-                if (u, t) != (0, LAST):
-                    nc.scalar.activation(g_planes[u][:, t, :], h[:], ACT.Copy, scale=us_col[:, t : t + 1])
-                turn_and_add([sh_turned[u][:, b, :] for b in range(2)], h[:], (t == 0, False), (False, t == LAST))
+                    nc.vector.scalar_tensor_tensor(h, probs[u, t][:], col(WT, t), dp_part(u, t), ALU.mult, ALU.mult)
+                turn_and_add([sh_turned[u][:, b, :] for b in range(2)], h, (t == 0, False), (False, t == LAST))
 
         def sh_as_row(u):
             sums = slot_sums(f"sh{u}", [sh_turned[u][:, b, :] for b in range(2)], 1.0)
-            sh_rows[u] = ps.tile([P, HALF], F32, name=f"sh_row{u}", tag=("bank2", "bank4")[u])
+            sh_rows[u] = bank(f"sh_row{u}", [P, HALF], u)
             spread(sh_rows[u], sums)
 
-        def weave_g(u):
-            g_words[u] = sb.tile([P, HALF, LANES], BF16, name=f"g_words{u}", align_bytes=64)
-            nc.vector.tensor_copy(
-                out=g_words[u][:].rearrange("s (c i) t -> s c t i", i=4),
-                in_=g_planes[u][:].rearrange("s t (c i) -> s c t i", i=4),
+        def form_g(u):
+            g_words[u] = buf(f"g_words{u}", [P, HALF, LANES], BF16)
+            nc.vector.tensor_tensor(
+                g_words[u][:].rearrange("s (c i) t -> s c t i", i=2),
+                h_tiles[u][:].rearrange("s t (c i) -> s c t i", i=2),
+                cols_ps[:, :, US : US + 1].unsqueeze(1).broadcast_to([P, HALF // 2, LANES, 2]),
+                ALU.mult,
             )
 
         def quantise_g(u):
             g_mx[u] = mx_tiles(f"g{u}", HALF)
-            codes, scales = g_mx[u]
-            nc.vector.quantize_mx(
-                out=codes[:].bitcast(E5M2), scales=scales[:], in_=g_words[u][:].rearrange("s i t -> s (i t)")
-            )
+            quantise(g_mx[u], g_words[u][:].rearrange("s i t -> s (i t)"), E5M2)
 
         def multiply(u, planes):
-            codes, scales = g_mx[u]
             for j in planes:
-                bank = PRODUCT_BANKS[u][j]
-                tenants = [k for k in (3, 2, 1, 0) if PRODUCT_BANKS[u][k] == bank]
-                if (u, bank) not in product_banks:
-                    product_banks[u, bank] = ps.tile([P, len(tenants), HALF], F32, name=f"xg{u}{j}", tag=f"bank{bank}")
-                products[u, j] = product_banks[u, bank][:, tenants.index(j), :]
-                cols = slice(P * j, P * (j + 1))
-                nc.tensor.matmul_mx(
-                    out=products[u, j], lhsT=xr_codes[:, cols].bitcast(E4M3), lhsT_scale=xr_scales[:, cols],
-                    rhs=codes[:].bitcast(E5M2), rhs_scale=scales[:], start=True, stop=True,
-                )
+                number = PRODUCT_BANKS[u][j]
+                tenants = [k for k in range(LANES) if PRODUCT_BANKS[u][k] == number]
+                if (u, number) not in product_banks:
+                    product_banks[u, number] = bank(f"xg{u}{j}", [P, len(tenants), HALF], number)
+                products[u, j] = product_banks[u, number][:, tenants.index(j), :]
+                product_pass(products[u, j], xr_mx[j // 2], j % 2, g_mx[u], E5M2)
 
-        def vector_pull(u, j, place=None):
-            if place is None:
-                place = sb.tile([P, HALF], F32, name=f"pull{u}{j}", align_bytes=64)[:]
-            pulls[u, j] = place
-            nc.vector.tensor_tensor(place, c_planes[j][:, halves[u]], sh_rows[u][:], ALU.mult)
+        def vector_pull(u, j):
+            pulls[u, j] = buf(f"pull{u}{j}", [P, HALF])[:]
+            nc.vector.tensor_tensor(pulls[u, j], c_planes[j][:, halves[u]], sh_rows[u][:], ALU.mult)
 
         def sh_to_sbuf(u):
-            row = sb.tile([P, HALF], F32, name=f"sh_sb{u}", align_bytes=64)
-            nc.scalar.copy(out=row[:], in_=sh_rows[u][:])
-            return row
+            sh_sb[u] = buf(f"sh_sb{u}", [P, HALF])
+            nc.scalar.copy(out=sh_sb[u][:], in_=sh_rows[u][:])
 
         def gpsimd_pull(u, j, place):
             pulls[u, j] = place
             nc.gpsimd.tensor_tensor(place, c_planes[j][:, halves[u]], sh_sb[u][:], ALU.mult)
 
         def gradient(u, j, place=None):
-            dc = place if place is not None else sb.tile([P, HALF], F32, name=f"dc{u}{j}", align_bytes=64)[:]
+            dc = place if place is not None else buf(f"dc{u}{j}", [P, HALF])[:]
             nc.vector.scalar_tensor_tensor(dc, pulls[u, j], neg_cd2[:, j : j + 1], products[u, j], ALU.mult, ALU.add)
             return dc
 
@@ -282,98 +282,88 @@ def tile_attend_grbf_pl_kernel(tc, xT, cT, hx, cs, cd, dp, us, wt, offs, out_0, 
         def store(j):
             nc.sync.dma_start(out=out_planes[j], in_=windows[j][:])
 
-        weighted_dp = sb.tile([P, GPSIMD_H_PLANES, HALF], F32, name="weighted_dp", tag="c_words1", align_bytes=64)
-        for t in range(GPSIMD_H_PLANES):
-            nc.gpsimd.tensor_scalar(
-                weighted_dp[:, t, :], dp_sb[:, t, halves[0]], wt_col[:, t : t + 1], 0.0, ALU.mult, ALU.add
-            )
-        neg_cd = sb.tile([P, LANES], F32, name="neg_cd")
-        nc.gpsimd.tensor_scalar(neg_cd[:], cd_col[:], -1.0, 0.0, ALU.mult, ALU.add)
-        nc.gpsimd.tensor_tensor(neg_cd2[:], neg_cd[:], cd_col[:], ALU.mult)
-        exponents(0, first_n2_row)
-        exponents(1, n2_as_row(1))
-        for u in range(2):
-            probabilities(u)
+        turn_x(1, 6)
         weights(0, range(LANES))
-        sh_as_row(0)
-        weights(1, (0,))
-        nc.vector.tensor_scalar(g_planes[0][:, LAST, :], h_planes[0, LAST][:], us_col[:, LAST:], None, ALU.mult)
-        weights(1, (1, 2, 3))
-        weave_g(0)
+        form_g(0)
+        quantise_x(1)
         quantise_g(0)
-        multiply(0, (3, 0, 1, 2))
-        sh_as_row(1)
-
+        sh_as_row(0)
+        multiply(0, (3, 2))
+        sh_to_sbuf(0)
+        turn_x(0, 6)
+        weights(1, range(LANES))
         vector_pull(0, 3)
-        sh_sb = [sh_to_sbuf(0)]
-        weave_g(1)
+        quantise_x(0)
+        sh_as_row(1)
+        multiply(0, (1, 0))
         scalar_scatter(0, 3, gradient(0, 3))
+        early_pulls = buf("early_pulls", [P, 2, HALF], tag="xr0")
+        gpsimd_pull(0, 2, early_pulls[:, 0, :])
+        gpsimd_pull(0, 1, early_pulls[:, 1, :])
+        form_g(1)
+        dc_02 = gradient(0, 2)
         quantise_g(1)
-        multiply(1, (3, 0, 2, 1))
-        reused = sb.tile([P, 2 * HALF], F32, name="reused", align_bytes=64)
-        vector_pull(1, 3, place=reused[:, HALF // 2 : 3 * HALF // 2])
-        vector_pull(1, 0)
-        sh_sb.append(sh_to_sbuf(1))
-        scalar_scatter(1, 3, gradient(1, 3))
+        multiply(1, (3, 2, 0, 1))
+        vector_pull(1, 3)
+        vector_pull(1, 2)
+        scalar_scatter(0, 2, dc_02)
+        sh_to_sbuf(1)
+        late_pulls = buf("late_pulls", [P, 3, HALF], tag="g_words1")
+        gpsimd_pull(0, 0, late_pulls[:, 0, :])
+        gpsimd_pull(1, 0, late_pulls[:, 1, :])
+        gpsimd_pull(1, 1, late_pulls[:, 2, :])
+        dc_13 = gradient(1, 3)
+        scalar_scatter(1, 2, gradient(1, 2))
+        vector_scatter(1, 3, dc_13)
         store(3)
-        late_pulls = sb.tile([P, 3 * HALF], F32, name="late_pulls", tag="g_words1", align_bytes=64)
-        for j in range(3):
-            gpsimd_pull(0, j, late_pulls[:, HALF * j : HALF * (j + 1)])
-        dc_10 = gradient(1, 0)
+        store(2)
         dc_00 = gradient(0, 0, place=pulls[1, 3])
-        scalar_scatter(0, 1, gradient(0, 1, place=pulls[1, 0]))
+        scalar_scatter(0, 1, gradient(0, 1, place=pulls[1, 2]))
         vector_scatter(0, 0, dc_00)
-        gpsimd_pull(1, 1, reused[:, :HALF])
-        gpsimd_pull(1, 2, reused[:, HALF:])
-        scalar_scatter(0, 2, gradient(0, 2, place=pulls[0, 0]))
+        dc_10 = gradient(1, 0, place=pulls[0, 0])
+        scalar_scatter(1, 1, gradient(1, 1, place=pulls[0, 1]))
         vector_scatter(1, 0, dc_10)
         store(0)
-        dc_11 = gradient(1, 1)
-        scalar_scatter(1, 2, gradient(1, 2))
-        vector_scatter(1, 1, dc_11)
         store(1)
-        store(2)
 
         y_words = {}
-        rounded = [
-            sb.tile([P, LANES, width], BF16, name=f"rounded{k}", align_bytes=64) for k, (first, width) in enumerate(PIECES)
-        ]
-        for j in (3, 0, 1, 2):
-            engine_copy = nc.gpsimd.tensor_copy if j in (3, 0) else nc.vector.tensor_copy
-            done = SCALAR_ROUNDS if j == 2 else 0
+        rounded = [buf(f"rounded{k}", [P, LANES, width], BF16) for k, (first, width) in enumerate(PIECES)]
+        for j in (3, 2, 0, 1):
+            engine_copy = nc.gpsimd.tensor_copy if j in (3, 2) else nc.vector.tensor_copy
+            done = SCALAR_ROUNDS if j == 1 else 0
             if done:
                 nc.scalar.copy(out=rounded[0][:, j, :done], in_=windows[j][:, :done])
             for k, (first, width) in enumerate(PIECES):
                 skip = max(done - first, 0)
                 engine_copy(out=rounded[k][:, j, skip:], in_=windows[j][:, first + skip : first + width])
         for k, (first, width) in enumerate(PIECES):
-            y_words[first] = sb.tile([P, width, LANES], BF16, name=f"y_words{first}", align_bytes=64)
+            y_words[first] = buf(f"y_words{first}", [P, width, LANES], BF16)
             nc.vector.tensor_copy(
                 out=y_words[first][:].rearrange("p (c i) t -> p c t i", i=4),
                 in_=rounded[k][:].rearrange("p t (c i) -> p c t i", i=4),
             )
 
         starts = range(VECTOR_COLUMNS, T, P)
-        turned = [ps.tile([P, LANES, P], F32, name=f"y_turned{c}", tag=f"bank{b}") for c, b in zip(starts, TURN_BANKS)]
-        for planes in ((3,), (0,), (1, 2)):
-            for c, bank in zip(starts, turned):
+        turned = [bank(f"y_turned{c}", [P, LANES, P], b) for c, b in zip(starts, TURN_BANKS)]
+        for planes in ((3,), (2,), (0, 1)):
+            for c, block in zip(starts, turned):
                 for j in planes:
-                    nc.tensor.transpose(bank[:, j, :], windows[j][:, c : c + P], ident[:])
-        rows = []
+                    nc.tensor.transpose(block[:, j, :], windows[j][:, c : c + P], ident[:])
+        y_rows = []
 
         def round_block(n):
-            row = sb.tile([P, 2, P, 2], BF16, name=f"y_rows{n}", align_bytes=64)
+            row = buf(f"y_rows{n}", [P, 2, P, 2], BF16)
             nc.scalar.copy(out=row[:], in_=turned[n][:].rearrange("c (u e) p -> c u p e", u=2))
-            rows.append(row[:].rearrange("c u p e -> c (u p e)").bitcast(F32))
+            y_rows.append(row[:].rearrange("c u p e -> c (u p e)").bitcast(F32))
 
-        def turn_back(group):
+        def turn_back(group, number):
             width = P * len(group)
-            back = ps.tile([P, 2, width], F32, name=f"y_back{group[0]}", tag=f"bank{TURN_BANKS[group[0]]}")
+            back = bank(f"y_back{group[0]}", [P, 2, width], number)
             for e, n in enumerate(group):
                 for u in range(2):
-                    nc.tensor.transpose(back[:, u, P * e : P * (e + 1)], rows[n][:, P * u : P * (u + 1)], ident[:])
+                    nc.tensor.transpose(back[:, u, P * e : P * (e + 1)], y_rows[n][:, P * u : P * (u + 1)], ident[:])
             first = starts[group[0]]
-            y_words[first] = sb.tile([P, width, LANES], BF16, name=f"y_words{first}", align_bytes=64)
+            y_words[first] = buf(f"y_words{first}", [P, width, LANES], BF16)
             nc.scalar.copy(
                 out=y_words[first][:].rearrange("p c t -> p (c t)").bitcast(F32).rearrange("p (c u) -> p c u", u=2),
                 in_=back[:].rearrange("p u c -> p c u"),
@@ -381,18 +371,18 @@ def tile_attend_grbf_pl_kernel(tc, xT, cT, hx, cs, cd, dp, us, wt, offs, out_0, 
 
         for n in range(4):
             round_block(n)
-        turn_back((0, 1))
+        turn_back((0, 1), BACK_BANKS[0])
         for n in (4, 5):
             round_block(n)
-        for group in ((2, 3), (4,), (5,)):
-            turn_back(group)
+        for group, number in zip(((2, 3), (4,), (5,)), BACK_BANKS[1:]):
+            turn_back(group, number)
 
-        y_scales = sb.tile([P, T // 4], U8, name="y_scales", align_bytes=64)
+        y_scales = buf("y_scales", [P, T // 4], U8)
         words_out = out_1[0].rearrange("p c l -> p (c l)").bitcast(I32)
         for group, freed in CODE_STORES:
             start = CHUNKS[group[0]][0]
             span = sum(CHUNKS[k][1] for k in group)
-            y_codes = sb.tile([P, span], U32, name=f"y_codes{group[0]}", tag=freed, align_bytes=64)
+            y_codes = buf(f"y_codes{group[0]}", [P, span], U32, tag=freed)
             for k in group:
                 first, width = CHUNKS[k]
                 quarter, place = divmod(first, T // 4)

from contextlib import ExitStack

import concourse.mybir as mybir
from concourse.masks import make_identity

F32 = mybir.dt.float32
BF16 = mybir.dt.bfloat16
I32 = mybir.dt.int32
U32 = mybir.dt.uint32
U16 = mybir.dt.uint16
U8 = mybir.dt.uint8
E4M3 = mybir.dt.float8_e4m3fn_x4
E5M2 = mybir.dt.float8_e5m2_x4
ACT = mybir.ActivationFunctionType
ALU = mybir.AluOpType

P = 128
LANES = 4
LAST = LANES - 1
D = 512
R = 512
SLOTS = 512
HALF = SLOTS // 2
T = 2048
CS, HX, US, WT, CD = range(5)

VECTOR_COLUMNS = 1280
PIECES = ((0, 512), (512, 768))
SCALAR_ROUNDS = 256
TURN_BANKS = (6, 7, 4, 0, 2, 1)
BACK_BANKS = (5, 3, 6, 7)
CHUNKS = tuple((first, 256) for first in range(0, 1792, 256)) + ((1792, 128), (1920, 128))
CODE_STORES = (((0, 1), "y_codes0"), ((2, 3, 4), "y_codes1"), ((5, 6), "y_words0"), ((7, 8), "y_words512"))
SCORE_BANKS = ((3, 4, 5, 6), (7, 0, 1, 3))
GPSIMD_H_PLANES = 2
PRODUCT_BANKS = ({3: 3, 2: 4, 1: 5, 0: 5}, {3: 0, 2: 2, 1: 3, 0: 3})

FLOPS = 2 * 2 * D * R * SLOTS


def tile_attend_grbf_pl_kernel(tc, xT, cT, hx, cs, cd, dp, us, wt, offs, out_0, out_1, out_2):
    nc = tc.nc
    with ExitStack() as ctx:
        sb = ctx.enter_context(tc.tile_pool(name="sb", bufs=1))
        ps = ctx.enter_context(tc.psum_pool(name="ps", bufs=1))

        def buf(name, shape, dtype=F32, tag=None):
            return sb.tile(shape, dtype, name=name, tag=tag or name, align_bytes=64)

        def bank(name, shape, number, dtype=F32):
            return ps.tile(shape, dtype, name=name, tag=f"bank{number}")

        def mx_tiles(name, width, tag=None):
            return buf(name + "_codes", [P, width], U32, tag), buf(name + "_scales", [P, width], U8)

        def quantise(tiles, words, fmt, cols=None):
            codes, scales = tiles
            cols = cols if cols is not None else slice(0, codes.shape[1])
            nc.vector.quantize_mx(out=codes[:, cols].bitcast(fmt), scales=scales[:, cols], in_=words)

        def turn_and_add(turned, plane, start, stop):
            for b in range(2):
                nc.tensor.matmul(
                    turned[b], plane[:, P * b : P * (b + 1)], ident[:], is_transpose=True, start=start[b], stop=stop[b]
                )

        def slot_sums(name, turned, scale):
            sums = []
            for b in range(2):
                total = buf(f"{name}_col{b}", [P, 1])
                terms = buf(f"{name}_summed{b}", [P, P])
                nc.scalar.activation(terms[:], turned[b], ACT.Identity, scale=scale, accum_out=total[:])
                sums.append(total)
            return sums

        def spread(row, sums):
            for b, total in enumerate(sums):
                nc.tensor.transpose(row[:, P * b : P * (b + 1)], total[:].to_broadcast([P, P]), ident[:])

        halves = [slice(HALF * u, HALF * (u + 1)) for u in range(2)]

        offsets = sb.tile([P, SLOTS // 16], U16, name="offsets")
        nc.sync.dma_start(offsets[:], offs)
        rows = buf("rows", [P, D])
        nc.gpsimd.memset(rows[:], 0.0)
        for k, vector in enumerate((cs[0:1, :], hx, us, wt, cd)):
            nc.scalar.dma_start(out=rows[k : k + 1, :], in_=vector if k == CS else vector.rearrange("r o -> o r"))
        cT_planes = cT.rearrange("(p j) c -> j p c", j=LANES)
        table = []
        for j in range(LANES):
            plane = buf(f"table{j}", [P, T])
            nc.sync.dma_start(out=plane[:], in_=cT_planes[j])
            table.append(plane)
        x_raw = buf("x_raw", [P, LANES, R])
        nc.sync.dma_start(out=x_raw[:], in_=xT.rearrange("(p j) r -> p j r", j=LANES))
        dp_rows = dp.rearrange("(s t) i -> s t i", t=LANES)
        dp_pairs = []
        for v in range(2):
            pair = buf(f"dp_pair{v}", [P, 2, SLOTS])
            nc.sync.dma_start(out=pair[:], in_=dp_rows[:, 2 * v : 2 * v + 2, :])
            dp_pairs.append(pair)

        def dp_part(u, t):
            return dp_pairs[t // 2][:, t % 2, halves[u]]

        ident = buf("ident", [P, P])
        make_identity(nc, ident[:])
        windows = {}
        for j in (3, 2, 1, 0):
            windows[j] = buf(f"window{j}", [P, T])
            (nc.vector if j > 1 else nc.gpsimd).memset(windows[j][:], 0.0)

        cols_ps = bank("cols_ps", [P, LANES, P], 2)
        for j in range(LANES):
            nc.tensor.transpose(cols_ps[:, j, :], rows[:, j : D : LANES], ident[:])
        cols = buf("cols", [P, LANES, 8])
        nc.scalar.copy(out=cols[:], in_=cols_ps[:, :, 0:8])
        neg_hx = buf("neg_hx", [P, LANES])
        nc.gpsimd.tensor_scalar(neg_hx[:], cols[:, :, HX], -1.0, 0.0, ALU.mult, ALU.add)
        neg_cd = buf("neg_cd", [P, LANES])
        nc.gpsimd.tensor_scalar(neg_cd[:], cols[:, :, CD], -1.0, 0.0, ALU.mult, ALU.add)
        neg_cd2 = buf("neg_cd2", [P, LANES])
        nc.gpsimd.tensor_tensor(neg_cd2[:], neg_cd[:], cols[:, :, CD], ALU.mult)

        def col(k, j):
            return cols[:, j, k : k + 1]

        c_pairs = [buf(f"c_pair{v}", [P, 2, SLOTS]) for v in range(2)]
        c_planes = [c_pairs[j // 2][:, j % 2, :] for j in range(LANES)]
        c_words = [buf(f"c_words{u}", [P, HALF, LANES], BF16) for u in range(2)]
        n2_turned = [[bank(f"n2_turned{u}{b}", [P, P], 4 + 2 * u + b)[:] for b in range(2)] for u in range(2)]

        def lay_centres(u, v):
            nc.vector.tensor_copy(
                out=c_words[u][:, :, 2 * v : 2 * v + 2], in_=c_pairs[v][:, :, halves[u]].rearrange("p e i -> p i e")
            )

        for j in range(LAST):
            square = buf(f"square{j}", [P, SLOTS])
            nc.vector.tensor_copy(c_planes[j], table[j][:].indirect(offsets[:]))
            nc.scalar.activation(square[:], c_planes[j], ACT.Square, scale=col(CS, j))
            for u in range(2):
                turn_and_add(n2_turned[u], square[:, halves[u]], (j == 0, j == 0), (False, False))
            if j == 1:
                for u in range(2):
                    lay_centres(u, 0)
        half_lists = [offsets[:, HALF // 16 * u : HALF // 16 * (u + 1)] for u in range(2)]
        for u in range(2):
            nc.vector.tensor_copy(c_planes[LAST][:, halves[u]], table[LAST][:].indirect(half_lists[u]))
            square = buf(f"square{LAST}_{u}", [P, HALF])
            nc.scalar.activation(square[:], c_planes[LAST][:, halves[u]], ACT.Square, scale=col(CS, LAST))
            turn_and_add(n2_turned[u], square[:], (False, False), (True, True))
        for u in range(2):
            lay_centres(u, 1)
        n2_rows = []
        for u in range(2):
            sums = slot_sums(f"n2_{u}", n2_turned[u], 0.5)
            spread_ps = bank(f"n2_row_ps{u}", [P, HALF], u)
            spread(spread_ps, sums)
            row = buf(f"n2_row{u}", [P, HALF])
            nc.scalar.copy(out=row[:], in_=spread_ps[:])
            n2_rows.append(row)

        c_mx = [mx_tiles("c0", HALF)]
        quantise(c_mx[0], c_words[0][:].rearrange("p i t -> p (i t)"), E4M3)
        xd_all = buf("xd", [P, LANES, P, LANES], BF16, tag=f"square{LAST}_1")
        xd = [xd_all[:, 2 * v : 2 * v + 2, :, :] for v in range(2)]
        x_dealt = x_raw[:].rearrange("p j (s t) -> p s j t", t=LANES)
        for v in range(2):
            nc.vector.tensor_copy(out=xd[v].rearrange("p t s j -> p s j t"), in_=x_dealt[:, :, :, 2 * v : 2 * v + 2])
        xd_mx = []
        for v in range(2):
            xd_mx.append(mx_tiles(f"xd{v}", 2 * P))
            quantise(xd_mx[v], xd[v].rearrange("p t s j -> p (t s j)"), E4M3)
        c_mx.append(mx_tiles("c1", HALF, tag="x_raw"))
        quantise(c_mx[1], c_words[1][:].rearrange("p i t -> p (i t)"), E4M3)

        weighted_dp = buf("weighted_dp", [P, GPSIMD_H_PLANES, HALF], tag="c_words1")
        for t in range(GPSIMD_H_PLANES):
            nc.gpsimd.tensor_scalar(weighted_dp[:, t, :], dp_part(0, t), col(WT, t), 0.0, ALU.mult, ALU.add)

        out_planes = out_0.rearrange("(p j) c -> j p c", j=LANES)
        expos, probs, h_tiles, g_words, g_mx, xr, xr_mx = {}, {}, {}, {}, {}, {}, {}
        sh_turned, sh_rows, sh_sb, product_banks, products, pulls = {}, {}, {}, {}, {}, {}

        def product_pass(out, stationary, b, moving, fmt):
            (s_codes, s_scales), (m_codes, m_scales) = stationary, moving
            block = slice(P * b, P * (b + 1))
            nc.tensor.matmul_mx(
                out=out, lhsT=s_codes[:, block].bitcast(E4M3), lhsT_scale=s_scales[:, block],
                rhs=m_codes[:].bitcast(fmt), rhs_scale=m_scales[:], start=True, stop=True,
            )

        for u in range(2):
            for t, number in enumerate(SCORE_BANKS[u]):
                a = bank(f"a{u}{t}", [P, HALF], number)
                product_pass(a[:], xd_mx[t // 2], t % 2, c_mx[u], E4M3)
                expos[u, t] = buf(f"expo{u}{t}", [P, HALF])
                nc.vector.scalar_tensor_tensor(expos[u, t][:], a[:], col(US, t), n2_rows[u][:], ALU.mult, ALU.subtract)
        for u in range(2):
            for t in range(LANES):
                probs[u, t] = buf(f"prob{u}{t}", [P, HALF])
                nc.scalar.activation(probs[u, t][:], expos[u, t][:], ACT.Exp, bias=neg_hx[:, t : t + 1])

        def turn_x(v, number):
            x_turned = bank(f"x_turned{v}", [P, LANES, P], number)
            for t in range(LANES):
                pairs = xd[t // 2][:, t % 2, :, :].rearrange("p s j -> p (s j)").bitcast(F32)
                nc.tensor.transpose(x_turned[:, t, :], pairs[:, v : 2 * P : 2], ident[:])
            xr[v] = buf(f"xr{v}", [P, 2, P, LANES], BF16)
            nc.scalar.copy(
                out=xr[v][:],
                in_=x_turned[:].rearrange("s t p -> s (t p)").bitcast(BF16).rearrange("s (t p e) -> s e p t", t=LANES, e=2),
            )

        def quantise_x(v):
            xr_mx[v] = mx_tiles(f"xr{v}", 2 * P)
            quantise(xr_mx[v], xr[v][:].rearrange("s e p t -> s (e p t)"), E4M3)

        def weights(u, planes):
            if u not in h_tiles:
                h_tiles[u] = buf(f"h{u}", [P, LANES, HALF])
                sh_turned[u] = bank(f"sh_turned{u}", [P, 2, P], (4, 7)[u])
            for t in planes:
                h = h_tiles[u][:, t, :]
                if u == 0 and t < GPSIMD_H_PLANES:
                    nc.gpsimd.tensor_tensor(h, probs[u, t][:], weighted_dp[:, t, :], ALU.mult)
                else:
                    nc.vector.scalar_tensor_tensor(h, probs[u, t][:], col(WT, t), dp_part(u, t), ALU.mult, ALU.mult)
                turn_and_add([sh_turned[u][:, b, :] for b in range(2)], h, (t == 0, False), (False, t == LAST))

        def sh_as_row(u):
            sums = slot_sums(f"sh{u}", [sh_turned[u][:, b, :] for b in range(2)], 1.0)
            sh_rows[u] = bank(f"sh_row{u}", [P, HALF], u)
            spread(sh_rows[u], sums)

        def form_g(u):
            g_words[u] = buf(f"g_words{u}", [P, HALF, LANES], BF16)
            nc.vector.tensor_tensor(
                g_words[u][:].rearrange("s (c i) t -> s c t i", i=2),
                h_tiles[u][:].rearrange("s t (c i) -> s c t i", i=2),
                cols_ps[:, :, US : US + 1].unsqueeze(1).broadcast_to([P, HALF // 2, LANES, 2]),
                ALU.mult,
            )

        def quantise_g(u):
            g_mx[u] = mx_tiles(f"g{u}", HALF)
            quantise(g_mx[u], g_words[u][:].rearrange("s i t -> s (i t)"), E5M2)

        def multiply(u, planes):
            for j in planes:
                number = PRODUCT_BANKS[u][j]
                tenants = [k for k in range(LANES) if PRODUCT_BANKS[u][k] == number]
                if (u, number) not in product_banks:
                    product_banks[u, number] = bank(f"xg{u}{j}", [P, len(tenants), HALF], number)
                products[u, j] = product_banks[u, number][:, tenants.index(j), :]
                product_pass(products[u, j], xr_mx[j // 2], j % 2, g_mx[u], E5M2)

        def vector_pull(u, j):
            pulls[u, j] = buf(f"pull{u}{j}", [P, HALF])[:]
            nc.vector.tensor_tensor(pulls[u, j], c_planes[j][:, halves[u]], sh_rows[u][:], ALU.mult)

        def sh_to_sbuf(u):
            sh_sb[u] = buf(f"sh_sb{u}", [P, HALF])
            nc.scalar.copy(out=sh_sb[u][:], in_=sh_rows[u][:])

        def gpsimd_pull(u, j, place):
            pulls[u, j] = place
            nc.gpsimd.tensor_tensor(place, c_planes[j][:, halves[u]], sh_sb[u][:], ALU.mult)

        def gradient(u, j, place=None):
            dc = place if place is not None else buf(f"dc{u}{j}", [P, HALF])[:]
            nc.vector.scalar_tensor_tensor(dc, pulls[u, j], neg_cd2[:, j : j + 1], products[u, j], ALU.mult, ALU.add)
            return dc

        def scalar_scatter(u, j, dc):
            nc.scalar.activation(windows[j][:].indirect(half_lists[u]), dc, ACT.Copy)

        def vector_scatter(u, j, dc):
            nc.vector.tensor_copy(windows[j][:].indirect(half_lists[u]), dc)

        def store(j):
            nc.sync.dma_start(out=out_planes[j], in_=windows[j][:])

        turn_x(1, 6)
        weights(0, range(LANES))
        form_g(0)
        quantise_x(1)
        quantise_g(0)
        sh_as_row(0)
        multiply(0, (3, 2))
        sh_to_sbuf(0)
        turn_x(0, 6)
        weights(1, range(LANES))
        vector_pull(0, 3)
        quantise_x(0)
        sh_as_row(1)
        multiply(0, (1, 0))
        scalar_scatter(0, 3, gradient(0, 3))
        early_pulls = buf("early_pulls", [P, 2, HALF], tag="xr0")
        gpsimd_pull(0, 2, early_pulls[:, 0, :])
        gpsimd_pull(0, 1, early_pulls[:, 1, :])
        form_g(1)
        dc_02 = gradient(0, 2)
        quantise_g(1)
        multiply(1, (3, 2, 0, 1))
        vector_pull(1, 3)
        vector_pull(1, 2)
        scalar_scatter(0, 2, dc_02)
        sh_to_sbuf(1)
        late_pulls = buf("late_pulls", [P, 3, HALF], tag="g_words1")
        gpsimd_pull(0, 0, late_pulls[:, 0, :])
        gpsimd_pull(1, 0, late_pulls[:, 1, :])
        gpsimd_pull(1, 1, late_pulls[:, 2, :])
        dc_13 = gradient(1, 3)
        scalar_scatter(1, 2, gradient(1, 2))
        vector_scatter(1, 3, dc_13)
        store(3)
        store(2)
        dc_00 = gradient(0, 0, place=pulls[1, 3])
        scalar_scatter(0, 1, gradient(0, 1, place=pulls[1, 2]))
        vector_scatter(0, 0, dc_00)
        dc_10 = gradient(1, 0, place=pulls[0, 0])
        scalar_scatter(1, 1, gradient(1, 1, place=pulls[0, 1]))
        vector_scatter(1, 0, dc_10)
        store(0)
        store(1)

        y_words = {}
        rounded = [buf(f"rounded{k}", [P, LANES, width], BF16) for k, (first, width) in enumerate(PIECES)]
        for j in (3, 2, 0, 1):
            engine_copy = nc.gpsimd.tensor_copy if j in (3, 2) else nc.vector.tensor_copy
            done = SCALAR_ROUNDS if j == 1 else 0
            if done:
                nc.scalar.copy(out=rounded[0][:, j, :done], in_=windows[j][:, :done])
            for k, (first, width) in enumerate(PIECES):
                skip = max(done - first, 0)
                engine_copy(out=rounded[k][:, j, skip:], in_=windows[j][:, first + skip : first + width])
        for k, (first, width) in enumerate(PIECES):
            y_words[first] = buf(f"y_words{first}", [P, width, LANES], BF16)
            nc.vector.tensor_copy(
                out=y_words[first][:].rearrange("p (c i) t -> p c t i", i=4),
                in_=rounded[k][:].rearrange("p t (c i) -> p c t i", i=4),
            )

        starts = range(VECTOR_COLUMNS, T, P)
        turned = [bank(f"y_turned{c}", [P, LANES, P], b) for c, b in zip(starts, TURN_BANKS)]
        for planes in ((3,), (2,), (0, 1)):
            for c, block in zip(starts, turned):
                for j in planes:
                    nc.tensor.transpose(block[:, j, :], windows[j][:, c : c + P], ident[:])
        y_rows = []

        def round_block(n):
            row = buf(f"y_rows{n}", [P, 2, P, 2], BF16)
            nc.scalar.copy(out=row[:], in_=turned[n][:].rearrange("c (u e) p -> c u p e", u=2))
            y_rows.append(row[:].rearrange("c u p e -> c (u p e)").bitcast(F32))

        def turn_back(group, number):
            width = P * len(group)
            back = bank(f"y_back{group[0]}", [P, 2, width], number)
            for e, n in enumerate(group):
                for u in range(2):
                    nc.tensor.transpose(back[:, u, P * e : P * (e + 1)], y_rows[n][:, P * u : P * (u + 1)], ident[:])
            first = starts[group[0]]
            y_words[first] = buf(f"y_words{first}", [P, width, LANES], BF16)
            nc.scalar.copy(
                out=y_words[first][:].rearrange("p c t -> p (c t)").bitcast(F32).rearrange("p (c u) -> p c u", u=2),
                in_=back[:].rearrange("p u c -> p c u"),
            )

        for n in range(4):
            round_block(n)
        turn_back((0, 1), BACK_BANKS[0])
        for n in (4, 5):
            round_block(n)
        for group, number in zip(((2, 3), (4,), (5,)), BACK_BANKS[1:]):
            turn_back(group, number)

        y_scales = buf("y_scales", [P, T // 4], U8)
        words_out = out_1[0].rearrange("p c l -> p (c l)").bitcast(I32)
        for group, freed in CODE_STORES:
            start = CHUNKS[group[0]][0]
            span = sum(CHUNKS[k][1] for k in group)
            y_codes = buf(f"y_codes{group[0]}", [P, span], U32, tag=freed)
            for k in group:
                first, width = CHUNKS[k]
                quarter, place = divmod(first, T // 4)
                home = max(c for c in y_words if c <= first)
                nc.vector.quantize_mx(
                    out=y_codes[:, first - start : first - start + width].bitcast(E4M3),
                    scales=y_scales[4 * quarter :, place : place + width],
                    in_=y_words[home][:, first - home : first - home + width, :].rearrange("p c t -> p (c t)"),
                )
            nc.sync.dma_start(out=words_out[:, start : start + span], in_=y_codes[:].bitcast(I32))
        scales_out = out_2[0].bitcast(I32).rearrange("f (quarter c) -> quarter f c", quarter=4)
        for q in range(4):
            queue = nc.scalar if q < 2 else nc.sync
            queue.dma_start(out=scales_out[:, 4 * q : 4 * q + 4, :], in_=y_scales[32 * q : 32 * q + 16, :].bitcast(I32))
